import numpy as np
import ml_dtypes


def mxq(x, axis, fmt="e4m3"):
    dtype, down = {"e4m3": (ml_dtypes.float8_e4m3fn, 7), "e5m2": (ml_dtypes.float8_e5m2, 14)}[fmt]
    v = np.moveaxis(np.asarray(x, np.float32).astype(ml_dtypes.bfloat16).astype(np.float64), axis, -1)
    blocks = v.reshape(v.shape[:-1] + (-1, 32))
    amax = np.abs(blocks).max(-1, keepdims=True)
    byte = np.maximum(np.where(amax > 0, np.frexp(amax)[1] - 1 + 127, 0) - down, 1)
    scale = np.exp2(byte - 127.0)
    codes = (blocks / scale).astype(np.float32).astype(dtype).astype(np.float64)
    return np.moveaxis((codes * scale).reshape(v.shape), -1, axis)


WIDE = False


def mx_kscale(k):
    if not WIDE:
        return np.ones(k)
    levels = np.array([10, -10, 5, -5, 0])
    if k % 512:
        return np.exp2(np.random.permutation(np.resize(levels, k // 32))).repeat(32)
    a = np.empty((k // 512, 16))
    for p in range(k // 512):
        a[p, :8] = np.random.permutation(np.resize(levels, 8))
        for g in range(8):
            far = levels[np.abs(levels - a[p, g]) >= 10]
            a[p, g + 8] = far[np.random.randint(len(far))]
    return np.exp2(a.ravel()).repeat(32)


def f64(x):
    return np.asarray(x).astype(np.float64)


def striped(idx):
    return np.tile(idx.reshape(-1, 16).T, (8, 1)).astype(np.uint16)


def unstriped(offs):
    return offs[:16].T.reshape(-1).astype(np.int64)


E2M1 = np.array([0.0, 0.5, 1.0, 1.5, 2.0, 3.0, 4.0, 6.0, -0.0, -0.5, -1.0, -1.5, -2.0, -3.0, -4.0, -6.0])


def pack_weight(w, fmt):
    k, n = w.shape
    w = f64(np.asarray(w, np.float32).astype(ml_dtypes.bfloat16)).reshape(k // 32, 32, n)
    amax = np.abs(w).max(1)
    if fmt == "e4m3":
        byte = np.frexp(amax)[1] - 1 + 127 - 7
    else:
        mant, ex = np.frexp(amax / 6.0)
        byte = np.where(mant > 0.5, ex, ex - 1) + 127
    byte = np.clip(np.where(amax > 0, byte, 1), 1, 254)
    scaled = (w * np.exp2(127.0 - byte)[:, None, :]).reshape(k, n).astype(np.float32)
    by_word = np.ascontiguousarray(scaled.reshape(k // 512, 128, 4, n).transpose(0, 1, 3, 2))
    if fmt == "e4m3":
        words = by_word.astype(ml_dtypes.float8_e4m3fn).view(np.uint8)
    else:
        c = by_word.astype(ml_dtypes.float4_e2m1fn).view(np.uint8) & 0xF
        words = (c[..., 0::2] | (c[..., 1::2] << 4)).reshape(k // 512, 128, 2 * n)
    return np.ascontiguousarray(words), np.ascontiguousarray(byte.astype(np.uint8).reshape(k // 512, 16, n))


def unpack_weight(words, scales, fmt):
    g, _, n = scales.shape
    words = np.ascontiguousarray(words).reshape(g, 128, n, -1)
    if fmt == "e4m3":
        vals = words.view(ml_dtypes.float8_e4m3fn).astype(np.float64)
    else:
        nib = np.empty((g, 128, n, 4), np.uint8)
        nib[..., 0::2] = words & 0xF
        nib[..., 1::2] = words >> 4
        vals = E2M1[nib]
    vals = vals * np.repeat(np.exp2(scales.astype(np.float64) - 127.0), 8, axis=1)[..., None]
    return vals.transpose(0, 1, 3, 2).reshape(g * 512, n)


def gelu(v):
    return 0.5 * v * (1.0 + np.tanh(np.sqrt(2.0 / np.pi) * (v + 0.044715 * v**3)))


K, H, N, T, S, P, P2 = 1024, 1536, 512, 2048, 1024, 512, 256

def setup_inputs():
    n = np.random.standard_normal
    s = mx_kscale(K)[:, None]
    u = mx_kscale(H)[:, None]
    tab_words, tab_scales = pack_weight(n((K, T)) * s, "e4m3")
    wd_words, wd_scales = pack_weight(0.6 * n((H, N)) / np.sqrt(H) / u, "e2m1")
    return {
        "tab_words": tab_words, "tab_scales": tab_scales,
        "offs": striped(np.random.permutation(T)[:S]),
        "pos1": striped(np.random.permutation(S)[:P]),
        "pos2": striped(np.random.permutation(S)[:P]),
        "pos3": striped(np.random.permutation(P)[:P2]),
        "pos4": striped(np.random.permutation(P)[:P2]),
        "w1": (n((K, H)) / np.sqrt(K) / s * u.T).astype(np.float32),
        "wd_words": wd_words, "wd_scales": wd_scales,
        "wb": (0.8 * n((H, N)) / np.sqrt(H) / (u * u)).astype(np.float32),
    }

def reference(tab_words, tab_scales, offs, pos1, pos2, pos3, pos4, w1, wd_words, wd_scales, wb):
    v = unpack_weight(tab_words, tab_scales, "e4m3")[:, unstriped(offs)]
    h = mxq(f64(w1), 0, "e4m3").T @ v
    x1 = h[:, unstriped(pos1)]
    x2 = h[:, unstriped(pos2)]
    d = mxq(np.abs(x1 - x2), 0, "e4m3")
    b = mxq(x1 * x2, 0, "e4m3")
    wd = unpack_weight(wd_words, wd_scales, "e2m1")
    y = wd.T @ d + mxq(f64(wb), 0, "e4m3").T @ b
    top = np.maximum(y[:, unstriped(pos3)], y[:, unstriped(pos4)])
    return 1.0 + np.square(top)

@@ -1,0 +1,211 @@
+from contextlib import ExitStack
+
+import concourse.mybir as mybir
+
+K, H, N, T, S, M1, M2 = 1024, 1536, 512, 2048, 1024, 512, 256
+FLOPS = 2 * K * H * S + 2 * 2 * H * N * M1
+
+F32 = mybir.dt.float32
+BF16 = mybir.dt.bfloat16
+I32 = mybir.dt.int32
+U32 = mybir.dt.uint32
+U16 = mybir.dt.uint16
+U8 = mybir.dt.uint8
+FP8X4 = mybir.dt.float8_e4m3fn_x4
+FP4X4 = mybir.dt.float4_e2m1fn_x4
+ACT = mybir.ActivationFunctionType
+ALU = mybir.AluOpType
+
+P = 128
+PACK = 4
+PASS = P * PACK
+BANK = 512
+K_PASSES = K // PASS
+H_PASSES = H // PASS
+N_TILES = N // P
+
+
+def tile_list_subtitle_couple_score_kernel(
+    tc, tab_words, tab_scales, offs, pos1, pos2, pos3, pos4, w1, wd_words, wd_scales, wb, out
+):
+    nc = tc.nc
+    with ExitStack() as ctx:
+        keep = ctx.enter_context(tc.tile_pool(name="keep", bufs=1))
+        ring = ctx.enter_context(tc.tile_pool(name="ring", bufs=2))
+        psum = ctx.enter_context(tc.psum_pool(name="psum", bufs=1))
+
+        def load_list(src, name):
+            tile = keep.tile(list(src.shape), U16, name=name)
+            nc.sync.dma_start(tile[:], src)
+            return tile
+
+        def load_rows(src, g, cols):
+            raw = ring.tile([P, PACK, PASS], F32, name="raw", bufs=5)
+            nc.sync.dma_start(
+                out=raw[:], in_=src[g * PASS : (g + 1) * PASS, cols].rearrange("(p j) c -> p j c", j=PACK)
+            )
+            return raw
+
+        def quantize(grouped, name):
+            codes = keep.tile([P, PASS], U32, name=name + "_codes", align_bytes=64)
+            scales = keep.tile([P, PASS], U8, name=name + "_scales", align_bytes=64)
+            nc.vector.quantize_mx(out=codes[:].bitcast(FP8X4), scales=scales[:], in_=grouped[:])
+            return codes, scales
+
+        def round_w1(raw):
+            grouped = ring.tile([P, PACK * PASS], BF16, name="w_grouped", bufs=3, align_bytes=64)
+            nc.scalar.activation(
+                grouped[:].rearrange("p (t m j) -> p m j t", t=PACK, j=PACK),
+                raw[:].rearrange("p j (m t) -> p m j t", t=PACK),
+                ACT.Copy,
+            )
+            return grouped
+
+        def round_wb(raw):
+            grouped = ring.tile([P, PACK * PASS], BF16, name="w_grouped", bufs=3, align_bytes=64)
+            nc.scalar.activation(
+                grouped[:].rearrange("p (c i j) -> p c j i", i=PACK, j=PACK),
+                raw[:].rearrange("p j (c i) -> p c j i", i=PACK),
+                ACT.Copy,
+            )
+            return grouped
+
+        tab_planes = keep.tile([P, T], U8, name="tab_planes", align_bytes=64)
+        nc.vector.memset(tab_planes[:].bitcast(I32), 0)
+        wd_planes = keep.tile([P, H_PASSES, N], U8, name="wd_planes", align_bytes=64)
+        nc.gpsimd.memset(wd_planes[:].rearrange("p g n -> p (g n)").bitcast(I32), 0)
+
+        offs_sb = load_list(offs, "offs_sb")
+        tab_sb = []
+        for a in range(K_PASSES):
+            words = keep.tile([P, T], I32, name=f"tab_sb{a}", align_bytes=64)
+            nc.sync.dma_start(out=words[:], in_=tab_words[a].rearrange("p t i -> p (t i)").bitcast(I32))
+            tab_sb.append(words)
+            if a == 0:
+                for q in range(4):
+                    nc.sync.dma_start(
+                        out=tab_planes[32 * q : 32 * q + 4 * K_PASSES, :].bitcast(I32),
+                        in_=tab_scales[:, 4 * q : 4 * q + 4, :].bitcast(I32),
+                    )
+        w1_raw = {}
+        for g in range(H_PASSES):
+            for a in range(K_PASSES):
+                w1_raw[g, a] = load_rows(w1, a, slice(g * PASS, (g + 1) * PASS))
+            if g == 0:
+                pos1_sb = load_list(pos1, "pos1_sb")
+                pos2_sb = load_list(pos2, "pos2_sb")
+
+        v_codes = []
+        for a in range(K_PASSES):
+            picked = keep.tile([P, S], U32, name=f"v_codes{a}", align_bytes=64)
+            nc.vector.tensor_copy(picked[:], tab_sb[a][:].bitcast(U32).indirect(offs_sb[:]))
+            v_codes.append(picked)
+        v_planes = keep.tile([P, S], U8, name="v_planes", align_bytes=64)
+        nc.vector.tensor_copy(v_planes[:], tab_planes[:].indirect(offs_sb[:]))
+
+        w1_mx = {}
+
+        def prepare_w1(g, a):
+            w1_mx[g, a] = quantize(round_w1(w1_raw[g, a]), f"w1_{g}_{a}")
+
+        def first_stage(g, t):
+            h = ring.tile([P, S], F32, name="h", bufs=6)
+            for half in range(S // BANK):
+                cols = slice(half * BANK, (half + 1) * BANK)
+                acc = psum.tile([P, BANK], F32, name="h_acc", bufs=4)
+                for a in range(K_PASSES):
+                    codes, scales = w1_mx[g, a]
+                    nc.tensor.matmul_mx(
+                        out=acc[:],
+                        lhsT=codes[:, t * P : (t + 1) * P].bitcast(FP8X4),
+                        lhsT_scale=scales[:, t * P : (t + 1) * P],
+                        rhs=v_codes[a][:, cols].bitcast(FP8X4),
+                        rhs_scale=v_planes[4 * a : P, cols],
+                        start=(a == 0),
+                        stop=(a == K_PASSES - 1),
+                    )
+                nc.scalar.copy(h[:, cols], acc[:])
+            return h
+
+        for a in range(K_PASSES):
+            prepare_w1(0, a)
+
+        wb_raw = [load_rows(wb, g, slice(0, N)) for g in range(H_PASSES)]
+        wd_sb = keep.tile([P, H_PASSES, 2 * N], U8, name="wd_sb", align_bytes=64)
+        nc.sync.dma_start(out=wd_sb[:].bitcast(I32), in_=wd_words.rearrange("g p c -> p g c").bitcast(I32))
+        for q in range(4):
+            nc.sync.dma_start(
+                out=wd_planes[32 * q : 32 * q + 4, :, :].bitcast(I32),
+                in_=wd_scales[:, 4 * q : 4 * q + 4, :].rearrange("g r n -> r g n").bitcast(I32),
+            )
+        pos3_sb = load_list(pos3, "pos3_sb")
+        pos4_sb = load_list(pos4, "pos4_sb")
+
+        y_acc = [psum.tile([P, M1], F32, name=f"y_acc{nt}") for nt in range(N_TILES)]
+
+        def interleaved_in(x):
+            return x[:].rearrange("p t (c i) -> p c t i", i=PACK)
+
+        def interleaved_out(x):
+            return x[:].rearrange("p (c i t) -> p c t i", i=PACK, t=PACK)
+
+        hs = {}
+        for t in range(PACK):
+            hs[0, t] = first_stage(0, t)
+            if t % 2 == 0:
+                prepare_w1(1, t // 2)
+        for g in range(H_PASSES):
+            x1 = ring.tile([P, PACK, M1], F32, name="x1")
+            x2 = ring.tile([P, PACK, M1], F32, name="x2")
+            for t in range(PACK):
+                nc.vector.tensor_copy(x1[:, t, :], hs[g, t][:].indirect(pos1_sb[:]))
+                nc.vector.tensor_copy(x2[:, t, :], hs[g, t][:].indirect(pos2_sb[:]))
+            if g + 1 < H_PASSES:
+                for t in range(PACK):
+                    hs[g + 1, t] = first_stage(g + 1, t)
+                    if g + 2 < H_PASSES and t % 2 == 0:
+                        prepare_w1(g + 2, t // 2)
+            diff = ring.tile([P, PACK * M1], BF16, name="diff", bufs=1, align_bytes=64)
+            nc.vector.tensor_tensor(interleaved_out(diff), interleaved_in(x1), interleaved_in(x2), ALU.subtract)
+            prod = ring.tile([P, PACK * M1], BF16, name="prod", bufs=1, align_bytes=64)
+            nc.vector.tensor_tensor(interleaved_out(prod), interleaved_in(x1), interleaved_in(x2), ALU.mult)
+            dist = ring.tile([P, PACK * M1], BF16, name="dist", bufs=1, align_bytes=64)
+            nc.scalar.activation(dist[:], diff[:], ACT.Abs)
+            wb_codes, wb_scales = quantize(round_wb(wb_raw[g]), f"wb_{g}")
+            b_codes, b_scales = quantize(prod, f"b_{g}")
+            d_codes, d_scales = quantize(dist, f"d_{g}")
+            for nt in range(N_TILES):
+                nc.tensor.matmul_mx(
+                    out=y_acc[nt][:],
+                    lhsT=wb_codes[:, nt * P : (nt + 1) * P].bitcast(FP8X4),
+                    lhsT_scale=wb_scales[:, nt * P : (nt + 1) * P],
+                    rhs=b_codes[:].bitcast(FP8X4),
+                    rhs_scale=b_scales[:],
+                    start=(g == 0),
+                    stop=False,
+                )
+            for nt in range(N_TILES):
+                nc.tensor.matmul_mx(
+                    out=y_acc[nt][:],
+                    lhsT=wd_sb[:, g, 2 * nt * P : 2 * (nt + 1) * P].bitcast(FP4X4),
+                    lhsT_scale=wd_planes[:, g, nt * P : (nt + 1) * P],
+                    rhs=d_codes[:].bitcast(FP8X4),
+                    rhs_scale=d_scales[:],
+                    start=False,
+                    stop=(g == H_PASSES - 1),
+                )
+
+        for nt in range(N_TILES):
+            y = ring.tile([P, M1], F32, name="y", bufs=4)
+            nc.scalar.copy(y[:], y_acc[nt][:])
+            first = ring.tile([P, M2], F32, name="first")
+            second = ring.tile([P, M2], F32, name="second")
+            nc.vector.tensor_copy(first[:], y[:].indirect(pos3_sb[:]))
+            nc.vector.tensor_copy(second[:], y[:].indirect(pos4_sb[:]))
+            top = ring.tile([P, M2], F32, name="top")
+            nc.vector.tensor_tensor(top[:], first[:], second[:], ALU.max)
+            squared = ring.tile([P, M2], F32, name="squared")
+            nc.scalar.activation(squared[:], top[:], ACT.Square)
+            score = ring.tile([P, M2], F32, name="score", bufs=4)
+            nc.scalar.activation(score[:], squared[:], ACT.Copy, bias=1.0)
+            nc.sync.dma_start(out=out[nt * P : (nt + 1) * P, :], in_=score[:])

@@ -1,6 +1,7 @@
 from contextlib import ExitStack
 
 import concourse.mybir as mybir
+from concourse.masks import make_identity
 
 K, H, N, T, S, M1, M2 = 1024, 1536, 512, 2048, 1024, 512, 256
 FLOPS = 2 * K * H * S + 2 * 2 * H * N * M1
@@ -23,6 +24,9 @@ BANK = 512
 K_PASSES = K // PASS
 H_PASSES = H // PASS
 N_TILES = N // P
+M_TILES = M1 // P
+H_SLOTS = 4
+RAW_BUFS = 3
 
 
 def tile_list_subtitle_couple_score_kernel(
@@ -39,69 +43,91 @@ def tile_list_subtitle_couple_score_kernel(
             nc.sync.dma_start(tile[:], src)
             return tile
 
-        def load_rows(src, g, cols):
-            raw = ring.tile([P, PACK, PASS], F32, name="raw", bufs=5)
+        def load_rows(src, g, c0, width, name, bufs):
+            raw = ring.tile([P, PACK, width], F32, name=name, bufs=bufs)
             nc.sync.dma_start(
-                out=raw[:], in_=src[g * PASS : (g + 1) * PASS, cols].rearrange("(p j) c -> p j c", j=PACK)
+                out=raw[:],
+                in_=src[g * PASS : (g + 1) * PASS, c0 : c0 + width].rearrange("(p j) c -> p j c", j=PACK),
             )
             return raw
 
-        def quantize(grouped, name):
+        def quantize(grouped, name, pieces=1):
             codes = keep.tile([P, PASS], U32, name=name + "_codes", align_bytes=64)
             scales = keep.tile([P, PASS], U8, name=name + "_scales", align_bytes=64)
-            nc.vector.quantize_mx(out=codes[:].bitcast(FP8X4), scales=scales[:], in_=grouped[:])
+            width = PASS // pieces
+            for piece in range(pieces):
+                nc.vector.quantize_mx(
+                    out=codes[:, piece * width : (piece + 1) * width].bitcast(FP8X4),
+                    scales=scales[:, piece * width : (piece + 1) * width],
+                    in_=grouped[:, piece * width * PACK : (piece + 1) * width * PACK],
+                )
             return codes, scales
 
+        def new_grouped():
+            return ring.tile([P, PACK * PASS], BF16, name="w_grouped", bufs=3, align_bytes=64)
+
+        def w1_views(grouped, raw, m0):
+            ms = raw.shape[2] // PACK
+            dst = grouped[:].rearrange("p (t m j) -> p m j t", t=PACK, j=PACK)[:, m0 : m0 + ms]
+            return dst, raw[:].rearrange("p j (m t) -> p m j t", t=PACK)
+
         def round_w1(raw):
-            grouped = ring.tile([P, PACK * PASS], BF16, name="w_grouped", bufs=3, align_bytes=64)
-            nc.scalar.activation(
-                grouped[:].rearrange("p (t m j) -> p m j t", t=PACK, j=PACK),
-                raw[:].rearrange("p j (m t) -> p m j t", t=PACK),
-                ACT.Copy,
-            )
+            grouped = new_grouped()
+            dst, src = w1_views(grouped, raw, 0)
+            nc.scalar.activation(dst, src, ACT.Copy)
             return grouped
 
         def round_wb(raw):
-            grouped = ring.tile([P, PACK * PASS], BF16, name="w_grouped", bufs=3, align_bytes=64)
+            grouped = new_grouped()
             nc.scalar.activation(
                 grouped[:].rearrange("p (c i j) -> p c j i", i=PACK, j=PACK),
                 raw[:].rearrange("p j (c i) -> p c j i", i=PACK),
                 ACT.Copy,
+                scale=-1.0,
             )
             return grouped
 
         tab_planes = keep.tile([P, T], U8, name="tab_planes", align_bytes=64)
-        nc.vector.memset(tab_planes[:].bitcast(I32), 0)
+        nc.gpsimd.memset(tab_planes[:].bitcast(I32), 0)
         wd_planes = keep.tile([P, H_PASSES, N], U8, name="wd_planes", align_bytes=64)
         nc.gpsimd.memset(wd_planes[:].rearrange("p g n -> p (g n)").bitcast(I32), 0)
+        identity = keep.tile([P, P], F32, name="identity")
+        make_identity(nc, identity[:])
+        h_tiles = [keep.tile([P, 2 * S], F32, name=f"h{i}") for i in range(H_SLOTS)]
+        for i, h in enumerate(h_tiles):
+            (nc.vector if i < H_SLOTS // 2 else nc.gpsimd).memset(h[:, S:], 0.0)
 
-        offs_sb = load_list(offs, "offs_sb")
-        tab_sb = []
-        for a in range(K_PASSES):
+        def load_table(a):
             words = keep.tile([P, T], I32, name=f"tab_sb{a}", align_bytes=64)
             nc.sync.dma_start(out=words[:], in_=tab_words[a].rearrange("p t i -> p (t i)").bitcast(I32))
-            tab_sb.append(words)
-            if a == 0:
-                for q in range(4):
-                    nc.sync.dma_start(
-                        out=tab_planes[32 * q : 32 * q + 4 * K_PASSES, :].bitcast(I32),
-                        in_=tab_scales[:, 4 * q : 4 * q + 4, :].bitcast(I32),
-                    )
-        w1_raw = {}
-        for g in range(H_PASSES):
-            for a in range(K_PASSES):
-                w1_raw[g, a] = load_rows(w1, a, slice(g * PASS, (g + 1) * PASS))
-            if g == 0:
-                pos1_sb = load_list(pos1, "pos1_sb")
-                pos2_sb = load_list(pos2, "pos2_sb")
+            return words
 
-        v_codes = []
-        for a in range(K_PASSES):
-            picked = keep.tile([P, S], U32, name=f"v_codes{a}", align_bytes=64)
-            nc.vector.tensor_copy(picked[:], tab_sb[a][:].bitcast(U32).indirect(offs_sb[:]))
-            v_codes.append(picked)
+        offs_sb = load_list(offs, "offs_sb")
+        tab_sb = [load_table(0)]
+        for q in range(4):
+            nc.sync.dma_start(
+                out=tab_planes[32 * q : 32 * q + 4 * K_PASSES, :].bitcast(I32),
+                in_=tab_scales[:, 4 * q : 4 * q + 4, :].bitcast(I32),
+            )
+        tab_sb.append(load_table(1))
+        w1_raw = {}
+        w1_halves = [
+            [load_rows(w1, a, half * PASS // 2, PASS // 2, "raw_half", 4) for half in range(2)] for a in range(K_PASSES)
+        ]
+        pos1_sb = load_list(pos1, "pos1_sb")
+        pos2_sb = load_list(pos2, "pos2_sb")
+        wb_raw = []
+        for g in range(1, H_PASSES):
+            for a in range(K_PASSES):
+                w1_raw[g, a] = load_rows(w1, a, g * PASS, PASS, "raw", RAW_BUFS)
+            wb_raw.append(load_rows(wb, g - 1, 0, N, "raw", RAW_BUFS))
+        wb_raw.append(load_rows(wb, H_PASSES - 1, 0, N, "raw", RAW_BUFS))
+
+        v_codes = [keep.tile([P, S], U32, name=f"v_codes{a}", align_bytes=64) for a in range(K_PASSES)]
         v_planes = keep.tile([P, S], U8, name="v_planes", align_bytes=64)
+        nc.vector.tensor_copy(v_codes[0][:], tab_sb[0][:].bitcast(U32).indirect(offs_sb[:]))
         nc.vector.tensor_copy(v_planes[:], tab_planes[:].indirect(offs_sb[:]))
+        nc.vector.tensor_copy(v_codes[1][:], tab_sb[1][:].bitcast(U32).indirect(offs_sb[:]))
 
         w1_mx = {}
 
@@ -109,11 +135,12 @@ def tile_list_subtitle_couple_score_kernel(
             w1_mx[g, a] = quantize(round_w1(w1_raw[g, a]), f"w1_{g}_{a}")
 
         def first_stage(g, t):
-            h = ring.tile([P, S], F32, name="h", bufs=6)
+            h = h_tiles[(g * PACK + t) % H_SLOTS]
             for half in range(S // BANK):
                 cols = slice(half * BANK, (half + 1) * BANK)
-                acc = psum.tile([P, BANK], F32, name="h_acc", bufs=4)
-                for a in range(K_PASSES):
+                acc = psum.tile([P, BANK], F32, name="acc", bufs=4)
+                order = list(range(K_PASSES)) if (g, t) == (0, 0) else list(reversed(range(K_PASSES)))
+                for a in order:
                     codes, scales = w1_mx[g, a]
                     nc.tensor.matmul_mx(
                         out=acc[:],
@@ -121,16 +148,22 @@ def tile_list_subtitle_couple_score_kernel(
                         lhsT_scale=scales[:, t * P : (t + 1) * P],
                         rhs=v_codes[a][:, cols].bitcast(FP8X4),
                         rhs_scale=v_planes[4 * a : P, cols],
-                        start=(a == 0),
-                        stop=(a == K_PASSES - 1),
+                        start=(a == order[0]),
+                        stop=(a == order[-1]),
                     )
-                nc.scalar.copy(h[:, cols], acc[:])
+                if (g, t, half) == (0, 0, 1):
+                    nc.vector.tensor_copy(h[:, cols], acc[:])
+                else:
+                    nc.scalar.copy(h[:, cols], acc[:])
             return h
 
         for a in range(K_PASSES):
-            prepare_w1(0, a)
+            grouped = new_grouped()
+            for half in range(2):
+                dst, src = w1_views(grouped, w1_halves[a][half], half * P // 2)
+                nc.scalar.activation(dst, src, ACT.Copy)
+            w1_mx[0, a] = quantize(grouped, f"w1_0_{a}", pieces=PACK)
 
-        wb_raw = [load_rows(wb, g, slice(0, N)) for g in range(H_PASSES)]
         wd_sb = keep.tile([P, H_PASSES, 2 * N], U8, name="wd_sb", align_bytes=64)
         nc.sync.dma_start(out=wd_sb[:].bitcast(I32), in_=wd_words.rearrange("g p c -> p g c").bitcast(I32))
         for q in range(4):
@@ -141,69 +174,162 @@ def tile_list_subtitle_couple_score_kernel(
         pos3_sb = load_list(pos3, "pos3_sb")
         pos4_sb = load_list(pos4, "pos4_sb")
 
-        y_acc = [psum.tile([P, M1], F32, name=f"y_acc{nt}") for nt in range(N_TILES)]
-
         def interleaved_in(x):
             return x[:].rearrange("p t (c i) -> p c t i", i=PACK)
 
         def interleaved_out(x):
             return x[:].rearrange("p (c i t) -> p c t i", i=PACK, t=PACK)
 
-        hs = {}
-        for t in range(PACK):
-            hs[0, t] = first_stage(0, t)
-            if t % 2 == 0:
-                prepare_w1(1, t // 2)
-        for g in range(H_PASSES):
-            x1 = ring.tile([P, PACK, M1], F32, name="x1")
-            x2 = ring.tile([P, PACK, M1], F32, name="x2")
-            for t in range(PACK):
-                nc.vector.tensor_copy(x1[:, t, :], hs[g, t][:].indirect(pos1_sb[:]))
-                nc.vector.tensor_copy(x2[:, t, :], hs[g, t][:].indirect(pos2_sb[:]))
-            if g + 1 < H_PASSES:
-                for t in range(PACK):
-                    hs[g + 1, t] = first_stage(g + 1, t)
-                    if g + 2 < H_PASSES and t % 2 == 0:
-                        prepare_w1(g + 2, t // 2)
-            diff = ring.tile([P, PACK * M1], BF16, name="diff", bufs=1, align_bytes=64)
-            nc.vector.tensor_tensor(interleaved_out(diff), interleaved_in(x1), interleaved_in(x2), ALU.subtract)
+        def distances(x1, x2):
+            dist = ring.tile([P, PACK * M1], BF16, name="dist", bufs=1, align_bytes=64)
+            dist_words = dist[:].bitcast(F32)
+            for pair in range(M_TILES // 2):
+                back = psum.tile([P, 2, 2, P], F32, name="back", bufs=2)
+                for jj in range(2):
+                    cols = slice((2 * pair + jj) * P, (2 * pair + jj + 1) * P)
+                    diff = psum.tile([P, PACK, P], F32, name="diff", bufs=2)
+                    for t in range(PACK):
+                        for x, first in ((x1, True), (x2, False)):
+                            nc.tensor.matmul(
+                                diff[:, t, :], lhsT=x[:, t, cols], rhs=identity[:],
+                                is_transpose=True, start=first, stop=not first,
+                            )
+                    turned = ring.tile([P, 2, P, 2], BF16, name="turned", bufs=4)
+                    nc.scalar.activation(turned[:], diff[:].rearrange("m (u e) p -> m u p e", e=2), ACT.Abs)
+                    turned_words = turned[:].rearrange("m u p e -> m (u p e)").bitcast(F32)
+                    for u in range(2):
+                        nc.tensor.transpose(back[:, jj, u, :], turned_words[:, u * P : (u + 1) * P], identity[:])
+                nc.scalar.copy(
+                    dist_words[:, pair * BANK : (pair + 1) * BANK].rearrange("p (jj m u) -> p jj m u", jj=2, u=2),
+                    back[:].rearrange("p jj u m -> p jj m u"),
+                )
+            return dist
+
+        hs, xs, wb_mx, b_mx, d_mx = {}, {}, {}, {}, {}
+
+        def evac(g, t):
+            hs[g, t] = first_stage(g, t)
+
+        def pick(g, t):
+            if t == 0:
+                xs[g] = (ring.tile([P, PACK, M1], F32, name="x1"), ring.tile([P, PACK, M1], F32, name="x2"))
+            x1, x2 = xs[g]
+            nc.vector.tensor_copy(x1[:, t, :], hs[g, t][:].indirect(pos1_sb[:]))
+            nc.vector.tensor_scalar(x2[:, t, :], hs[g, t][:].indirect(pos2_sb[:]), -1.0, 0.0, ALU.mult, ALU.add)
+
+        def products(g):
+            x1, x2 = xs[g]
             prod = ring.tile([P, PACK * M1], BF16, name="prod", bufs=1, align_bytes=64)
             nc.vector.tensor_tensor(interleaved_out(prod), interleaved_in(x1), interleaved_in(x2), ALU.mult)
+            b_mx[g] = quantize(prod, f"b_{g}")
+
+        def prepare_wb(g):
+            wb_mx[g] = quantize(round_wb(wb_raw[g]), f"wb_{g}")
+
+        def prepare_d(g):
+            d_mx[g] = quantize(distances(*xs[g]), f"d_{g}")
+
+        def b_pass(g, nt, start, stop):
+            nc.tensor.matmul_mx(
+                out=y_acc[nt][:],
+                lhsT=wb_mx[g][0][:, nt * P : (nt + 1) * P].bitcast(FP8X4),
+                lhsT_scale=wb_mx[g][1][:, nt * P : (nt + 1) * P],
+                rhs=b_mx[g][0][:].bitcast(FP8X4),
+                rhs_scale=b_mx[g][1][:],
+                start=start,
+                stop=stop,
+            )
+
+        def d_pass(g, nt, start, stop):
+            nc.tensor.matmul_mx(
+                out=y_acc[nt][:],
+                lhsT=wd_sb[:, g, 2 * nt * P : 2 * (nt + 1) * P].bitcast(FP4X4),
+                lhsT_scale=wd_planes[:, g, nt * P : (nt + 1) * P],
+                rhs=d_mx[g][0][:].bitcast(FP8X4),
+                rhs_scale=d_mx[g][1][:],
+                start=start,
+                stop=stop,
+            )
+
+        def second_stage(g):
+            for nt in range(N_TILES):
+                b_pass(g, nt, g == 0, False)
+            for nt in range(N_TILES):
+                d_pass(g, nt, False, False)
+
+        def last_group(g):
+            x1, x2 = xs[g]
+            diff = ring.tile([P, PACK * M1], BF16, name="last_diff", bufs=1, align_bytes=64)
             dist = ring.tile([P, PACK * M1], BF16, name="dist", bufs=1, align_bytes=64)
-            nc.scalar.activation(dist[:], diff[:], ACT.Abs)
-            wb_codes, wb_scales = quantize(round_wb(wb_raw[g]), f"wb_{g}")
-            b_codes, b_scales = quantize(prod, f"b_{g}")
-            d_codes, d_scales = quantize(dist, f"d_{g}")
-            for nt in range(N_TILES):
-                nc.tensor.matmul_mx(
-                    out=y_acc[nt][:],
-                    lhsT=wb_codes[:, nt * P : (nt + 1) * P].bitcast(FP8X4),
-                    lhsT_scale=wb_scales[:, nt * P : (nt + 1) * P],
-                    rhs=b_codes[:].bitcast(FP8X4),
-                    rhs_scale=b_scales[:],
-                    start=(g == 0),
-                    stop=False,
+            prod = ring.tile([P, PACK * M1], BF16, name="prod", bufs=1, align_bytes=64)
+            quads = M1 // PACK // 2
+            halves = [slice(half * quads, (half + 1) * quads) for half in range(2)]
+            flat = [slice(half * PACK * M1 // 2, (half + 1) * PACK * M1 // 2) for half in range(2)]
+
+            def combine(dst, half, op):
+                c = halves[half]
+                nc.vector.tensor_tensor(
+                    interleaved_out(dst)[:, c], interleaved_in(x1)[:, c], interleaved_in(x2)[:, c], op
                 )
+
+            for half in range(2):
+                combine(diff, half, ALU.add)
+                nc.scalar.activation(dist[:, flat[half]], diff[:, flat[half]], ACT.Abs)
+            combine(prod, 0, ALU.mult)
+            d_mx[g] = quantize(dist, f"d_{g}")
+            combine(prod, 1, ALU.mult)
+            b_mx[g] = quantize(prod, f"b_{g}", pieces=2)
             for nt in range(N_TILES):
-                nc.tensor.matmul_mx(
-                    out=y_acc[nt][:],
-                    lhsT=wd_sb[:, g, 2 * nt * P : 2 * (nt + 1) * P].bitcast(FP4X4),
-                    lhsT_scale=wd_planes[:, g, nt * P : (nt + 1) * P],
-                    rhs=d_codes[:].bitcast(FP8X4),
-                    rhs_scale=d_scales[:],
-                    start=False,
-                    stop=(g == H_PASSES - 1),
-                )
+                d_pass(g, nt, False, False)
+            for nt in range(N_TILES):
+                b_pass(g, nt, False, True)
+
+        evac(0, 0)
+        evac(0, 1)
+        prepare_w1(1, 0)
+        evac(0, 2)
+        prepare_w1(1, 1)
+        evac(0, 3)
+        for t in range(PACK):
+            pick(0, t)
+        products(0)
+        prepare_wb(0)
+        evac(1, 0)
+        evac(1, 1)
+        prepare_w1(2, 0)
+        prepare_w1(2, 1)
+        evac(1, 2)
+        evac(1, 3)
+        prepare_d(0)
+        for t in range(PACK):
+            pick(1, t)
+        products(1)
+        evac(2, 0)
+        evac(2, 1)
+        prepare_wb(1)
+        prepare_d(1)
+        evac(2, 2)
+        evac(2, 3)
+        prepare_wb(2)
+        y_acc = [psum.tile([P, M1], F32, name=f"y_acc{nt}", tag="acc", bufs=4) for nt in range(N_TILES)]
+        second_stage(0)
+        second_stage(1)
+        for t in range(PACK):
+            pick(2, t)
+        last_group(2)
 
         for nt in range(N_TILES):
             y = ring.tile([P, M1], F32, name="y", bufs=4)
-            nc.scalar.copy(y[:], y_acc[nt][:])
+            if nt == 0:
+                nc.vector.tensor_copy(y[:], y_acc[nt][:])
+            else:
+                nc.scalar.copy(y[:], y_acc[nt][:])
             first = ring.tile([P, M2], F32, name="first")
-            second = ring.tile([P, M2], F32, name="second")
+            other = ring.tile([P, M2], F32, name="other")
             nc.vector.tensor_copy(first[:], y[:].indirect(pos3_sb[:]))
-            nc.vector.tensor_copy(second[:], y[:].indirect(pos4_sb[:]))
+            nc.vector.tensor_copy(other[:], y[:].indirect(pos4_sb[:]))
             top = ring.tile([P, M2], F32, name="top")
-            nc.vector.tensor_tensor(top[:], first[:], second[:], ALU.max)
+            nc.vector.tensor_tensor(top[:], first[:], other[:], ALU.max)
             squared = ring.tile([P, M2], F32, name="squared")
             nc.scalar.activation(squared[:], top[:], ACT.Square)
             score = ring.tile([P, M2], F32, name="score", bufs=4)

@@ -27,6 +27,7 @@ N_TILES = N // P
 M_TILES = M1 // P
 H_SLOTS = 4
 RAW_BUFS = 3
+SIDE_PIECES = 4
 
 
 def tile_list_subtitle_couple_score_kernel(
@@ -151,7 +152,7 @@ def tile_list_subtitle_couple_score_kernel(
                         start=(a == order[0]),
                         stop=(a == order[-1]),
                     )
-                if (g, t, half) == (0, 0, 1):
+                if (g, t) == (0, 0):
                     nc.vector.tensor_copy(h[:, cols], acc[:])
                 else:
                     nc.scalar.copy(h[:, cols], acc[:])
@@ -180,9 +181,8 @@ def tile_list_subtitle_couple_score_kernel(
         def interleaved_out(x):
             return x[:].rearrange("p (c i t) -> p c t i", i=PACK, t=PACK)
 
-        def distances(x1, x2):
-            dist = ring.tile([P, PACK * M1], BF16, name="dist", bufs=1, align_bytes=64)
-            dist_words = dist[:].bitcast(F32)
+        def distances(x1, x2, dist):
+            dist_words = dist.bitcast(F32)
             for pair in range(M_TILES // 2):
                 back = psum.tile([P, 2, 2, P], F32, name="back", bufs=2)
                 for jj in range(2):
@@ -203,7 +203,6 @@ def tile_list_subtitle_couple_score_kernel(
                     dist_words[:, pair * BANK : (pair + 1) * BANK].rearrange("p (jj m u) -> p jj m u", jj=2, u=2),
                     back[:].rearrange("p jj u m -> p jj m u"),
                 )
-            return dist
 
         hs, xs, wb_mx, b_mx, d_mx = {}, {}, {}, {}, {}
 
@@ -217,17 +216,29 @@ def tile_list_subtitle_couple_score_kernel(
             nc.vector.tensor_copy(x1[:, t, :], hs[g, t][:].indirect(pos1_sb[:]))
             nc.vector.tensor_scalar(x2[:, t, :], hs[g, t][:].indirect(pos2_sb[:]), -1.0, 0.0, ALU.mult, ALU.add)
 
+        pairs = {}
+
         def products(g):
             x1, x2 = xs[g]
-            prod = ring.tile([P, PACK * M1], BF16, name="prod", bufs=1, align_bytes=64)
-            nc.vector.tensor_tensor(interleaved_out(prod), interleaved_in(x1), interleaved_in(x2), ALU.mult)
-            b_mx[g] = quantize(prod, f"b_{g}")
+            pairs[g] = ring.tile([P, 2 * PACK * M1], BF16, name="pair", bufs=2, align_bytes=64)
+            prod = pairs[g][:, PACK * M1 :]
+            quads = M1 // PACK // SIDE_PIECES
+            for piece in range(SIDE_PIECES):
+                c = slice(piece * quads, (piece + 1) * quads)
+                nc.gpsimd.tensor_tensor(
+                    interleaved_out(prod)[:, c], interleaved_in(x1)[:, c], interleaved_in(x2)[:, c], ALU.mult
+                )
 
         def prepare_wb(g):
             wb_mx[g] = quantize(round_wb(wb_raw[g]), f"wb_{g}")
 
         def prepare_d(g):
-            d_mx[g] = quantize(distances(*xs[g]), f"d_{g}")
+            distances(*xs[g], pairs[g][:, : PACK * M1])
+            codes = keep.tile([P, 2 * M1], U32, name=f"pair_codes{g}", align_bytes=64)
+            scales = keep.tile([P, 2 * M1], U8, name=f"pair_scales{g}", align_bytes=64)
+            nc.vector.quantize_mx(out=codes[:].bitcast(FP8X4), scales=scales[:], in_=pairs[g][:])
+            d_mx[g] = codes[:, :M1], scales[:, :M1]
+            b_mx[g] = codes[:, M1:], scales[:, M1:]
 
         def b_pass(g, nt, start, stop):
             nc.tensor.matmul_mx(
@@ -306,10 +317,10 @@ def tile_list_subtitle_couple_score_kernel(
         products(1)
         evac(2, 0)
         evac(2, 1)
-        prepare_wb(1)
         prepare_d(1)
         evac(2, 2)
         evac(2, 3)
+        prepare_wb(1)
         prepare_wb(2)
         y_acc = [psum.tile([P, M1], F32, name=f"y_acc{nt}", tag="acc", bufs=4) for nt in range(N_TILES)]
         second_stage(0)

@@ -26,7 +26,7 @@ H_PASSES = H // PASS
 N_TILES = N // P
 M_TILES = M1 // P
 H_SLOTS = 4
-RAW_BUFS = 3
+RAW_BUFS = 4
 SIDE_PIECES = 4
 
 
@@ -65,20 +65,28 @@ def tile_list_subtitle_couple_score_kernel(
             return codes, scales
 
         def new_grouped():
-            return ring.tile([P, PACK * PASS], BF16, name="w_grouped", bufs=3, align_bytes=64)
-
-        def w1_views(grouped, raw, m0):
-            ms = raw.shape[2] // PACK
-            dst = grouped[:].rearrange("p (t m j) -> p m j t", t=PACK, j=PACK)[:, m0 : m0 + ms]
-            return dst, raw[:].rearrange("p j (m t) -> p m j t", t=PACK)
+            return ring.tile([P, PACK * PASS], BF16, name="w_grouped", bufs=4, align_bytes=64)
 
         def round_w1(raw):
             grouped = new_grouped()
-            dst, src = w1_views(grouped, raw, 0)
-            nc.scalar.activation(dst, src, ACT.Copy)
+            nc.scalar.activation(
+                grouped[:].rearrange("p (t m j) -> p m j t", t=PACK, j=PACK),
+                raw[:].rearrange("p j (m t) -> p m j t", t=PACK),
+                ACT.Copy,
+            )
             return grouped
 
         def round_wb(raw):
+            grouped = new_grouped()
+            dst = grouped[:].rearrange("p (n j) -> p n j", j=PACK)
+            src = raw[:].rearrange("p j n -> p n j")
+            width = N // SIDE_PIECES
+            for piece in range(SIDE_PIECES):
+                cols = slice(piece * width, (piece + 1) * width)
+                nc.gpsimd.tensor_scalar(dst[:, cols], src[:, cols], -1.0, 0.0, ALU.mult, ALU.add)
+            return grouped
+
+        def round_wb_scalar(raw):
             grouped = new_grouped()
             nc.scalar.activation(
                 grouped[:].rearrange("p (c i j) -> p c j i", i=PACK, j=PACK),
@@ -117,12 +125,14 @@ def tile_list_subtitle_couple_score_kernel(
         ]
         pos1_sb = load_list(pos1, "pos1_sb")
         pos2_sb = load_list(pos2, "pos2_sb")
-        wb_raw = []
+        wb_raw = {}
+        for a in range(K_PASSES):
+            w1_raw[1, a] = load_rows(w1, a, PASS, PASS, "raw", RAW_BUFS)
+        w1_raw[2, 0] = load_rows(w1, 0, 2 * PASS, PASS, "raw", RAW_BUFS)
+        wb_raw[0] = load_rows(wb, 0, 0, N, "raw", RAW_BUFS)
+        w1_raw[2, 1] = load_rows(w1, 1, 2 * PASS, PASS, "raw", RAW_BUFS)
         for g in range(1, H_PASSES):
-            for a in range(K_PASSES):
-                w1_raw[g, a] = load_rows(w1, a, g * PASS, PASS, "raw", RAW_BUFS)
-            wb_raw.append(load_rows(wb, g - 1, 0, N, "raw", RAW_BUFS))
-        wb_raw.append(load_rows(wb, H_PASSES - 1, 0, N, "raw", RAW_BUFS))
+            wb_raw[g] = load_rows(wb, g, 0, N, "raw", RAW_BUFS)
 
         v_codes = [keep.tile([P, S], U32, name=f"v_codes{a}", align_bytes=64) for a in range(K_PASSES)]
         v_planes = keep.tile([P, S], U8, name="v_planes", align_bytes=64)
@@ -133,7 +143,9 @@ def tile_list_subtitle_couple_score_kernel(
         w1_mx = {}
 
         def prepare_w1(g, a):
-            w1_mx[g, a] = quantize(round_w1(w1_raw[g, a]), f"w1_{g}_{a}")
+            codes, scales = quantize(round_w1(w1_raw[g, a]), f"w1_{g}_{a}")
+            for t in range(PACK):
+                w1_mx[g, a, t] = codes[:, t * P : (t + 1) * P], scales[:, t * P : (t + 1) * P]
 
         def first_stage(g, t):
             h = h_tiles[(g * PACK + t) % H_SLOTS]
@@ -142,11 +154,11 @@ def tile_list_subtitle_couple_score_kernel(
                 acc = psum.tile([P, BANK], F32, name="acc", bufs=4)
                 order = list(range(K_PASSES)) if (g, t) == (0, 0) else list(reversed(range(K_PASSES)))
                 for a in order:
-                    codes, scales = w1_mx[g, a]
+                    codes, scales = w1_mx[g, a, t]
                     nc.tensor.matmul_mx(
                         out=acc[:],
-                        lhsT=codes[:, t * P : (t + 1) * P].bitcast(FP8X4),
-                        lhsT_scale=scales[:, t * P : (t + 1) * P],
+                        lhsT=codes.bitcast(FP8X4),
+                        lhsT_scale=scales,
                         rhs=v_codes[a][:, cols].bitcast(FP8X4),
                         rhs_scale=v_planes[4 * a : P, cols],
                         start=(a == order[0]),
@@ -158,12 +170,32 @@ def tile_list_subtitle_couple_score_kernel(
                     nc.scalar.copy(h[:, cols], acc[:])
             return h
 
+        head = ring.tile([P, 2 * PACK * PASS], BF16, name="pair", bufs=2, align_bytes=64)
+        head_dst = head[:].rearrange("p (t a m j) -> p a m j t", t=PACK, a=K_PASSES, j=PACK)
+        head_codes = keep.tile([P, K_PASSES * PASS], U32, name="head_codes", align_bytes=64)
+        head_scales = keep.tile([P, K_PASSES * PASS], U8, name="head_scales", align_bytes=64)
+
+        def quantize_head(c0, c1):
+            nc.vector.quantize_mx(
+                out=head_codes[:, c0:c1].bitcast(FP8X4), scales=head_scales[:, c0:c1], in_=head[:, PACK * c0 : PACK * c1]
+            )
+
         for a in range(K_PASSES):
-            grouped = new_grouped()
             for half in range(2):
-                dst, src = w1_views(grouped, w1_halves[a][half], half * P // 2)
-                nc.scalar.activation(dst, src, ACT.Copy)
-            w1_mx[0, a] = quantize(grouped, f"w1_0_{a}", pieces=PACK)
+                dst = head_dst[:, a, half * P // 2 : (half + 1) * P // 2]
+                src = w1_halves[a][half][:].rearrange("p j (m t) -> p m j t", t=PACK)
+                if (a, half) == (K_PASSES - 1, 1):
+                    nc.scalar.activation(dst[:, : P // 4], src[:, : P // 4], ACT.Copy)
+                    nc.vector.tensor_copy(dst[:, P // 4 :], src[:, P // 4 :])
+                else:
+                    nc.scalar.activation(dst, src, ACT.Copy)
+            quantize_head(a * P, (a + 1) * P)
+        for t in range(1, PACK):
+            quantize_head(t * K_PASSES * P, (t + 1) * K_PASSES * P)
+        for t in range(PACK):
+            for a in range(K_PASSES):
+                cols = slice((t * K_PASSES + a) * P, (t * K_PASSES + a + 1) * P)
+                w1_mx[0, a, t] = head_codes[:, cols], head_scales[:, cols]
 
         wd_sb = keep.tile([P, H_PASSES, 2 * N], U8, name="wd_sb", align_bytes=64)
         nc.sync.dma_start(out=wd_sb[:].bitcast(I32), in_=wd_words.rearrange("g p c -> p g c").bitcast(I32))
@@ -230,7 +262,7 @@ def tile_list_subtitle_couple_score_kernel(
                 )
 
         def prepare_wb(g):
-            wb_mx[g] = quantize(round_wb(wb_raw[g]), f"wb_{g}")
+            wb_mx[g] = quantize((round_wb if g == 0 else round_wb_scalar)(wb_raw[g]), f"wb_{g}")
 
         def prepare_d(g):
             distances(*xs[g], pairs[g][:, : PACK * M1])
@@ -271,56 +303,53 @@ def tile_list_subtitle_couple_score_kernel(
         def last_group(g):
             x1, x2 = xs[g]
             diff = ring.tile([P, PACK * M1], BF16, name="last_diff", bufs=1, align_bytes=64)
-            dist = ring.tile([P, PACK * M1], BF16, name="dist", bufs=1, align_bytes=64)
-            prod = ring.tile([P, PACK * M1], BF16, name="prod", bufs=1, align_bytes=64)
-            quads = M1 // PACK // 2
-            halves = [slice(half * quads, (half + 1) * quads) for half in range(2)]
-            flat = [slice(half * PACK * M1 // 2, (half + 1) * PACK * M1 // 2) for half in range(2)]
+            pair = ring.tile([P, 2 * PACK * M1], BF16, name="pair", bufs=2, align_bytes=64)
+            dist, prod = pair[:, : PACK * M1], pair[:, PACK * M1 :]
+            quads = M1 // PACK
 
-            def combine(dst, half, op):
-                c = halves[half]
+            def combine(dst, c0, c1, op):
                 nc.vector.tensor_tensor(
-                    interleaved_out(dst)[:, c], interleaved_in(x1)[:, c], interleaved_in(x2)[:, c], op
+                    interleaved_out(dst)[:, c0:c1], interleaved_in(x1)[:, c0:c1], interleaved_in(x2)[:, c0:c1], op
                 )
 
-            for half in range(2):
-                combine(diff, half, ALU.add)
-                nc.scalar.activation(dist[:, flat[half]], diff[:, flat[half]], ACT.Abs)
-            combine(prod, 0, ALU.mult)
+            for c0, c1 in ((0, quads // 2), (quads // 2, quads)):
+                combine(diff, c0, c1, ALU.add)
+                flat = slice(c0 * PACK * PACK, c1 * PACK * PACK)
+                nc.scalar.activation(dist[:, flat], diff[:, flat], ACT.Abs)
+            combine(prod, 0, 3 * quads // 4, ALU.mult)
             d_mx[g] = quantize(dist, f"d_{g}")
-            combine(prod, 1, ALU.mult)
+            combine(prod, 3 * quads // 4, quads, ALU.mult)
             b_mx[g] = quantize(prod, f"b_{g}", pieces=2)
             for nt in range(N_TILES):
                 d_pass(g, nt, False, False)
-            for nt in range(N_TILES):
                 b_pass(g, nt, False, True)
 
         evac(0, 0)
-        evac(0, 1)
         prepare_w1(1, 0)
-        evac(0, 2)
+        evac(0, 1)
         prepare_w1(1, 1)
+        evac(0, 2)
         evac(0, 3)
+        prepare_wb(0)
         for t in range(PACK):
             pick(0, t)
         products(0)
-        prepare_wb(0)
-        evac(1, 0)
-        evac(1, 1)
         prepare_w1(2, 0)
+        evac(1, 0)
         prepare_w1(2, 1)
+        evac(1, 1)
         evac(1, 2)
-        evac(1, 3)
         prepare_d(0)
+        evac(1, 3)
+        prepare_wb(1)
         for t in range(PACK):
             pick(1, t)
         products(1)
         evac(2, 0)
         evac(2, 1)
-        prepare_d(1)
         evac(2, 2)
+        prepare_d(1)
         evac(2, 3)
-        prepare_wb(1)
         prepare_wb(2)
         y_acc = [psum.tile([P, M1], F32, name=f"y_acc{nt}", tag="acc", bufs=4) for nt in range(N_TILES)]
         second_stage(0)
@@ -330,7 +359,7 @@ def tile_list_subtitle_couple_score_kernel(
         last_group(2)
 
         for nt in range(N_TILES):
-            y = ring.tile([P, M1], F32, name="y", bufs=4)
+            y = ring.tile([P, M1], F32, name="y", tag="raw_half", bufs=4)
             if nt == 0:
                 nc.vector.tensor_copy(y[:], y_acc[nt][:])
             else:

@@ -65,7 +65,7 @@ def tile_list_subtitle_couple_score_kernel(
             return codes, scales
 
         def new_grouped():
-            return ring.tile([P, PACK * PASS], BF16, name="w_grouped", bufs=4, align_bytes=64)
+            return ring.tile([P, PACK * PASS], BF16, name="w_grouped", bufs=2, align_bytes=64)
 
         def round_w1(raw):
             grouped = new_grouped()
@@ -76,8 +76,11 @@ def tile_list_subtitle_couple_score_kernel(
             )
             return grouped
 
+        def new_wb_grouped():
+            return ring.tile([P, PACK * PASS], BF16, name="wb_grouped", bufs=H_PASSES, align_bytes=64)
+
         def round_wb(raw):
-            grouped = new_grouped()
+            grouped = new_wb_grouped()
             dst = grouped[:].rearrange("p (n j) -> p n j", j=PACK)
             src = raw[:].rearrange("p j n -> p n j")
             width = N // SIDE_PIECES
@@ -87,7 +90,7 @@ def tile_list_subtitle_couple_score_kernel(
             return grouped
 
         def round_wb_scalar(raw):
-            grouped = new_grouped()
+            grouped = new_wb_grouped()
             nc.scalar.activation(
                 grouped[:].rearrange("p (c i j) -> p c j i", i=PACK, j=PACK),
                 raw[:].rearrange("p j (c i) -> p c j i", i=PACK),
@@ -107,7 +110,7 @@ def tile_list_subtitle_couple_score_kernel(
             (nc.vector if i < H_SLOTS // 2 else nc.gpsimd).memset(h[:, S:], 0.0)
 
         def load_table(a):
-            words = keep.tile([P, T], I32, name=f"tab_sb{a}", align_bytes=64)
+            words = ring.tile([P, T], I32, name=f"tab_sb{a}", tag=f"x{a + 1}", align_bytes=64)
             nc.sync.dma_start(out=words[:], in_=tab_words[a].rearrange("p t i -> p (t i)").bitcast(I32))
             return words
 
@@ -213,24 +216,43 @@ def tile_list_subtitle_couple_score_kernel(
         def interleaved_out(x):
             return x[:].rearrange("p (c i t) -> p c t i", i=PACK, t=PACK)
 
-        def distances(x1, x2, dist):
-            dist_words = dist.bitcast(F32)
-            for pair in range(M_TILES // 2):
-                back = psum.tile([P, 2, 2, P], F32, name="back", bufs=2)
-                for jj in range(2):
-                    cols = slice((2 * pair + jj) * P, (2 * pair + jj + 1) * P)
-                    diff = psum.tile([P, PACK, P], F32, name="diff", bufs=2)
-                    for t in range(PACK):
+        def side_banks(name):
+            return [psum.tile([P, 2, 2, P], F32, name=name, tag="side", bufs=4) for pair in range(M_TILES // 2)]
+
+        def subtract(x1, x2, u):
+            diffs = side_banks("diff")
+            for e in range(2):
+                for pair, diff in enumerate(diffs):
+                    for jj in range(2):
+                        cols = slice((2 * pair + jj) * P, (2 * pair + jj + 1) * P)
                         for x, first in ((x1, True), (x2, False)):
                             nc.tensor.matmul(
-                                diff[:, t, :], lhsT=x[:, t, cols], rhs=identity[:],
+                                diff[:, jj, e, :], lhsT=x[:, 2 * u + e, cols], rhs=identity[:],
                                 is_transpose=True, start=first, stop=not first,
                             )
-                    turned = ring.tile([P, 2, P, 2], BF16, name="turned", bufs=4)
-                    nc.scalar.activation(turned[:], diff[:].rearrange("m (u e) p -> m u p e", e=2), ACT.Abs)
-                    turned_words = turned[:].rearrange("m u p e -> m (u p e)").bitcast(F32)
-                    for u in range(2):
-                        nc.tensor.transpose(back[:, jj, u, :], turned_words[:, u * P : (u + 1) * P], identity[:])
+            return diffs
+
+        def magnitudes(diffs):
+            words = []
+            for diff in diffs:
+                turned = ring.tile([P, 2, P, 2], BF16, name="turned", bufs=4)
+                nc.scalar.activation(turned[:], diff[:].rearrange("m jj e p -> m jj p e"), ACT.Abs)
+                words.append(turned[:].rearrange("m jj p e -> m (jj p e)").bitcast(F32))
+            return words
+
+        def turn_back(back, words, u):
+            for jj in range(2):
+                nc.tensor.transpose(back[:, jj, u, :], words[:, jj * P : (jj + 1) * P], identity[:])
+
+        def distances(x1, x2, low, dist):
+            high = subtract(x1, x2, 1)
+            backs = side_banks("back")
+            for back, words in zip(backs, low):
+                turn_back(back, words, 0)
+            dist_words = dist.bitcast(F32)
+            for back, words in zip(backs, magnitudes(high)):
+                turn_back(back, words, 1)
+            for pair, back in enumerate(backs):
                 nc.scalar.copy(
                     dist_words[:, pair * BANK : (pair + 1) * BANK].rearrange("p (jj m u) -> p jj m u", jj=2, u=2),
                     back[:].rearrange("p jj u m -> p jj m u"),
@@ -243,12 +265,12 @@ def tile_list_subtitle_couple_score_kernel(
 
         def pick(g, t):
             if t == 0:
-                xs[g] = (ring.tile([P, PACK, M1], F32, name="x1"), ring.tile([P, PACK, M1], F32, name="x2"))
+                xs[g] = tuple(ring.tile([P, PACK, M1], F32, name=f"x{i}", align_bytes=64) for i in (1, 2))
             x1, x2 = xs[g]
             nc.vector.tensor_copy(x1[:, t, :], hs[g, t][:].indirect(pos1_sb[:]))
             nc.vector.tensor_scalar(x2[:, t, :], hs[g, t][:].indirect(pos2_sb[:]), -1.0, 0.0, ALU.mult, ALU.add)
 
-        pairs = {}
+        pairs, wb_grouped = {}, {}
 
         def products(g):
             x1, x2 = xs[g]
@@ -262,21 +284,30 @@ def tile_list_subtitle_couple_score_kernel(
                 )
 
         def prepare_wb(g):
-            wb_mx[g] = quantize((round_wb if g == 0 else round_wb_scalar)(wb_raw[g]), f"wb_{g}")
+            wb_grouped[g] = (round_wb if g == 0 else round_wb_scalar)(wb_raw[g])
+
+        def quantize_wb(g, half, codes, scales):
+            nc.vector.quantize_mx(
+                out=codes.bitcast(FP8X4), scales=scales,
+                in_=wb_grouped[g][:, half * PACK * N // 2 : (half + 1) * PACK * N // 2],
+            )
+            for i in range(N_TILES // 2):
+                wb_mx[g, half * N_TILES // 2 + i] = codes[:, i * P : (i + 1) * P], scales[:, i * P : (i + 1) * P]
 
         def prepare_d(g):
-            distances(*xs[g], pairs[g][:, : PACK * M1])
-            codes = keep.tile([P, 2 * M1], U32, name=f"pair_codes{g}", align_bytes=64)
+            distances(*xs[g], magnitudes(subtract(*xs[g], 0)), pairs[g][:, : PACK * M1])
+
+        def quantize_pair(g, codes):
             scales = keep.tile([P, 2 * M1], U8, name=f"pair_scales{g}", align_bytes=64)
-            nc.vector.quantize_mx(out=codes[:].bitcast(FP8X4), scales=scales[:], in_=pairs[g][:])
+            nc.vector.quantize_mx(out=codes.bitcast(FP8X4), scales=scales[:], in_=pairs[g][:])
             d_mx[g] = codes[:, :M1], scales[:, :M1]
             b_mx[g] = codes[:, M1:], scales[:, M1:]
 
         def b_pass(g, nt, start, stop):
             nc.tensor.matmul_mx(
                 out=y_acc[nt][:],
-                lhsT=wb_mx[g][0][:, nt * P : (nt + 1) * P].bitcast(FP8X4),
-                lhsT_scale=wb_mx[g][1][:, nt * P : (nt + 1) * P],
+                lhsT=wb_mx[g, nt][0].bitcast(FP8X4),
+                lhsT_scale=wb_mx[g, nt][1],
                 rhs=b_mx[g][0][:].bitcast(FP8X4),
                 rhs_scale=b_mx[g][1][:],
                 start=start,
@@ -294,35 +325,45 @@ def tile_list_subtitle_couple_score_kernel(
                 stop=stop,
             )
 
-        def second_stage(g):
-            for nt in range(N_TILES):
-                b_pass(g, nt, g == 0, False)
-            for nt in range(N_TILES):
-                d_pass(g, nt, False, False)
-
         def last_group(g):
+            pick(g, 0)
+            pick(g, 1)
             x1, x2 = xs[g]
-            diff = ring.tile([P, PACK * M1], BF16, name="last_diff", bufs=1, align_bytes=64)
-            pair = ring.tile([P, 2 * PACK * M1], BF16, name="pair", bufs=2, align_bytes=64)
-            dist, prod = pair[:, : PACK * M1], pair[:, PACK * M1 :]
-            quads = M1 // PACK
-
-            def combine(dst, c0, c1, op):
+            low = magnitudes(subtract(x1, x2, 0))
+            pick(g, 2)
+            pick(g, 3)
+            dist = ring.tile([P, PACK * M1], BF16, name="last_dist", bufs=1, align_bytes=64)
+            prod = ring.tile([P, PACK * M1], BF16, name="last_prod", bufs=1, align_bytes=64)
+            distances(x1, x2, low, dist[:])
+            quads = M1 // PACK // 2
+            for half in range(2):
+                c = slice(half * quads, (half + 1) * quads)
                 nc.vector.tensor_tensor(
-                    interleaved_out(dst)[:, c0:c1], interleaved_in(x1)[:, c0:c1], interleaved_in(x2)[:, c0:c1], op
+                    interleaved_out(prod)[:, c], interleaved_in(x1)[:, c], interleaved_in(x2)[:, c], ALU.mult
                 )
-
-            for c0, c1 in ((0, quads // 2), (quads // 2, quads)):
-                combine(diff, c0, c1, ALU.add)
-                flat = slice(c0 * PACK * PACK, c1 * PACK * PACK)
-                nc.scalar.activation(dist[:, flat], diff[:, flat], ACT.Abs)
-            combine(prod, 0, 3 * quads // 4, ALU.mult)
-            d_mx[g] = quantize(dist, f"d_{g}")
-            combine(prod, 3 * quads // 4, quads, ALU.mult)
             b_mx[g] = quantize(prod, f"b_{g}", pieces=2)
-            for nt in range(N_TILES):
+            held = ring.tile([P, 2 * M1 + H_PASSES * N // 2], U32, name="held", tag="last_prod", bufs=1, align_bytes=64)
+            wb_scales = keep.tile([P, 2, H_PASSES, N // 2], U8, name="wb_scales", align_bytes=64)
+            for gg in (g, 0, 1):
+                c0 = 2 * M1 + gg * N // 2
+                quantize_wb(gg, 0, held[:, c0 : c0 + N // 2], wb_scales[:, 0, gg, :])
+            quantize_pair(g - 1, held[:, : 2 * M1])
+            d_mx[g] = quantize(dist, f"d_{g}")
+            for gg in (g, 0):
+                for nt in range(N_TILES // 2):
+                    b_pass(gg, nt, False, False)
+            for nt in range(N_TILES // 2):
+                b_pass(1, nt, False, False)
+                d_pass(1, nt, False, False)
+                d_pass(g, nt, False, True)
+            codes = ring.tile([P, H_PASSES, N // 2], U32, name="late_codes", tag="last_dist", bufs=1, align_bytes=64)
+            for gg in range(H_PASSES):
+                quantize_wb(gg, 1, codes[:, gg, :], wb_scales[:, 1, gg, :])
+            for nt in range(N_TILES // 2, N_TILES):
+                d_pass(1, nt, False, False)
                 d_pass(g, nt, False, False)
-                b_pass(g, nt, False, True)
+                for gg in range(H_PASSES):
+                    b_pass(gg, nt, False, gg == H_PASSES - 1)
 
         evac(0, 0)
         prepare_w1(1, 0)
@@ -340,6 +381,8 @@ def tile_list_subtitle_couple_score_kernel(
         evac(1, 1)
         evac(1, 2)
         prepare_d(0)
+        first_codes = keep.tile([P, 2 * M1], U32, name="first_codes", align_bytes=64)
+        quantize_pair(0, first_codes[:])
         evac(1, 3)
         prepare_wb(1)
         for t in range(PACK):
@@ -352,26 +395,31 @@ def tile_list_subtitle_couple_score_kernel(
         evac(2, 3)
         prepare_wb(2)
         y_acc = [psum.tile([P, M1], F32, name=f"y_acc{nt}", tag="acc", bufs=4) for nt in range(N_TILES)]
-        second_stage(0)
-        second_stage(1)
-        for t in range(PACK):
-            pick(2, t)
+        for nt in range(N_TILES):
+            d_pass(0, nt, True, False)
         last_group(2)
 
-        for nt in range(N_TILES):
-            y = ring.tile([P, M1], F32, name="y", tag="raw_half", bufs=4)
-            if nt == 0:
-                nc.vector.tensor_copy(y[:], y_acc[nt][:])
-            else:
-                nc.scalar.copy(y[:], y_acc[nt][:])
-            first = ring.tile([P, M2], F32, name="first")
-            other = ring.tile([P, M2], F32, name="other")
-            nc.vector.tensor_copy(first[:], y[:].indirect(pos3_sb[:]))
-            nc.vector.tensor_copy(other[:], y[:].indirect(pos4_sb[:]))
-            top = ring.tile([P, M2], F32, name="top")
+        def finish(nt, first, other):
+            top = ring.tile([P, M2], F32, name="top", bufs=N_TILES)
             nc.vector.tensor_tensor(top[:], first[:], other[:], ALU.max)
-            squared = ring.tile([P, M2], F32, name="squared")
+            squared = ring.tile([P, M2], F32, name="squared", tag="last_dist", bufs=1, align_bytes=64)
             nc.scalar.activation(squared[:], top[:], ACT.Square)
             score = ring.tile([P, M2], F32, name="score", bufs=4)
             nc.scalar.activation(score[:], squared[:], ACT.Copy, bias=1.0)
             nc.sync.dma_start(out=out[nt * P : (nt + 1) * P, :], in_=score[:])
+
+        ys = []
+        for nt in range(N_TILES):
+            y = ring.tile([P, M1], F32, name="y", tag="raw_half", bufs=4)
+            nc.scalar.copy(y[:], y_acc[nt][:])
+            ys.append(y)
+        waiting = None
+        for nt, y in enumerate(ys):
+            first = ring.tile([P, M2], F32, name="first", bufs=N_TILES)
+            other = ring.tile([P, M2], F32, name="other", bufs=N_TILES)
+            nc.vector.tensor_copy(first[:], y[:].indirect(pos3_sb[:]))
+            if waiting:
+                finish(*waiting)
+            nc.vector.tensor_copy(other[:], y[:].indirect(pos4_sb[:]))
+            waiting = (nt, first, other)
+        finish(*waiting)

@@ -26,7 +26,7 @@ H_PASSES = H // PASS
 N_TILES = N // P
 M_TILES = M1 // P
 H_SLOTS = 4
-RAW_BUFS = 4
+RAW_BUFS = 5
 SIDE_PIECES = 4
 
 
@@ -76,28 +76,14 @@ def tile_list_subtitle_couple_score_kernel(
             )
             return grouped
 
-        def new_wb_grouped():
-            return ring.tile([P, PACK * PASS], BF16, name="wb_grouped", bufs=H_PASSES, align_bytes=64)
+        wb_grouped = keep.tile([P, N_TILES, H_PASSES, P, PACK], BF16, name="wb_grouped", align_bytes=64)
 
-        def round_wb(raw):
-            grouped = new_wb_grouped()
-            dst = grouped[:].rearrange("p (n j) -> p n j", j=PACK)
-            src = raw[:].rearrange("p j n -> p n j")
-            width = N // SIDE_PIECES
-            for piece in range(SIDE_PIECES):
-                cols = slice(piece * width, (piece + 1) * width)
-                nc.gpsimd.tensor_scalar(dst[:, cols], src[:, cols], -1.0, 0.0, ALU.mult, ALU.add)
-            return grouped
-
-        def round_wb_scalar(raw):
-            grouped = new_wb_grouped()
-            nc.scalar.activation(
-                grouped[:].rearrange("p (c i j) -> p c j i", i=PACK, j=PACK),
-                raw[:].rearrange("p j (c i) -> p c j i", i=PACK),
-                ACT.Copy,
-                scale=-1.0,
-            )
-            return grouped
+        def round_wb(g):
+            src = wb_raw[g][:].rearrange("p j n -> p n j")
+            for nt in range(N_TILES):
+                nc.gpsimd.tensor_scalar(
+                    wb_grouped[:, nt, g], src[:, nt * P : (nt + 1) * P], -1.0, 0.0, ALU.mult, ALU.add
+                )
 
         tab_planes = keep.tile([P, T], U8, name="tab_planes", align_bytes=64)
         nc.gpsimd.memset(tab_planes[:].bitcast(I32), 0)
@@ -114,34 +100,36 @@ def tile_list_subtitle_couple_score_kernel(
             nc.sync.dma_start(out=words[:], in_=tab_words[a].rearrange("p t i -> p (t i)").bitcast(I32))
             return words
 
-        offs_sb = load_list(offs, "offs_sb")
         tab_sb = [load_table(0)]
+        offs_sb = load_list(offs, "offs_sb")
         for q in range(4):
             nc.sync.dma_start(
                 out=tab_planes[32 * q : 32 * q + 4 * K_PASSES, :].bitcast(I32),
                 in_=tab_scales[:, 4 * q : 4 * q + 4, :].bitcast(I32),
             )
-        tab_sb.append(load_table(1))
         w1_raw = {}
-        w1_halves = [
-            [load_rows(w1, a, half * PASS // 2, PASS // 2, "raw_half", 4) for half in range(2)] for a in range(K_PASSES)
-        ]
+
+        def load_halves(a):
+            return [load_rows(w1, a, half * PASS // 2, PASS // 2, "raw_half", 4) for half in range(2)]
+
+        w1_halves = [load_halves(0)]
+        tab_sb.append(load_table(1))
+        w1_halves.append(load_halves(1))
         pos1_sb = load_list(pos1, "pos1_sb")
         pos2_sb = load_list(pos2, "pos2_sb")
         wb_raw = {}
         for a in range(K_PASSES):
             w1_raw[1, a] = load_rows(w1, a, PASS, PASS, "raw", RAW_BUFS)
-        w1_raw[2, 0] = load_rows(w1, 0, 2 * PASS, PASS, "raw", RAW_BUFS)
         wb_raw[0] = load_rows(wb, 0, 0, N, "raw", RAW_BUFS)
+        w1_raw[2, 0] = load_rows(w1, 0, 2 * PASS, PASS, "raw", RAW_BUFS)
         w1_raw[2, 1] = load_rows(w1, 1, 2 * PASS, PASS, "raw", RAW_BUFS)
-        for g in range(1, H_PASSES):
-            wb_raw[g] = load_rows(wb, g, 0, N, "raw", RAW_BUFS)
+        wb_raw[1] = load_rows(wb, 1, 0, N, "raw", RAW_BUFS)
+        wb_raw[2] = load_rows(wb, 2, 0, N, "raw", RAW_BUFS)
 
         v_codes = [keep.tile([P, S], U32, name=f"v_codes{a}", align_bytes=64) for a in range(K_PASSES)]
         v_planes = keep.tile([P, S], U8, name="v_planes", align_bytes=64)
         nc.vector.tensor_copy(v_codes[0][:], tab_sb[0][:].bitcast(U32).indirect(offs_sb[:]))
         nc.vector.tensor_copy(v_planes[:], tab_planes[:].indirect(offs_sb[:]))
-        nc.vector.tensor_copy(v_codes[1][:], tab_sb[1][:].bitcast(U32).indirect(offs_sb[:]))
 
         w1_mx = {}
 
@@ -155,7 +143,7 @@ def tile_list_subtitle_couple_score_kernel(
             for half in range(S // BANK):
                 cols = slice(half * BANK, (half + 1) * BANK)
                 acc = psum.tile([P, BANK], F32, name="acc", bufs=4)
-                order = list(range(K_PASSES)) if (g, t) == (0, 0) else list(reversed(range(K_PASSES)))
+                order = list(range(K_PASSES)) if g == 0 and t < 2 else list(reversed(range(K_PASSES)))
                 for a in order:
                     codes, scales = w1_mx[g, a, t]
                     nc.tensor.matmul_mx(
@@ -167,14 +155,14 @@ def tile_list_subtitle_couple_score_kernel(
                         start=(a == order[0]),
                         stop=(a == order[-1]),
                     )
-                if (g, t) == (0, 0):
+                if (g, t, half) == (0, 0, 1):
                     nc.vector.tensor_copy(h[:, cols], acc[:])
                 else:
                     nc.scalar.copy(h[:, cols], acc[:])
             return h
 
         head = ring.tile([P, 2 * PACK * PASS], BF16, name="pair", bufs=2, align_bytes=64)
-        head_dst = head[:].rearrange("p (t a m j) -> p a m j t", t=PACK, a=K_PASSES, j=PACK)
+        head_dst = head[:].rearrange("p (a t m j) -> p a m j t", t=PACK, a=K_PASSES, j=PACK)
         head_codes = keep.tile([P, K_PASSES * PASS], U32, name="head_codes", align_bytes=64)
         head_scales = keep.tile([P, K_PASSES * PASS], U8, name="head_scales", align_bytes=64)
 
@@ -183,21 +171,28 @@ def tile_list_subtitle_couple_score_kernel(
                 out=head_codes[:, c0:c1].bitcast(FP8X4), scales=head_scales[:, c0:c1], in_=head[:, PACK * c0 : PACK * c1]
             )
 
-        for a in range(K_PASSES):
-            for half in range(2):
-                dst = head_dst[:, a, half * P // 2 : (half + 1) * P // 2]
-                src = w1_halves[a][half][:].rearrange("p j (m t) -> p m j t", t=PACK)
-                if (a, half) == (K_PASSES - 1, 1):
-                    nc.scalar.activation(dst[:, : P // 4], src[:, : P // 4], ACT.Copy)
-                    nc.vector.tensor_copy(dst[:, P // 4 :], src[:, P // 4 :])
-                else:
-                    nc.scalar.activation(dst, src, ACT.Copy)
-            quantize_head(a * P, (a + 1) * P)
-        for t in range(1, PACK):
-            quantize_head(t * K_PASSES * P, (t + 1) * K_PASSES * P)
+        def round_head(a, half, tiles):
+            dst = head_dst[:, a, half * P // 2 : (half + 1) * P // 2]
+            src = w1_halves[a][half][:].rearrange("p j (m t) -> p m j t", t=PACK)
+            nc.scalar.activation(dst[:, :, :, tiles], src[:, :, :, tiles], ACT.Copy)
+
+        for half in range(2):
+            round_head(0, half, slice(0, PACK))
+        quantize_head(0, PASS)
+        for half in range(2):
+            entries = slice(half * BANK // 16, (half + 1) * BANK // 16)
+            nc.vector.tensor_copy(
+                v_codes[1][:, half * BANK : (half + 1) * BANK], tab_sb[1][:].bitcast(U32).indirect(offs_sb[:, entries])
+            )
+        round_head(1, 0, slice(0, PACK))
+        round_head(1, 1, slice(0, PACK // 2))
+        quantize_head(PASS, PASS + P)
+        round_head(1, 1, slice(PACK // 2, PACK))
+        quantize_head(PASS + P, PASS + 2 * P)
+        quantize_head(PASS + 2 * P, 2 * PASS)
         for t in range(PACK):
             for a in range(K_PASSES):
-                cols = slice((t * K_PASSES + a) * P, (t * K_PASSES + a + 1) * P)
+                cols = slice(a * PASS + t * P, a * PASS + (t + 1) * P)
                 w1_mx[0, a, t] = head_codes[:, cols], head_scales[:, cols]
 
         wd_sb = keep.tile([P, H_PASSES, 2 * N], U8, name="wd_sb", align_bytes=64)
@@ -232,10 +227,13 @@ def tile_list_subtitle_couple_score_kernel(
                             )
             return diffs
 
-        def magnitudes(diffs):
+        def magnitudes(diffs, last_tag=None):
             words = []
             for diff in diffs:
-                turned = ring.tile([P, 2, P, 2], BF16, name="turned", bufs=4)
+                if last_tag and len(words) == len(diffs) - 1:
+                    turned = ring.tile([P, 2, P, 2], BF16, name="turned", tag=last_tag, bufs=1, align_bytes=64)
+                else:
+                    turned = ring.tile([P, 2, P, 2], BF16, name="turned", bufs=4)
                 nc.scalar.activation(turned[:], diff[:].rearrange("m jj e p -> m jj p e"), ACT.Abs)
                 words.append(turned[:].rearrange("m jj p e -> m (jj p e)").bitcast(F32))
             return words
@@ -244,14 +242,16 @@ def tile_list_subtitle_couple_score_kernel(
             for jj in range(2):
                 nc.tensor.transpose(back[:, jj, u, :], words[:, jj * P : (jj + 1) * P], identity[:])
 
-        def distances(x1, x2, low, dist):
+        def distances(x1, x2, low, dist, between=None, last_tag=None):
             high = subtract(x1, x2, 1)
             backs = side_banks("back")
             for back, words in zip(backs, low):
                 turn_back(back, words, 0)
             dist_words = dist.bitcast(F32)
-            for back, words in zip(backs, magnitudes(high)):
+            for back, words in zip(backs, magnitudes(high, last_tag)):
                 turn_back(back, words, 1)
+            if between:
+                evac(*between)
             for pair, back in enumerate(backs):
                 nc.scalar.copy(
                     dist_words[:, pair * BANK : (pair + 1) * BANK].rearrange("p (jj m u) -> p jj m u", jj=2, u=2),
@@ -270,7 +270,7 @@ def tile_list_subtitle_couple_score_kernel(
             nc.vector.tensor_copy(x1[:, t, :], hs[g, t][:].indirect(pos1_sb[:]))
             nc.vector.tensor_scalar(x2[:, t, :], hs[g, t][:].indirect(pos2_sb[:]), -1.0, 0.0, ALU.mult, ALU.add)
 
-        pairs, wb_grouped = {}, {}
+        pairs = {}
 
         def products(g):
             x1, x2 = xs[g]
@@ -283,19 +283,28 @@ def tile_list_subtitle_couple_score_kernel(
                     interleaved_out(prod)[:, c], interleaved_in(x1)[:, c], interleaved_in(x2)[:, c], ALU.mult
                 )
 
-        def prepare_wb(g):
-            wb_grouped[g] = (round_wb if g == 0 else round_wb_scalar)(wb_raw[g])
+        wb_scales = keep.tile([P, N_TILES * H_PASSES * P], U8, name="wb_scales", align_bytes=64)
 
-        def quantize_wb(g, half, codes, scales):
-            nc.vector.quantize_mx(
-                out=codes.bitcast(FP8X4), scales=scales,
-                in_=wb_grouped[g][:, half * PACK * N // 2 : (half + 1) * PACK * N // 2],
-            )
-            for i in range(N_TILES // 2):
-                wb_mx[g, half * N_TILES // 2 + i] = codes[:, i * P : (i + 1) * P], scales[:, i * P : (i + 1) * P]
+        def quantize_wb(tiles, codes, widths):
+            flat = wb_grouped[:].rearrange("p a g n j -> p (a g n j)")
+            base = tiles[0] * H_PASSES * P
+            c0 = 0
+            for width in widths:
+                nc.vector.quantize_mx(
+                    out=codes[:, c0 : c0 + width].bitcast(FP8X4),
+                    scales=wb_scales[:, base + c0 : base + c0 + width],
+                    in_=flat[:, PACK * (base + c0) : PACK * (base + c0 + width)],
+                )
+                c0 += width
+            for i, nt in enumerate(tiles):
+                for g in range(H_PASSES):
+                    c = (i * H_PASSES + g) * P
+                    wb_mx[g, nt] = codes[:, c : c + P], wb_scales[:, base + c : base + c + P]
 
         def prepare_d(g):
-            distances(*xs[g], magnitudes(subtract(*xs[g], 0)), pairs[g][:, : PACK * M1])
+            low = magnitudes(subtract(*xs[g], 0))
+            evac(g + 1, PACK - 1)
+            distances(*xs[g], low, pairs[g][:, : PACK * M1], (2, 0) if g == 0 else None)
 
         def quantize_pair(g, codes):
             scales = keep.tile([P, 2 * M1], U8, name=f"pair_scales{g}", align_bytes=64)
@@ -326,7 +335,6 @@ def tile_list_subtitle_couple_score_kernel(
             )
 
         def last_group(g):
-            pick(g, 0)
             pick(g, 1)
             x1, x2 = xs[g]
             low = magnitudes(subtract(x1, x2, 0))
@@ -334,7 +342,7 @@ def tile_list_subtitle_couple_score_kernel(
             pick(g, 3)
             dist = ring.tile([P, PACK * M1], BF16, name="last_dist", bufs=1, align_bytes=64)
             prod = ring.tile([P, PACK * M1], BF16, name="last_prod", bufs=1, align_bytes=64)
-            distances(x1, x2, low, dist[:])
+            distances(x1, x2, low, dist[:], None, "held")
             quads = M1 // PACK // 2
             for half in range(2):
                 c = slice(half * quads, (half + 1) * quads)
@@ -342,84 +350,91 @@ def tile_list_subtitle_couple_score_kernel(
                     interleaved_out(prod)[:, c], interleaved_in(x1)[:, c], interleaved_in(x2)[:, c], ALU.mult
                 )
             b_mx[g] = quantize(prod, f"b_{g}", pieces=2)
-            held = ring.tile([P, 2 * M1 + H_PASSES * N // 2], U32, name="held", tag="last_prod", bufs=1, align_bytes=64)
-            wb_scales = keep.tile([P, 2, H_PASSES, N // 2], U8, name="wb_scales", align_bytes=64)
-            for gg in (g, 0, 1):
-                c0 = 2 * M1 + gg * N // 2
-                quantize_wb(gg, 0, held[:, c0 : c0 + N // 2], wb_scales[:, 0, gg, :])
+            run = H_PASSES * P
+            held = ring.tile([P, 2 * M1 + run], U32, name="held", bufs=1, align_bytes=64)
+            quantize_wb([0], held[:, 2 * M1 :], (2 * P, P))
             quantize_pair(g - 1, held[:, : 2 * M1])
             d_mx[g] = quantize(dist, f"d_{g}")
-            for gg in (g, 0):
-                for nt in range(N_TILES // 2):
-                    b_pass(gg, nt, False, False)
-            for nt in range(N_TILES // 2):
-                b_pass(1, nt, False, False)
-                d_pass(1, nt, False, False)
-                d_pass(g, nt, False, True)
-            codes = ring.tile([P, H_PASSES, N // 2], U32, name="late_codes", tag="last_dist", bufs=1, align_bytes=64)
-            for gg in range(H_PASSES):
-                quantize_wb(gg, 1, codes[:, gg, :], wb_scales[:, 1, gg, :])
-            for nt in range(N_TILES // 2, N_TILES):
+            for gg in (g, 0, 1):
+                b_pass(gg, 0, False, False)
+            d_pass(1, 0, False, False)
+            d_pass(g, 0, False, True)
+            late = ring.tile([P, (N_TILES - 1) * run], U32, name="late", tag="last_dist", bufs=1, align_bytes=64)
+            quantize_wb([1], late[:, :run], (2 * P, P))
+            quantize_wb([2, 3], late[:, run:], (4 * P, 2 * P))
+            for nt in range(1, N_TILES):
                 d_pass(1, nt, False, False)
                 d_pass(g, nt, False, False)
                 for gg in range(H_PASSES):
                     b_pass(gg, nt, False, gg == H_PASSES - 1)
 
         evac(0, 0)
-        prepare_w1(1, 0)
         evac(0, 1)
-        prepare_w1(1, 1)
+        prepare_w1(1, 0)
         evac(0, 2)
+        prepare_w1(1, 1)
         evac(0, 3)
-        prepare_wb(0)
         for t in range(PACK):
             pick(0, t)
         products(0)
-        prepare_w1(2, 0)
+        round_wb(0)
+        round_wb(1)
+        round_wb(2)
         evac(1, 0)
-        prepare_w1(2, 1)
+        prepare_w1(2, 0)
         evac(1, 1)
+        prepare_w1(2, 1)
         evac(1, 2)
+        pick(1, 0)
         prepare_d(0)
-        first_codes = keep.tile([P, 2 * M1], U32, name="first_codes", align_bytes=64)
-        quantize_pair(0, first_codes[:])
-        evac(1, 3)
-        prepare_wb(1)
-        for t in range(PACK):
+        for t in range(1, PACK):
             pick(1, t)
         products(1)
-        evac(2, 0)
         evac(2, 1)
         evac(2, 2)
         prepare_d(1)
-        evac(2, 3)
-        prepare_wb(2)
+        first_codes = keep.tile([P, 2 * M1], U32, name="first_codes", align_bytes=64)
+        pick(2, 0)
+        quantize_pair(0, first_codes[:])
         y_acc = [psum.tile([P, M1], F32, name=f"y_acc{nt}", tag="acc", bufs=4) for nt in range(N_TILES)]
         for nt in range(N_TILES):
             d_pass(0, nt, True, False)
         last_group(2)
-
-        def finish(nt, first, other):
-            top = ring.tile([P, M2], F32, name="top", bufs=N_TILES)
-            nc.vector.tensor_tensor(top[:], first[:], other[:], ALU.max)
-            squared = ring.tile([P, M2], F32, name="squared", tag="last_dist", bufs=1, align_bytes=64)
-            nc.scalar.activation(squared[:], top[:], ACT.Square)
-            score = ring.tile([P, M2], F32, name="score", bufs=4)
-            nc.scalar.activation(score[:], squared[:], ACT.Copy, bias=1.0)
-            nc.sync.dma_start(out=out[nt * P : (nt + 1) * P, :], in_=score[:])
 
         ys = []
         for nt in range(N_TILES):
             y = ring.tile([P, M1], F32, name="y", tag="raw_half", bufs=4)
             nc.scalar.copy(y[:], y_acc[nt][:])
             ys.append(y)
-        waiting = None
-        for nt, y in enumerate(ys):
-            first = ring.tile([P, M2], F32, name="first", bufs=N_TILES)
-            other = ring.tile([P, M2], F32, name="other", bufs=N_TILES)
-            nc.vector.tensor_copy(first[:], y[:].indirect(pos3_sb[:]))
-            if waiting:
-                finish(*waiting)
-            nc.vector.tensor_copy(other[:], y[:].indirect(pos4_sb[:]))
-            waiting = (nt, first, other)
-        finish(*waiting)
+        first = ring.tile([P, N_TILES, M2], F32, name="first", tag="x1", align_bytes=64)
+        other = ring.tile([P, N_TILES, M2], F32, name="other", tag="x2", align_bytes=64)
+        top = ring.tile([P, N_TILES, M2], F32, name="top", tag="w_grouped", align_bytes=64)
+        squared = ring.tile([P, N_TILES, M2], F32, name="squared", tag="last_dist", bufs=1, align_bytes=64)
+        score = ring.tile([P, N_TILES, M2], F32, name="score", tag="w_grouped", align_bytes=64)
+
+        def pick_y(nt):
+            nc.vector.tensor_copy(first[:, nt, :], ys[nt][:].indirect(pos3_sb[:]))
+            nc.vector.tensor_copy(other[:, nt, :], ys[nt][:].indirect(pos4_sb[:]))
+
+        def store(tiles):
+            nc.sync.dma_start(
+                out=out[tiles.start * P : tiles.stop * P, :].rearrange("(a p) j -> p a j", p=P), in_=score[:, tiles, :]
+            )
+
+        last = N_TILES - 1
+        for tiles in (slice(0, last - 1), slice(last - 1, last)):
+            for nt in range(tiles.start, tiles.stop):
+                pick_y(nt)
+            nc.vector.tensor_tensor(top[:, tiles, :], first[:, tiles, :], other[:, tiles, :], ALU.max)
+            nc.scalar.activation(squared[:, tiles, :], top[:, tiles, :], ACT.Square)
+            nc.scalar.activation(score[:, tiles, :], squared[:, tiles, :], ACT.Copy, bias=1.0)
+            store(tiles)
+        pick_y(last)
+        halves = [slice(0, M2 // 2), slice(M2 // 2, M2)]
+        for c in halves:
+            nc.vector.tensor_tensor(top[:, last, c], first[:, last, c], other[:, last, c], ALU.max)
+        for c in halves:
+            nc.vector.tensor_tensor(squared[:, last, c], top[:, last, c], top[:, last, c], ALU.mult)
+        for c in halves:
+            nc.vector.tensor_scalar(score[:, last, c], squared[:, last, c], 1.0, None, ALU.add)
+        store(slice(last, N_TILES))

@@ -64,11 +64,8 @@ def tile_list_subtitle_couple_score_kernel(
                 )
             return codes, scales
 
-        def new_grouped():
-            return ring.tile([P, PACK * PASS], BF16, name="w_grouped", bufs=2, align_bytes=64)
-
-        def round_w1(raw):
-            grouped = new_grouped()
+        def round_w1(raw, tag):
+            grouped = ring.tile([P, PACK * PASS], BF16, name="w_grouped", tag=tag, bufs=1, align_bytes=64)
             nc.scalar.activation(
                 grouped[:].rearrange("p (t m j) -> p m j t", t=PACK, j=PACK),
                 raw[:].rearrange("p j (m t) -> p m j t", t=PACK),
@@ -76,14 +73,26 @@ def tile_list_subtitle_couple_score_kernel(
             )
             return grouped
 
-        wb_grouped = keep.tile([P, N_TILES, H_PASSES, P, PACK], BF16, name="wb_grouped", align_bytes=64)
-
-        def round_wb(g):
-            src = wb_raw[g][:].rearrange("p j n -> p n j")
+        def round_first_wb():
+            wb_first = ring.tile([P, N * PACK], BF16, name="wb_first", tag="odd", bufs=1, align_bytes=64)
+            dst = wb_first[:].rearrange("p (n j) -> p n j", j=PACK)
+            src = wb_raw[0][:].rearrange("p j n -> p n j")
             for nt in range(N_TILES):
-                nc.gpsimd.tensor_scalar(
-                    wb_grouped[:, nt, g], src[:, nt * P : (nt + 1) * P], -1.0, 0.0, ALU.mult, ALU.add
-                )
+                cols = slice(nt * P, (nt + 1) * P)
+                nc.gpsimd.tensor_scalar(dst[:, cols], src[:, cols], -1.0, 0.0, ALU.mult, ALU.add)
+            return wb_first
+
+        def round_later_wb(name, tiles):
+            grouped = ring.tile([P, len(tiles), H_PASSES - 1, PASS], BF16, name=name, bufs=1, align_bytes=64)
+            for i, nt in enumerate(tiles):
+                for g in range(1, H_PASSES):
+                    nc.scalar.activation(
+                        grouped[:, i, g - 1, :].rearrange("p (c i j) -> p c j i", i=PACK, j=PACK),
+                        wb_raw[g][:, :, nt * P : (nt + 1) * P].rearrange("p j (c i) -> p c j i", i=PACK),
+                        ACT.Copy,
+                        scale=-1.0,
+                    )
+            return grouped[:].rearrange("p a g c -> p (a g c)")
 
         tab_planes = keep.tile([P, T], U8, name="tab_planes", align_bytes=64)
         nc.gpsimd.memset(tab_planes[:].bitcast(I32), 0)
@@ -96,7 +105,7 @@ def tile_list_subtitle_couple_score_kernel(
             (nc.vector if i < H_SLOTS // 2 else nc.gpsimd).memset(h[:, S:], 0.0)
 
         def load_table(a):
-            words = ring.tile([P, T], I32, name=f"tab_sb{a}", tag=f"x{a + 1}", align_bytes=64)
+            words = ring.tile([P, T], I32, name=f"tab_sb{a}", tag=f"x{a + 1}", bufs=3, align_bytes=64)
             nc.sync.dma_start(out=words[:], in_=tab_words[a].rearrange("p t i -> p (t i)").bitcast(I32))
             return words
 
@@ -134,7 +143,7 @@ def tile_list_subtitle_couple_score_kernel(
         w1_mx = {}
 
         def prepare_w1(g, a):
-            codes, scales = quantize(round_w1(w1_raw[g, a]), f"w1_{g}_{a}")
+            codes, scales = quantize(round_w1(w1_raw[g, a], ("even", "odd" if g == 1 else "pair")[a]), f"w1_{g}_{a}")
             for t in range(PACK):
                 w1_mx[g, a, t] = codes[:, t * P : (t + 1) * P], scales[:, t * P : (t + 1) * P]
 
@@ -161,7 +170,7 @@ def tile_list_subtitle_couple_score_kernel(
                     nc.scalar.copy(h[:, cols], acc[:])
             return h
 
-        head = ring.tile([P, 2 * PACK * PASS], BF16, name="pair", bufs=2, align_bytes=64)
+        head = ring.tile([P, 2 * PACK * PASS], BF16, name="pair", bufs=1, align_bytes=64)
         head_dst = head[:].rearrange("p (a t m j) -> p a m j t", t=PACK, a=K_PASSES, j=PACK)
         head_codes = keep.tile([P, K_PASSES * PASS], U32, name="head_codes", align_bytes=64)
         head_scales = keep.tile([P, K_PASSES * PASS], U8, name="head_scales", align_bytes=64)
@@ -230,8 +239,8 @@ def tile_list_subtitle_couple_score_kernel(
         def magnitudes(diffs, last_tag=None):
             words = []
             for diff in diffs:
-                if last_tag and len(words) == len(diffs) - 1:
-                    turned = ring.tile([P, 2, P, 2], BF16, name="turned", tag=last_tag, bufs=1, align_bytes=64)
+                if last_tag and last_tag[len(words)]:
+                    turned = ring.tile([P, 2, P, 2], BF16, name="turned", tag=last_tag[len(words)], bufs=1, align_bytes=64)
                 else:
                     turned = ring.tile([P, 2, P, 2], BF16, name="turned", bufs=4)
                 nc.scalar.activation(turned[:], diff[:].rearrange("m jj e p -> m jj p e"), ACT.Abs)
@@ -265,7 +274,7 @@ def tile_list_subtitle_couple_score_kernel(
 
         def pick(g, t):
             if t == 0:
-                xs[g] = tuple(ring.tile([P, PACK, M1], F32, name=f"x{i}", align_bytes=64) for i in (1, 2))
+                xs[g] = tuple(ring.tile([P, PACK, M1], F32, name=f"x{i}", bufs=3, align_bytes=64) for i in (1, 2))
             x1, x2 = xs[g]
             nc.vector.tensor_copy(x1[:, t, :], hs[g, t][:].indirect(pos1_sb[:]))
             nc.vector.tensor_scalar(x2[:, t, :], hs[g, t][:].indirect(pos2_sb[:]), -1.0, 0.0, ALU.mult, ALU.add)
@@ -274,7 +283,7 @@ def tile_list_subtitle_couple_score_kernel(
 
         def products(g):
             x1, x2 = xs[g]
-            pairs[g] = ring.tile([P, 2 * PACK * M1], BF16, name="pair", bufs=2, align_bytes=64)
+            pairs[g] = ring.tile([P, 2 * PACK * M1], BF16, name="pair", bufs=1, align_bytes=64)
             prod = pairs[g][:, PACK * M1 :]
             quads = M1 // PACK // SIDE_PIECES
             for piece in range(SIDE_PIECES):
@@ -283,28 +292,16 @@ def tile_list_subtitle_couple_score_kernel(
                     interleaved_out(prod)[:, c], interleaved_in(x1)[:, c], interleaved_in(x2)[:, c], ALU.mult
                 )
 
-        wb_scales = keep.tile([P, N_TILES * H_PASSES * P], U8, name="wb_scales", align_bytes=64)
-
-        def quantize_wb(tiles, codes, widths):
-            flat = wb_grouped[:].rearrange("p a g n j -> p (a g n j)")
-            base = tiles[0] * H_PASSES * P
-            c0 = 0
-            for width in widths:
-                nc.vector.quantize_mx(
-                    out=codes[:, c0 : c0 + width].bitcast(FP8X4),
-                    scales=wb_scales[:, base + c0 : base + c0 + width],
-                    in_=flat[:, PACK * (base + c0) : PACK * (base + c0 + width)],
-                )
-                c0 += width
-            for i, nt in enumerate(tiles):
-                for g in range(H_PASSES):
-                    c = (i * H_PASSES + g) * P
-                    wb_mx[g, nt] = codes[:, c : c + P], wb_scales[:, base + c : base + c + P]
+        def quantize_wb(grouped, codes, keys):
+            scales = keep.tile([P, len(keys) * P], U8, name="wb_scales%d%d" % keys[0], align_bytes=64)
+            nc.vector.quantize_mx(out=codes.bitcast(FP8X4), scales=scales[:], in_=grouped)
+            for i, key in enumerate(keys):
+                wb_mx[key] = codes[:, i * P : (i + 1) * P], scales[:, i * P : (i + 1) * P]
 
         def prepare_d(g):
             low = magnitudes(subtract(*xs[g], 0))
             evac(g + 1, PACK - 1)
-            distances(*xs[g], low, pairs[g][:, : PACK * M1], (2, 0) if g == 0 else None)
+            distances(*xs[g], low, pairs[g][:, : PACK * M1], *(((2, 0), None) if g == 0 else (None, (None, "wb_low"))))
 
         def quantize_pair(g, codes):
             scales = keep.tile([P, 2 * M1], U8, name=f"pair_scales{g}", align_bytes=64)
@@ -338,11 +335,12 @@ def tile_list_subtitle_couple_score_kernel(
             pick(g, 1)
             x1, x2 = xs[g]
             low = magnitudes(subtract(x1, x2, 0))
+            wb_low = round_later_wb("wb_low", (0, 1))
             pick(g, 2)
             pick(g, 3)
             dist = ring.tile([P, PACK * M1], BF16, name="last_dist", bufs=1, align_bytes=64)
             prod = ring.tile([P, PACK * M1], BF16, name="last_prod", bufs=1, align_bytes=64)
-            distances(x1, x2, low, dist[:], None, "held")
+            distances(x1, x2, low, dist[:], None, ("wb_high", "held"))
             quads = M1 // PACK // 2
             for half in range(2):
                 c = slice(half * quads, (half + 1) * quads)
@@ -352,7 +350,9 @@ def tile_list_subtitle_couple_score_kernel(
             b_mx[g] = quantize(prod, f"b_{g}", pieces=2)
             run = H_PASSES * P
             held = ring.tile([P, 2 * M1 + run], U32, name="held", bufs=1, align_bytes=64)
-            quantize_wb([0], held[:, 2 * M1 :], (2 * P, P))
+            wb_high = round_later_wb("wb_high", (2, 3))
+            quantize_wb(wb_low[:, : 2 * PASS], held[:, 2 * M1 : 2 * M1 + 2 * P], [(1, 0), (2, 0)])
+            quantize_wb(wb_first[:, :PASS], held[:, 2 * M1 + 2 * P :], [(0, 0)])
             quantize_pair(g - 1, held[:, : 2 * M1])
             d_mx[g] = quantize(dist, f"d_{g}")
             for gg in (g, 0, 1):
@@ -360,8 +360,10 @@ def tile_list_subtitle_couple_score_kernel(
             d_pass(1, 0, False, False)
             d_pass(g, 0, False, True)
             late = ring.tile([P, (N_TILES - 1) * run], U32, name="late", tag="last_dist", bufs=1, align_bytes=64)
-            quantize_wb([1], late[:, :run], (2 * P, P))
-            quantize_wb([2, 3], late[:, run:], (4 * P, 2 * P))
+            quantize_wb(wb_low[:, 2 * PASS :], late[:, : 2 * P], [(1, 1), (2, 1)])
+            quantize_wb(wb_first[:, PASS : 2 * PASS], late[:, 2 * P : run], [(0, 1)])
+            quantize_wb(wb_first[:, 2 * PASS :], late[:, run : run + 2 * P], [(0, 2), (0, 3)])
+            quantize_wb(wb_high, late[:, run + 2 * P :], [(1, 2), (2, 2), (1, 3), (2, 3)])
             for nt in range(1, N_TILES):
                 d_pass(1, nt, False, False)
                 d_pass(g, nt, False, False)
@@ -376,26 +378,24 @@ def tile_list_subtitle_couple_score_kernel(
         evac(0, 3)
         for t in range(PACK):
             pick(0, t)
-        products(0)
-        round_wb(0)
-        round_wb(1)
-        round_wb(2)
+        wb_first = round_first_wb()
         evac(1, 0)
         prepare_w1(2, 0)
         evac(1, 1)
         prepare_w1(2, 1)
+        products(0)
         evac(1, 2)
         pick(1, 0)
         prepare_d(0)
         for t in range(1, PACK):
             pick(1, t)
+        first_codes = keep.tile([P, 2 * M1], U32, name="first_codes", align_bytes=64)
+        pick(2, 0)
+        quantize_pair(0, first_codes[:])
         products(1)
         evac(2, 1)
         evac(2, 2)
         prepare_d(1)
-        first_codes = keep.tile([P, 2 * M1], U32, name="first_codes", align_bytes=64)
-        pick(2, 0)
-        quantize_pair(0, first_codes[:])
         y_acc = [psum.tile([P, M1], F32, name=f"y_acc{nt}", tag="acc", bufs=4) for nt in range(N_TILES)]
         for nt in range(N_TILES):
             d_pass(0, nt, True, False)
@@ -406,11 +406,11 @@ def tile_list_subtitle_couple_score_kernel(
             y = ring.tile([P, M1], F32, name="y", tag="raw_half", bufs=4)
             nc.scalar.copy(y[:], y_acc[nt][:])
             ys.append(y)
-        first = ring.tile([P, N_TILES, M2], F32, name="first", tag="x1", align_bytes=64)
-        other = ring.tile([P, N_TILES, M2], F32, name="other", tag="x2", align_bytes=64)
-        top = ring.tile([P, N_TILES, M2], F32, name="top", tag="w_grouped", align_bytes=64)
+        first = ring.tile([P, N_TILES, M2], F32, name="first", tag="x1", bufs=3, align_bytes=64)
+        other = ring.tile([P, N_TILES, M2], F32, name="other", tag="x2", bufs=3, align_bytes=64)
+        top = ring.tile([P, N_TILES, M2], F32, name="top", tag="even", bufs=1, align_bytes=64)
         squared = ring.tile([P, N_TILES, M2], F32, name="squared", tag="last_dist", bufs=1, align_bytes=64)
-        score = ring.tile([P, N_TILES, M2], F32, name="score", tag="w_grouped", align_bytes=64)
+        score = ring.tile([P, N_TILES, M2], F32, name="score", tag="last_prod", bufs=1, align_bytes=64)
 
         def pick_y(nt):
             nc.vector.tensor_copy(first[:, nt, :], ys[nt][:].indirect(pos3_sb[:]))

@@ -44,13 +44,19 @@ def tile_list_subtitle_couple_score_kernel(
             nc.sync.dma_start(tile[:], src)
             return tile
 
-        def load_rows(src, g, c0, width, name, bufs):
-            raw = ring.tile([P, PACK, width], F32, name=name, bufs=bufs)
+        def load_into(raw, src, g, c0, width):
             nc.sync.dma_start(
-                out=raw[:],
+                out=raw,
                 in_=src[g * PASS : (g + 1) * PASS, c0 : c0 + width].rearrange("(p j) c -> p j c", j=PACK),
             )
             return raw
+
+        def load_rows(src, g, c0, width, name, bufs):
+            raw = ring.tile([P, PACK, width], F32, name=name, bufs=bufs, align_bytes=64)
+            return load_into(raw[:], src, g, c0, width)
+
+        def staged(slot):
+            return h_tiles[slot][:].rearrange("p (j c) -> p j c", j=PACK)
 
         def quantize(grouped, name, pieces=1):
             codes = keep.tile([P, PASS], U32, name=name + "_codes", align_bytes=64)
@@ -64,8 +70,14 @@ def tile_list_subtitle_couple_score_kernel(
                 )
             return codes, scales
 
-        def round_w1(raw, tag):
+        def round_w1(raw, tag, side):
             grouped = ring.tile([P, PACK * PASS], BF16, name="w_grouped", tag=tag, bufs=1, align_bytes=64)
+            if side:
+                dst = grouped[:].rearrange("p (t m j) -> p t m j", t=PACK, j=PACK)
+                src = raw[:].rearrange("p j (m t) -> p t m j", t=PACK)
+                for t in range(PACK):
+                    nc.gpsimd.tensor_scalar(dst[:, t], src[:, t], 1.0, 0.0, ALU.mult, ALU.add)
+                return grouped
             nc.scalar.activation(
                 grouped[:].rearrange("p (t m j) -> p m j t", t=PACK, j=PACK),
                 raw[:].rearrange("p j (m t) -> p m j t", t=PACK),
@@ -73,26 +85,26 @@ def tile_list_subtitle_couple_score_kernel(
             )
             return grouped
 
-        def round_first_wb():
-            wb_first = ring.tile([P, N * PACK], BF16, name="wb_first", tag="odd", bufs=1, align_bytes=64)
-            dst = wb_first[:].rearrange("p (n j) -> p n j", j=PACK)
-            src = wb_raw[0][:].rearrange("p j n -> p n j")
-            for nt in range(N_TILES):
-                cols = slice(nt * P, (nt + 1) * P)
-                nc.gpsimd.tensor_scalar(dst[:, cols], src[:, cols], -1.0, 0.0, ALU.mult, ALU.add)
-            return wb_first
-
-        def round_later_wb(name, tiles):
-            grouped = ring.tile([P, len(tiles), H_PASSES - 1, PASS], BF16, name=name, bufs=1, align_bytes=64)
-            for i, nt in enumerate(tiles):
-                for g in range(1, H_PASSES):
-                    nc.scalar.activation(
-                        grouped[:, i, g - 1, :].rearrange("p (c i j) -> p c j i", i=PACK, j=PACK),
-                        wb_raw[g][:, :, nt * P : (nt + 1) * P].rearrange("p j (c i) -> p c j i", i=PACK),
-                        ACT.Copy,
-                        scale=-1.0,
+        def round_early_wb():
+            grouped = ring.tile([P, N_TILES, H_PASSES - 1, P, PACK], BF16, name="wb_early", tag="odd", bufs=1, align_bytes=64)
+            for g in range(H_PASSES - 1):
+                src = wb_raw[g][:].rearrange("p j n -> p n j")
+                for nt in range(N_TILES):
+                    nc.gpsimd.tensor_scalar(
+                        grouped[:, nt, g], src[:, nt * P : (nt + 1) * P], -1.0, 0.0, ALU.mult, ALU.add
                     )
-            return grouped[:].rearrange("p a g c -> p (a g c)")
+            return grouped[:].rearrange("p a g n j -> p (a g n j)")
+
+        def round_last_wb(name, tiles):
+            grouped = ring.tile([P, len(tiles) * PASS], BF16, name=name, bufs=1, align_bytes=64)
+            cols = slice(tiles[0] * P, (tiles[-1] + 1) * P)
+            nc.scalar.activation(
+                grouped[:].rearrange("p (c i j) -> p c j i", i=PACK, j=PACK),
+                wb_raw[H_PASSES - 1][:, :, cols].rearrange("p j (c i) -> p c j i", i=PACK),
+                ACT.Copy,
+                scale=-1.0,
+            )
+            return grouped
 
         tab_planes = keep.tile([P, T], U8, name="tab_planes", align_bytes=64)
         nc.gpsimd.memset(tab_planes[:].bitcast(I32), 0)
@@ -101,7 +113,7 @@ def tile_list_subtitle_couple_score_kernel(
         identity = keep.tile([P, P], F32, name="identity")
         make_identity(nc, identity[:])
         h_tiles = [keep.tile([P, 2 * S], F32, name=f"h{i}") for i in range(H_SLOTS)]
-        for i, h in enumerate(h_tiles):
+        for i, h in enumerate(h_tiles[: H_SLOTS - 1]):
             (nc.vector if i < H_SLOTS // 2 else nc.gpsimd).memset(h[:, S:], 0.0)
 
         def load_table(a):
@@ -127,10 +139,10 @@ def tile_list_subtitle_couple_score_kernel(
         pos1_sb = load_list(pos1, "pos1_sb")
         pos2_sb = load_list(pos2, "pos2_sb")
         wb_raw = {}
-        for a in range(K_PASSES):
-            w1_raw[1, a] = load_rows(w1, a, PASS, PASS, "raw", RAW_BUFS)
-        wb_raw[0] = load_rows(wb, 0, 0, N, "raw", RAW_BUFS)
+        w1_raw[1, 0] = load_rows(w1, 0, PASS, PASS, "raw", RAW_BUFS)
+        w1_raw[1, 1] = load_into(staged(3), w1, 1, PASS, PASS)
         w1_raw[2, 0] = load_rows(w1, 0, 2 * PASS, PASS, "raw", RAW_BUFS)
+        wb_raw[0] = load_rows(wb, 0, 0, N, "raw", RAW_BUFS)
         w1_raw[2, 1] = load_rows(w1, 1, 2 * PASS, PASS, "raw", RAW_BUFS)
         wb_raw[1] = load_rows(wb, 1, 0, N, "raw", RAW_BUFS)
         wb_raw[2] = load_rows(wb, 2, 0, N, "raw", RAW_BUFS)
@@ -143,7 +155,7 @@ def tile_list_subtitle_couple_score_kernel(
         w1_mx = {}
 
         def prepare_w1(g, a):
-            codes, scales = quantize(round_w1(w1_raw[g, a], ("even", "odd" if g == 1 else "pair")[a]), f"w1_{g}_{a}")
+            codes, scales = quantize(round_w1(w1_raw[g, a], (("even", "odd") if g == 1 else ("last_prod", "pair"))[a], (g, a) == (1, 0)), f"w1_{g}_{a}")
             for t in range(PACK):
                 w1_mx[g, a, t] = codes[:, t * P : (t + 1) * P], scales[:, t * P : (t + 1) * P]
 
@@ -335,12 +347,14 @@ def tile_list_subtitle_couple_score_kernel(
             pick(g, 1)
             x1, x2 = xs[g]
             low = magnitudes(subtract(x1, x2, 0))
-            wb_low = round_later_wb("wb_low", (0, 1))
+            wb_low = round_last_wb("wb_low", (0, 1))
             pick(g, 2)
             pick(g, 3)
             dist = ring.tile([P, PACK * M1], BF16, name="last_dist", bufs=1, align_bytes=64)
             prod = ring.tile([P, PACK * M1], BF16, name="last_prod", bufs=1, align_bytes=64)
             distances(x1, x2, low, dist[:], None, ("wb_high", "held"))
+            for nt in range(N_TILES):
+                d_pass(0, nt, True, False)
             quads = M1 // PACK // 2
             for half in range(2):
                 c = slice(half * quads, (half + 1) * quads)
@@ -350,9 +364,9 @@ def tile_list_subtitle_couple_score_kernel(
             b_mx[g] = quantize(prod, f"b_{g}", pieces=2)
             run = H_PASSES * P
             held = ring.tile([P, 2 * M1 + run], U32, name="held", bufs=1, align_bytes=64)
-            wb_high = round_later_wb("wb_high", (2, 3))
-            quantize_wb(wb_low[:, : 2 * PASS], held[:, 2 * M1 : 2 * M1 + 2 * P], [(1, 0), (2, 0)])
-            quantize_wb(wb_first[:, :PASS], held[:, 2 * M1 + 2 * P :], [(0, 0)])
+            wb_high = round_last_wb("wb_high", (2, 3))
+            quantize_wb(wb_early[:, : 2 * PASS], held[:, 2 * M1 : 2 * M1 + 2 * P], [(0, 0), (1, 0)])
+            quantize_wb(wb_low[:, :PASS], held[:, 2 * M1 + 2 * P :], [(2, 0)])
             quantize_pair(g - 1, held[:, : 2 * M1])
             d_mx[g] = quantize(dist, f"d_{g}")
             for gg in (g, 0, 1):
@@ -360,10 +374,10 @@ def tile_list_subtitle_couple_score_kernel(
             d_pass(1, 0, False, False)
             d_pass(g, 0, False, True)
             late = ring.tile([P, (N_TILES - 1) * run], U32, name="late", tag="last_dist", bufs=1, align_bytes=64)
-            quantize_wb(wb_low[:, 2 * PASS :], late[:, : 2 * P], [(1, 1), (2, 1)])
-            quantize_wb(wb_first[:, PASS : 2 * PASS], late[:, 2 * P : run], [(0, 1)])
-            quantize_wb(wb_first[:, 2 * PASS :], late[:, run : run + 2 * P], [(0, 2), (0, 3)])
-            quantize_wb(wb_high, late[:, run + 2 * P :], [(1, 2), (2, 2), (1, 3), (2, 3)])
+            quantize_wb(wb_early[:, 2 * PASS : 4 * PASS], late[:, : 2 * P], [(0, 1), (1, 1)])
+            quantize_wb(wb_low[:, PASS:], late[:, 2 * P : run], [(2, 1)])
+            quantize_wb(wb_early[:, 4 * PASS :], late[:, run : run + 4 * P], [(0, 2), (1, 2), (0, 3), (1, 3)])
+            quantize_wb(wb_high[:], late[:, run + 4 * P :], [(2, 2), (2, 3)])
             for nt in range(1, N_TILES):
                 d_pass(1, nt, False, False)
                 d_pass(g, nt, False, False)
@@ -376,11 +390,11 @@ def tile_list_subtitle_couple_score_kernel(
         evac(0, 2)
         prepare_w1(1, 1)
         evac(0, 3)
+        prepare_w1(2, 0)
         for t in range(PACK):
             pick(0, t)
-        wb_first = round_first_wb()
+        wb_early = round_early_wb()
         evac(1, 0)
-        prepare_w1(2, 0)
         evac(1, 1)
         prepare_w1(2, 1)
         products(0)
@@ -397,13 +411,11 @@ def tile_list_subtitle_couple_score_kernel(
         evac(2, 2)
         prepare_d(1)
         y_acc = [psum.tile([P, M1], F32, name=f"y_acc{nt}", tag="acc", bufs=4) for nt in range(N_TILES)]
-        for nt in range(N_TILES):
-            d_pass(0, nt, True, False)
         last_group(2)
 
         ys = []
         for nt in range(N_TILES):
-            y = ring.tile([P, M1], F32, name="y", tag="raw_half", bufs=4)
+            y = ring.tile([P, M1], F32, name="y", tag="raw_half", bufs=4, align_bytes=64)
             nc.scalar.copy(y[:], y_acc[nt][:])
             ys.append(y)
         first = ring.tile([P, N_TILES, M2], F32, name="first", tag="x1", bufs=3, align_bytes=64)

@@ -26,8 +26,20 @@ H_PASSES = H // PASS
 N_TILES = N // P
 M_TILES = M1 // P
 H_SLOTS = 4
-RAW_BUFS = 5
 SIDE_PIECES = 4
+KB = 1024
+
+H_AT = 0
+TAB_AT = 34 * KB
+X_AT = 50 * KB
+XN_AT = 66 * KB
+RAW_AT = 78 * KB
+WB_AT = 101 * KB
+CAST_AT = 118 * KB
+PAIR_AT = 137 * KB
+LAST_AT = 145 * KB
+TURN_AT = 154 * KB
+WIDE_AT = CAST_AT - 13 * KB // 2
 
 
 def tile_list_subtitle_couple_score_kernel(
@@ -36,88 +48,70 @@ def tile_list_subtitle_couple_score_kernel(
     nc = tc.nc
     with ExitStack() as ctx:
         keep = ctx.enter_context(tc.tile_pool(name="keep", bufs=1))
-        ring = ctx.enter_context(tc.tile_pool(name="ring", bufs=2))
+        shared = ctx.enter_context(tc.tile_pool(name="shared", bufs=1))
         psum = ctx.enter_context(tc.psum_pool(name="psum", bufs=1))
+
+        def place(name, shape, dtype, at):
+            return shared.tile([P] + shape, dtype, name=name, offset=at, align_bytes=64)
+
+        def bank(name, shape, dtype, number):
+            return psum.tile([P] + shape, dtype, name=name, tag=f"bank{number}")
 
         def load_list(src, name):
             tile = keep.tile(list(src.shape), U16, name=name)
             nc.sync.dma_start(tile[:], src)
             return tile
 
-        def load_into(raw, src, g, c0, width):
+        def load_rows(raw, src, g, c0):
+            rows = raw.rearrange("p (j c) -> p j c", j=PACK)
             nc.sync.dma_start(
-                out=raw,
-                in_=src[g * PASS : (g + 1) * PASS, c0 : c0 + width].rearrange("(p j) c -> p j c", j=PACK),
+                out=rows,
+                in_=src[g * PASS : (g + 1) * PASS, c0 : c0 + rows.shape[2]].rearrange("(p j) c -> p j c", j=PACK),
             )
-            return raw
+            return rows
 
-        def load_rows(src, g, c0, width, name, bufs):
-            raw = ring.tile([P, PACK, width], F32, name=name, bufs=bufs, align_bytes=64)
-            return load_into(raw[:], src, g, c0, width)
+        def quantize(name, grouped, codes=None):
+            width = grouped.shape[1] // PACK
+            if codes is None:
+                codes = keep.tile([P, width], U32, name=name + "_codes", align_bytes=64)[:]
+            scales = keep.tile([P, width], U8, name=name + "_scales", align_bytes=64)
+            nc.vector.quantize_mx(out=codes.bitcast(FP8X4), scales=scales[:], in_=grouped)
+            return [(codes[:, c : c + P], scales[:, c : c + P]) for c in range(0, width, P)], (codes, scales[:])
 
-        def staged(slot):
-            return h_tiles[slot][:].rearrange("p (j c) -> p j c", j=PACK)
+        def rounded(engine, dst, src, sign):
+            if engine is nc.scalar:
+                nc.scalar.activation(dst, src, ACT.Copy, scale=sign)
+            else:
+                nc.gpsimd.tensor_scalar(dst, src, sign, 0.0, ALU.mult, ALU.add)
 
-        def quantize(grouped, name, pieces=1):
-            codes = keep.tile([P, PASS], U32, name=name + "_codes", align_bytes=64)
-            scales = keep.tile([P, PASS], U8, name=name + "_scales", align_bytes=64)
-            width = PASS // pieces
-            for piece in range(pieces):
-                nc.vector.quantize_mx(
-                    out=codes[:, piece * width : (piece + 1) * width].bitcast(FP8X4),
-                    scales=scales[:, piece * width : (piece + 1) * width],
-                    in_=grouped[:, piece * width * PACK : (piece + 1) * width * PACK],
-                )
-            return codes, scales
-
-        def round_w1(raw, tag, side):
-            grouped = ring.tile([P, PACK * PASS], BF16, name="w_grouped", tag=tag, bufs=1, align_bytes=64)
-            if side:
-                dst = grouped[:].rearrange("p (t m j) -> p t m j", t=PACK, j=PACK)
-                src = raw[:].rearrange("p j (m t) -> p t m j", t=PACK)
-                for t in range(PACK):
-                    nc.gpsimd.tensor_scalar(dst[:, t], src[:, t], 1.0, 0.0, ALU.mult, ALU.add)
-                return grouped
-            nc.scalar.activation(
-                grouped[:].rearrange("p (t m j) -> p m j t", t=PACK, j=PACK),
-                raw[:].rearrange("p j (m t) -> p m j t", t=PACK),
-                ACT.Copy,
+        def round_plain(engine, grouped, raw, sign=1.0):
+            if engine is nc.gpsimd:
+                return rounded(engine, grouped.rearrange("p (c j) -> p c j", j=PACK), raw.rearrange("p j c -> p c j"), sign)
+            rounded(
+                engine,
+                grouped.rearrange("p (c i j) -> p c j i", i=PACK, j=PACK),
+                raw.rearrange("p j (c i) -> p c j i", i=PACK),
+                sign,
             )
-            return grouped
 
-        def round_early_wb():
-            grouped = ring.tile([P, N_TILES, H_PASSES - 1, P, PACK], BF16, name="wb_early", tag="odd", bufs=1, align_bytes=64)
-            for g in range(H_PASSES - 1):
-                src = wb_raw[g][:].rearrange("p j n -> p n j")
-                for nt in range(N_TILES):
-                    nc.gpsimd.tensor_scalar(
-                        grouped[:, nt, g], src[:, nt * P : (nt + 1) * P], -1.0, 0.0, ALU.mult, ALU.add
-                    )
-            return grouped[:].rearrange("p a g n j -> p (a g n j)")
-
-        def round_last_wb(name, tiles):
-            grouped = ring.tile([P, len(tiles) * PASS], BF16, name=name, bufs=1, align_bytes=64)
-            cols = slice(tiles[0] * P, (tiles[-1] + 1) * P)
-            nc.scalar.activation(
-                grouped[:].rearrange("p (c i j) -> p c j i", i=PACK, j=PACK),
-                wb_raw[H_PASSES - 1][:, :, cols].rearrange("p j (c i) -> p c j i", i=PACK),
-                ACT.Copy,
-                scale=-1.0,
-            )
-            return grouped
+        def round_dealt(engine, grouped, raw, tiles=slice(0, PACK)):
+            walk = "p t m j" if engine is nc.gpsimd else "p m j t"
+            src = raw.rearrange("p j (m t) -> p t m j", t=PACK)[:, tiles]
+            rounded(engine, grouped.rearrange("p t m j -> " + walk), src.rearrange("p t m j -> " + walk), 1.0)
 
         tab_planes = keep.tile([P, T], U8, name="tab_planes", align_bytes=64)
-        nc.gpsimd.memset(tab_planes[:].bitcast(I32), 0)
+        nc.vector.memset(tab_planes[:].bitcast(I32), 0)
         wd_planes = keep.tile([P, H_PASSES, N], U8, name="wd_planes", align_bytes=64)
         nc.gpsimd.memset(wd_planes[:].rearrange("p g n -> p (g n)").bitcast(I32), 0)
         identity = keep.tile([P, P], F32, name="identity")
         make_identity(nc, identity[:])
-        h_tiles = [keep.tile([P, 2 * S], F32, name=f"h{i}") for i in range(H_SLOTS)]
-        for i, h in enumerate(h_tiles[: H_SLOTS - 1]):
-            (nc.vector if i < H_SLOTS // 2 else nc.gpsimd).memset(h[:, S:], 0.0)
+        identity_bf = keep.tile([P, P], BF16, name="identity_bf")
+        make_identity(nc, identity_bf[:])
+        h_tiles = [place(f"h{i}", [2 * S], F32, H_AT + 8 * KB * i) for i in range(H_SLOTS)]
+        nc.gpsimd.memset(h_tiles[3][:, S:], 0.0)
 
         def load_table(a):
-            words = ring.tile([P, T], I32, name=f"tab_sb{a}", tag=f"x{a + 1}", bufs=3, align_bytes=64)
+            words = place(f"tab{a}", [T], I32, TAB_AT + 8 * KB * a)
             nc.sync.dma_start(out=words[:], in_=tab_words[a].rearrange("p t i -> p (t i)").bitcast(I32))
             return words
 
@@ -128,24 +122,19 @@ def tile_list_subtitle_couple_score_kernel(
                 out=tab_planes[32 * q : 32 * q + 4 * K_PASSES, :].bitcast(I32),
                 in_=tab_scales[:, 4 * q : 4 * q + 4, :].bitcast(I32),
             )
-        w1_raw = {}
-
-        def load_halves(a):
-            return [load_rows(w1, a, half * PASS // 2, PASS // 2, "raw_half", 4) for half in range(2)]
-
-        w1_halves = [load_halves(0)]
+        raw = {}
+        raw[0, 0] = load_rows(h_tiles[0][:, S : S + PASS], w1, 0, 0)
+        raw[0, 1] = load_rows(h_tiles[0][:, S + PASS :], w1, 1, 0)
         tab_sb.append(load_table(1))
-        w1_halves.append(load_halves(1))
+        raw[1, 0] = load_rows(h_tiles[1][:, S + PASS :], w1, 0, P)
+        raw[1, 1] = load_rows(h_tiles[0][:, :PASS], w1, 1, P)
         pos1_sb = load_list(pos1, "pos1_sb")
         pos2_sb = load_list(pos2, "pos2_sb")
-        wb_raw = {}
-        w1_raw[1, 0] = load_rows(w1, 0, PASS, PASS, "raw", RAW_BUFS)
-        w1_raw[1, 1] = load_into(staged(3), w1, 1, PASS, PASS)
-        w1_raw[2, 0] = load_rows(w1, 0, 2 * PASS, PASS, "raw", RAW_BUFS)
-        wb_raw[0] = load_rows(wb, 0, 0, N, "raw", RAW_BUFS)
-        w1_raw[2, 1] = load_rows(w1, 1, 2 * PASS, PASS, "raw", RAW_BUFS)
-        wb_raw[1] = load_rows(wb, 1, 0, N, "raw", RAW_BUFS)
-        wb_raw[2] = load_rows(wb, 2, 0, N, "raw", RAW_BUFS)
+        raw[2, 0] = load_rows(h_tiles[2][:, S:], w1, 0, 2 * P)
+        raw[2, 1] = load_rows(h_tiles[1][:, BANK : BANK + S], w1, 1, 2 * P)
+        raw[4, 0] = load_rows(place("stage4", [PACK * PASS], F32, RAW_AT)[:], w1, 0, PASS)
+        raw[4, 1] = load_rows(place("stage5", [PACK * PASS], F32, RAW_AT + 8 * KB)[:], w1, 1, PASS)
+        raw[8, 0] = load_rows(place("stage8", [PACK * PASS], F32, RAW_AT + 16 * KB)[:], w1, 0, 2 * PASS)
 
         v_codes = [keep.tile([P, S], U32, name=f"v_codes{a}", align_bytes=64) for a in range(K_PASSES)]
         v_planes = keep.tile([P, S], U8, name="v_planes", align_bytes=64)
@@ -153,70 +142,189 @@ def tile_list_subtitle_couple_score_kernel(
         nc.vector.tensor_copy(v_planes[:], tab_planes[:].indirect(offs_sb[:]))
 
         w1_mx = {}
-
-        def prepare_w1(g, a):
-            codes, scales = quantize(round_w1(w1_raw[g, a], (("even", "odd") if g == 1 else ("last_prod", "pair"))[a], (g, a) == (1, 0)), f"w1_{g}_{a}")
-            for t in range(PACK):
-                w1_mx[g, a, t] = codes[:, t * P : (t + 1) * P], scales[:, t * P : (t + 1) * P]
-
-        def first_stage(g, t):
-            h = h_tiles[(g * PACK + t) % H_SLOTS]
-            for half in range(S // BANK):
-                cols = slice(half * BANK, (half + 1) * BANK)
-                acc = psum.tile([P, BANK], F32, name="acc", bufs=4)
-                order = list(range(K_PASSES)) if g == 0 and t < 2 else list(reversed(range(K_PASSES)))
-                for a in order:
-                    codes, scales = w1_mx[g, a, t]
-                    nc.tensor.matmul_mx(
-                        out=acc[:],
-                        lhsT=codes.bitcast(FP8X4),
-                        lhsT_scale=scales,
-                        rhs=v_codes[a][:, cols].bitcast(FP8X4),
-                        rhs_scale=v_planes[4 * a : P, cols],
-                        start=(a == order[0]),
-                        stop=(a == order[-1]),
-                    )
-                if (g, t, half) == (0, 0, 1):
-                    nc.vector.tensor_copy(h[:, cols], acc[:])
-                else:
-                    nc.scalar.copy(h[:, cols], acc[:])
-            return h
-
-        head = ring.tile([P, 2 * PACK * PASS], BF16, name="pair", bufs=1, align_bytes=64)
-        head_dst = head[:].rearrange("p (a t m j) -> p a m j t", t=PACK, a=K_PASSES, j=PACK)
-        head_codes = keep.tile([P, K_PASSES * PASS], U32, name="head_codes", align_bytes=64)
-        head_scales = keep.tile([P, K_PASSES * PASS], U8, name="head_scales", align_bytes=64)
-
-        def quantize_head(c0, c1):
-            nc.vector.quantize_mx(
-                out=head_codes[:, c0:c1].bitcast(FP8X4), scales=head_scales[:, c0:c1], in_=head[:, PACK * c0 : PACK * c1]
-            )
-
-        def round_head(a, half, tiles):
-            dst = head_dst[:, a, half * P // 2 : (half + 1) * P // 2]
-            src = w1_halves[a][half][:].rearrange("p j (m t) -> p m j t", t=PACK)
-            nc.scalar.activation(dst[:, :, :, tiles], src[:, :, :, tiles], ACT.Copy)
-
-        for half in range(2):
-            round_head(0, half, slice(0, PACK))
-        quantize_head(0, PASS)
+        cast0 = place("cast0", [K_PASSES, PASS], BF16, CAST_AT + 11 * KB)
+        for a in range(K_PASSES):
+            round_plain(nc.scalar, cast0[:, a], raw[0, a])
+        w1_mx[0, 0], w1_mx[0, 1] = quantize("w0", cast0[:].rearrange("p a c -> p (a c)"))[0]
         for half in range(2):
             entries = slice(half * BANK // 16, (half + 1) * BANK // 16)
             nc.vector.tensor_copy(
                 v_codes[1][:, half * BANK : (half + 1) * BANK], tab_sb[1][:].bitcast(U32).indirect(offs_sb[:, entries])
             )
-        round_head(1, 0, slice(0, PACK))
-        round_head(1, 1, slice(0, PACK // 2))
-        quantize_head(PASS, PASS + P)
-        round_head(1, 1, slice(PACK // 2, PACK))
-        quantize_head(PASS + P, PASS + 2 * P)
-        quantize_head(PASS + 2 * P, 2 * PASS)
-        for t in range(PACK):
-            for a in range(K_PASSES):
-                cols = slice(a * PASS + t * P, a * PASS + (t + 1) * P)
-                w1_mx[0, a, t] = head_codes[:, cols], head_scales[:, cols]
+        cast1 = h_tiles[0][:, BANK:S].bitcast(BF16).rearrange("p (a c) -> p a c", a=K_PASSES)
+        for a in range(K_PASSES):
+            round_plain(nc.scalar, cast1[:, a], raw[1, a])
+        w1_mx[1, 0], w1_mx[1, 1] = quantize("w1", cast1.rearrange("p a c -> p (a c)"))[0]
 
-        wd_sb = keep.tile([P, H_PASSES, 2 * N], U8, name="wd_sb", align_bytes=64)
+        accs = {}
+
+        def h_pass(n, half, a, start, stop):
+            if start:
+                accs[n, half] = bank("acc", [BANK], F32, ((0, 2, 0, 4, 2)[n] if n <= PACK else 4 + 2 * (n % 2)) + half)
+            cols = slice(half * BANK, (half + 1) * BANK)
+            nc.tensor.matmul_mx(
+                out=accs[n, half][:],
+                lhsT=w1_mx[n, a][0].bitcast(FP8X4),
+                lhsT_scale=w1_mx[n, a][1],
+                rhs=v_codes[a][:, cols].bitcast(FP8X4),
+                rhs_scale=v_planes[4 * a : P, cols],
+                start=start,
+                stop=stop,
+            )
+
+        def evac_half(n, half):
+            for a in reversed(range(K_PASSES)):
+                h_pass(n, half, a, a == K_PASSES - 1, a == 0)
+            nc.scalar.copy(h_tiles[n % H_SLOTS][:, half * BANK : (half + 1) * BANK], accs[n, half][:])
+
+        def evac(n):
+            evac_half(n, 0)
+            evac_half(n, 1)
+
+        def gather(n, x1, x2, between=None):
+            h = h_tiles[n % H_SLOTS]
+            nc.vector.tensor_copy(x1, h[:].indirect(pos1_sb[:]))
+            if between:
+                between()
+            nc.vector.tensor_scalar(x2, h[:].indirect(pos2_sb[:]), -1.0, 0.0, ALU.mult, ALU.add)
+
+        x1_at = [XN_AT, XN_AT + 10 * KB, XN_AT + 2 * KB, CAST_AT + 12 * KB]
+        x2_at = [XN_AT + 4 * KB, XN_AT + 6 * KB, XN_AT + 8 * KB, CAST_AT - KB]
+        first_x, first_diff, first_prod = {}, {}, {}
+        prod_at = [CAST_AT + 29 * KB // 2, CAST_AT + 11 * KB, RAW_AT + 16 * KB, RAW_AT + 17 * KB]
+
+        def pick_first(j, between=None):
+            first_x[j] = place(f"x1n{j}", [M1], F32, x1_at[j]), place(f"x2n{j}", [M1], F32, x2_at[j])
+            gather(j, first_x[j][0][:], first_x[j][1][:], between)
+
+        def first_distance(j, turned):
+            diff = bank("diff0", [M_TILES, P], F32, j)
+            for mt in range(M_TILES):
+                for x, first in zip(first_x[j], (True, False)):
+                    nc.tensor.matmul(
+                        diff[:, mt, :], lhsT=x[:, mt * P : (mt + 1) * P], rhs=identity[:],
+                        is_transpose=True, start=first, stop=not first,
+                    )
+            nc.scalar.activation(
+                turned[:].rearrange("m mt u (j p) e -> m j u mt p e", j=PACK)[:, j],
+                diff[:].rearrange("m mt (p u e) -> m u mt p e", u=2, e=2),
+                ACT.Abs,
+            )
+
+        def first_product(j):
+            first_prod[j] = place(f"prodn{j}", [M1], BF16, prod_at[j])
+            nc.gpsimd.tensor_tensor(first_prod[j][:], first_x[j][0][:], first_x[j][1][:], ALU.mult)
+
+        def turn_first_products(turned):
+            words = turned[:].rearrange("m mt u p e -> m (mt u p e)").bitcast(F32)
+            words = words.rearrange("m (mt u p) -> m mt u p", mt=M_TILES, u=2)
+            for pair in range(M_TILES // 2):
+                across = bank("across", [2, PASS], BF16, 2 + pair)
+                for jj in range(2):
+                    cols = slice((2 * pair + jj) * P, (2 * pair + jj + 1) * P)
+                    for j in range(PACK):
+                        nc.tensor.transpose(across[:, jj, j * P : (j + 1) * P], first_prod[j][:, cols], identity_bf[:])
+                nc.scalar.copy(
+                    words[:, 2 * pair : 2 * pair + 2], across[:].bitcast(F32).rearrange("m jj (p u) -> m jj u p", u=2)
+                )
+
+        def turn_back(words, dist, first_bank):
+            dist_words = dist.bitcast(F32)
+            backs = [bank("back", [2, 2, P], F32, first_bank + pair) for pair in range(M_TILES // 2)]
+            for u in range(2):
+                for pair, back in enumerate(backs):
+                    for jj in range(2):
+                        nc.tensor.transpose(back[:, jj, u, :], words(2 * pair + jj, u), identity[:])
+            for pair, back in enumerate(backs):
+                nc.scalar.copy(
+                    dist_words[:, pair * BANK : (pair + 1) * BANK].rearrange("p (jj m u) -> p jj m u", jj=2, u=2),
+                    back[:].rearrange("p jj u m -> p jj m u"),
+                )
+
+        def first_words(turned):
+            words = turned[:].rearrange("m mt u p e -> m mt u (p e)").bitcast(F32)
+            return lambda mt, u: words[:, mt, u, :]
+
+        xs, halves = {}, {}
+
+        def picked(g, at):
+            flat = [place(f"x{i + 1}_{g}", [PACK * M1], F32, at + 8 * KB * i) for i in range(2)]
+            xs[g] = [x[:].rearrange("p (t m) -> p t m", t=PACK) for x in flat]
+            return flat
+
+        def pick(g, t):
+            gather(g * PACK + t, xs[g][0][:, t, :], xs[g][1][:, t, :])
+
+        def distance(g, u, first_bank, at):
+            diffs = [bank("diff", [2, 2, P], F32, first_bank + pair) for pair in range(M_TILES // 2)]
+            for e in range(2):
+                for pair, diff in enumerate(diffs):
+                    for jj in range(2):
+                        cols = slice((2 * pair + jj) * P, (2 * pair + jj + 1) * P)
+                        for x, first in zip(xs[g], (True, False)):
+                            nc.tensor.matmul(
+                                diff[:, jj, e, :], lhsT=x[:, 2 * u + e, cols], rhs=identity[:],
+                                is_transpose=True, start=first, stop=not first,
+                            )
+            for pair, diff in enumerate(diffs):
+                turned = place(f"turned{g}{u}{pair}", [2, P, 2], BF16, at + pair * KB)
+                nc.scalar.activation(turned[:], diff[:].rearrange("m jj e p -> m jj p e"), ACT.Abs)
+                halves[g, u, pair] = turned[:].rearrange("m jj p e -> m jj (p e)").bitcast(F32)
+
+        def later_words(g):
+            return lambda mt, u: halves[g, u, mt // 2][:, mt % 2, :]
+
+        def interleaved_in(x):
+            return x.rearrange("p t (c i) -> p c t i", i=PACK)
+
+        def interleaved_out(x):
+            return x.rearrange("p (c i t) -> p c t i", i=PACK, t=PACK)
+
+        def product(engine, g, prod, pieces):
+            quads = M1 // PACK // pieces
+            for piece in range(pieces):
+                c = slice(piece * quads, (piece + 1) * quads)
+                engine.tensor_tensor(
+                    interleaved_out(prod)[:, c], interleaved_in(xs[g][0])[:, c], interleaved_in(xs[g][1])[:, c], ALU.mult
+                )
+
+        def quantize_w1(n, tiles, grouped):
+            for i, operand in enumerate(quantize(f"w{n}", grouped.rearrange("p a t m j -> p (a t m j)"))[0]):
+                w1_mx[n + i % tiles, i // tiles] = operand
+
+        for half in range(2):
+            h_pass(0, half, 0, True, False)
+        h_pass(0, 0, 1, False, True)
+        nc.scalar.copy(h_tiles[0][:, :BANK], accs[0, 0][:])
+        h_pass(0, 1, 1, False, True)
+        nc.vector.tensor_copy(h_tiles[0][:, BANK:S], accs[0, 1][:])
+        casts = [place(f"cast{n}", [K_PASSES, PASS], BF16, at) for n, at in ((2, x2_at[0]), (3, CAST_AT + 13 * KB))]
+        for i, cast in enumerate(casts):
+            round_plain(nc.gpsimd, cast[:, 0], raw[2, 0][:, :, i * P : (i + 1) * P])
+        evac_half(1, 0)
+        for i, cast in enumerate(casts):
+            round_plain(nc.scalar, cast[:, 1], raw[2, 1][:, :, i * P : (i + 1) * P])
+        evac_half(1, 1)
+        pick_first(0, lambda: quantize_w1(2, 1, casts[0][:].rearrange("p a (t m j) -> p a t m j", t=1, j=PACK)))
+        w1_mx[3, 0], w1_mx[3, 1] = quantize("w3", casts[1][:].rearrange("p a c -> p (a c)"))[0]
+        evac(2)
+        pick_first(1)
+        first_product(0)
+        cast4 = place("cast4", [K_PASSES, 2, P, PACK], BF16, CAST_AT + 10 * KB)
+        cast6 = place("cast6", [K_PASSES, 2, P, PACK], BF16, CAST_AT - 2 * KB)
+        round_dealt(nc.gpsimd, cast4[:, 0], raw[4, 0], slice(0, 2))
+        round_dealt(nc.gpsimd, cast6[:, 0], raw[4, 0], slice(2, 4))
+        evac(3)
+        round_dealt(nc.scalar, cast4[:, 1], raw[4, 1], slice(0, 2))
+        round_dealt(nc.scalar, cast6[:, 1], raw[4, 1], slice(2, 4))
+        pick_first(2)
+        quantize_w1(4, 2, cast4[:])
+        first_product(1)
+        pick_first(3, lambda: quantize_w1(6, 2, cast6[:]))
+        raw[8, 1] = load_rows(h_tiles[2][:], w1, 1, 2 * PASS)
+        wb_raw = [load_rows(place(f"wb_stage{g}", [PACK * N], F32, RAW_AT - KB)[:], wb, g, 0) for g in range(1)]
+        wb_raw.append(load_rows(place("wb_stage1", [PACK * N], F32, WB_AT)[:], wb, 1, 0))
+        wd_sb = place("wd_sb", [H_PASSES, 2 * N], U8, CAST_AT + 31 * KB // 2)
         nc.sync.dma_start(out=wd_sb[:].bitcast(I32), in_=wd_words.rearrange("g p c -> p g c").bitcast(I32))
         for q in range(4):
             nc.sync.dma_start(
@@ -225,99 +333,62 @@ def tile_list_subtitle_couple_score_kernel(
             )
         pos3_sb = load_list(pos3, "pos3_sb")
         pos4_sb = load_list(pos4, "pos4_sb")
+        turned_d = place("turned_d", [M_TILES, 2, P, 2], BF16, RAW_AT + 8 * KB)
+        first_distance(0, turned_d)
+        first_distance(1, turned_d)
+        evac(4)
+        evac(5)
+        cast8 = place("cast8", [K_PASSES, PACK, P, PACK], BF16, CAST_AT + KB)
+        round_dealt(nc.gpsimd, cast8[:, 0], raw[8, 0])
+        round_dealt(nc.scalar, cast8[:, 1], raw[8, 1])
+        first_distance(2, turned_d)
+        first_distance(3, turned_d)
+        evac(6)
+        evac(7)
+        first_product(2)
+        first_product(3)
+        picked(1, X_AT)
+        pick(1, 0)
+        pick(1, 1)
+        quantize_w1(8, PACK, cast8[:])
+        wb_raw.append(load_rows(place("wb_stage2", [PACK * N], F32, XN_AT)[:], wb, 2, 0))
+        wb_early = place("wb_early", [N_TILES, H_PASSES - 1, P, PACK], BF16, WIDE_AT)
+        for g in range(H_PASSES - 1):
+            rounded(nc.gpsimd, wb_early[:, :, g], wb_raw[g].rearrange("p j (a c) -> p a c j", c=P), -1.0)
+        wb_early = wb_early[:].rearrange("p a g c j -> p (a g c j)")
+        pairs = [place(f"pair{g}", [2, PACK * M1], BF16, (PAIR_AT, WB_AT)[g]) for g in range(2)]
+        pick(1, 2)
+        distance(1, 0, 0, CAST_AT + 3 * KB // 2)
+        evac(8)
+        turn_back(first_words(turned_d), pairs[0][:, 0], 0)
+        evac(9)
+        pick(1, 3)
+        turned_b = place("turned_b", [M_TILES, 2, P, 2], BF16, CAST_AT + 7 * KB // 2)
+        turn_first_products(turned_b)
+        product(nc.gpsimd, 1, pairs[1][:, 1], SIDE_PIECES)
+        evac(10)
+        distance(1, 1, 0, TURN_AT + 2 * KB)
+        picked(2, TAB_AT)
+        pick(2, 0)
+        evac(11)
+        turn_back(first_words(turned_b), pairs[0][:, 1], 2)
+        pick(2, 1)
+        turn_back(later_words(1), pairs[1][:, 0], 0)
+        distance(2, 0, 4, TURN_AT)
+        pick(2, 2)
+        pick(2, 3)
 
-        def interleaved_in(x):
-            return x[:].rearrange("p t (c i) -> p c t i", i=PACK)
+        wb_mx, b_mx, d_mx = {}, {}, {}
+        wb_low = place("wb_low", [2 * PASS], BF16, TURN_AT + 2 * KB)
+        round_plain(nc.scalar, wb_low[:], wb_raw[2][:, :, : 2 * P], -1.0)
+        distance(2, 1, 0, TURN_AT + 7 * KB)
+        dist = place("dist", [PACK * M1], BF16, LAST_AT)
+        prod = place("prod", [PACK * M1], BF16, LAST_AT + 5 * KB)
+        turn_back(later_words(2), dist[:], 2)
+        y_acc = [bank(f"y_acc{nt}", [M1], F32, (nt + 1) % N_TILES) for nt in range(N_TILES)]
 
-        def interleaved_out(x):
-            return x[:].rearrange("p (c i t) -> p c t i", i=PACK, t=PACK)
-
-        def side_banks(name):
-            return [psum.tile([P, 2, 2, P], F32, name=name, tag="side", bufs=4) for pair in range(M_TILES // 2)]
-
-        def subtract(x1, x2, u):
-            diffs = side_banks("diff")
-            for e in range(2):
-                for pair, diff in enumerate(diffs):
-                    for jj in range(2):
-                        cols = slice((2 * pair + jj) * P, (2 * pair + jj + 1) * P)
-                        for x, first in ((x1, True), (x2, False)):
-                            nc.tensor.matmul(
-                                diff[:, jj, e, :], lhsT=x[:, 2 * u + e, cols], rhs=identity[:],
-                                is_transpose=True, start=first, stop=not first,
-                            )
-            return diffs
-
-        def magnitudes(diffs, last_tag=None):
-            words = []
-            for diff in diffs:
-                if last_tag and last_tag[len(words)]:
-                    turned = ring.tile([P, 2, P, 2], BF16, name="turned", tag=last_tag[len(words)], bufs=1, align_bytes=64)
-                else:
-                    turned = ring.tile([P, 2, P, 2], BF16, name="turned", bufs=4)
-                nc.scalar.activation(turned[:], diff[:].rearrange("m jj e p -> m jj p e"), ACT.Abs)
-                words.append(turned[:].rearrange("m jj p e -> m (jj p e)").bitcast(F32))
-            return words
-
-        def turn_back(back, words, u):
-            for jj in range(2):
-                nc.tensor.transpose(back[:, jj, u, :], words[:, jj * P : (jj + 1) * P], identity[:])
-
-        def distances(x1, x2, low, dist, between=None, last_tag=None):
-            high = subtract(x1, x2, 1)
-            backs = side_banks("back")
-            for back, words in zip(backs, low):
-                turn_back(back, words, 0)
-            dist_words = dist.bitcast(F32)
-            for back, words in zip(backs, magnitudes(high, last_tag)):
-                turn_back(back, words, 1)
-            if between:
-                evac(*between)
-            for pair, back in enumerate(backs):
-                nc.scalar.copy(
-                    dist_words[:, pair * BANK : (pair + 1) * BANK].rearrange("p (jj m u) -> p jj m u", jj=2, u=2),
-                    back[:].rearrange("p jj u m -> p jj m u"),
-                )
-
-        hs, xs, wb_mx, b_mx, d_mx = {}, {}, {}, {}, {}
-
-        def evac(g, t):
-            hs[g, t] = first_stage(g, t)
-
-        def pick(g, t):
-            if t == 0:
-                xs[g] = tuple(ring.tile([P, PACK, M1], F32, name=f"x{i}", bufs=3, align_bytes=64) for i in (1, 2))
-            x1, x2 = xs[g]
-            nc.vector.tensor_copy(x1[:, t, :], hs[g, t][:].indirect(pos1_sb[:]))
-            nc.vector.tensor_scalar(x2[:, t, :], hs[g, t][:].indirect(pos2_sb[:]), -1.0, 0.0, ALU.mult, ALU.add)
-
-        pairs = {}
-
-        def products(g):
-            x1, x2 = xs[g]
-            pairs[g] = ring.tile([P, 2 * PACK * M1], BF16, name="pair", bufs=1, align_bytes=64)
-            prod = pairs[g][:, PACK * M1 :]
-            quads = M1 // PACK // SIDE_PIECES
-            for piece in range(SIDE_PIECES):
-                c = slice(piece * quads, (piece + 1) * quads)
-                nc.gpsimd.tensor_tensor(
-                    interleaved_out(prod)[:, c], interleaved_in(x1)[:, c], interleaved_in(x2)[:, c], ALU.mult
-                )
-
-        def quantize_wb(grouped, codes, keys):
-            scales = keep.tile([P, len(keys) * P], U8, name="wb_scales%d%d" % keys[0], align_bytes=64)
-            nc.vector.quantize_mx(out=codes.bitcast(FP8X4), scales=scales[:], in_=grouped)
-            for i, key in enumerate(keys):
-                wb_mx[key] = codes[:, i * P : (i + 1) * P], scales[:, i * P : (i + 1) * P]
-
-        def prepare_d(g):
-            low = magnitudes(subtract(*xs[g], 0))
-            evac(g + 1, PACK - 1)
-            distances(*xs[g], low, pairs[g][:, : PACK * M1], *(((2, 0), None) if g == 0 else (None, (None, "wb_low"))))
-
-        def quantize_pair(g, codes):
-            scales = keep.tile([P, 2 * M1], U8, name=f"pair_scales{g}", align_bytes=64)
-            nc.vector.quantize_mx(out=codes.bitcast(FP8X4), scales=scales[:], in_=pairs[g][:])
+        def quantize_pair(g, at):
+            codes, scales = quantize(f"pair{g}", pairs[g][:].rearrange("p s c -> p (s c)"), place(f"pair_codes{g}", [2 * M1], U32, at)[:])[1]
             d_mx[g] = codes[:, :M1], scales[:, :M1]
             b_mx[g] = codes[:, M1:], scales[:, M1:]
 
@@ -326,8 +397,8 @@ def tile_list_subtitle_couple_score_kernel(
                 out=y_acc[nt][:],
                 lhsT=wb_mx[g, nt][0].bitcast(FP8X4),
                 lhsT_scale=wb_mx[g, nt][1],
-                rhs=b_mx[g][0][:].bitcast(FP8X4),
-                rhs_scale=b_mx[g][1][:],
+                rhs=b_mx[g][0].bitcast(FP8X4),
+                rhs_scale=b_mx[g][1],
                 start=start,
                 stop=stop,
             )
@@ -337,92 +408,53 @@ def tile_list_subtitle_couple_score_kernel(
                 out=y_acc[nt][:],
                 lhsT=wd_sb[:, g, 2 * nt * P : 2 * (nt + 1) * P].bitcast(FP4X4),
                 lhsT_scale=wd_planes[:, g, nt * P : (nt + 1) * P],
-                rhs=d_mx[g][0][:].bitcast(FP8X4),
-                rhs_scale=d_mx[g][1][:],
+                rhs=d_mx[g][0].bitcast(FP8X4),
+                rhs_scale=d_mx[g][1],
                 start=start,
                 stop=stop,
             )
 
-        def last_group(g):
-            pick(g, 1)
-            x1, x2 = xs[g]
-            low = magnitudes(subtract(x1, x2, 0))
-            wb_low = round_last_wb("wb_low", (0, 1))
-            pick(g, 2)
-            pick(g, 3)
-            dist = ring.tile([P, PACK * M1], BF16, name="last_dist", bufs=1, align_bytes=64)
-            prod = ring.tile([P, PACK * M1], BF16, name="last_prod", bufs=1, align_bytes=64)
-            distances(x1, x2, low, dist[:], None, ("wb_high", "held"))
-            for nt in range(N_TILES):
-                d_pass(0, nt, True, False)
-            quads = M1 // PACK // 2
-            for half in range(2):
-                c = slice(half * quads, (half + 1) * quads)
-                nc.vector.tensor_tensor(
-                    interleaved_out(prod)[:, c], interleaved_in(x1)[:, c], interleaved_in(x2)[:, c], ALU.mult
-                )
-            b_mx[g] = quantize(prod, f"b_{g}", pieces=2)
-            run = H_PASSES * P
-            held = ring.tile([P, 2 * M1 + run], U32, name="held", bufs=1, align_bytes=64)
-            wb_high = round_last_wb("wb_high", (2, 3))
-            quantize_wb(wb_early[:, : 2 * PASS], held[:, 2 * M1 : 2 * M1 + 2 * P], [(0, 0), (1, 0)])
-            quantize_wb(wb_low[:, :PASS], held[:, 2 * M1 + 2 * P :], [(2, 0)])
-            quantize_pair(g - 1, held[:, : 2 * M1])
-            d_mx[g] = quantize(dist, f"d_{g}")
-            for gg in (g, 0, 1):
-                b_pass(gg, 0, False, False)
-            d_pass(1, 0, False, False)
-            d_pass(g, 0, False, True)
-            late = ring.tile([P, (N_TILES - 1) * run], U32, name="late", tag="last_dist", bufs=1, align_bytes=64)
-            quantize_wb(wb_early[:, 2 * PASS : 4 * PASS], late[:, : 2 * P], [(0, 1), (1, 1)])
-            quantize_wb(wb_low[:, PASS:], late[:, 2 * P : run], [(2, 1)])
-            quantize_wb(wb_early[:, 4 * PASS :], late[:, run : run + 4 * P], [(0, 2), (1, 2), (0, 3), (1, 3)])
-            quantize_wb(wb_high[:], late[:, run + 4 * P :], [(2, 2), (2, 3)])
-            for nt in range(1, N_TILES):
-                d_pass(1, nt, False, False)
-                d_pass(g, nt, False, False)
-                for gg in range(H_PASSES):
-                    b_pass(gg, nt, False, gg == H_PASSES - 1)
-
-        evac(0, 0)
-        evac(0, 1)
-        prepare_w1(1, 0)
-        evac(0, 2)
-        prepare_w1(1, 1)
-        evac(0, 3)
-        prepare_w1(2, 0)
-        for t in range(PACK):
-            pick(0, t)
-        wb_early = round_early_wb()
-        evac(1, 0)
-        evac(1, 1)
-        prepare_w1(2, 1)
-        products(0)
-        evac(1, 2)
-        pick(1, 0)
-        prepare_d(0)
-        for t in range(1, PACK):
-            pick(1, t)
-        first_codes = keep.tile([P, 2 * M1], U32, name="first_codes", align_bytes=64)
-        pick(2, 0)
-        quantize_pair(0, first_codes[:])
-        products(1)
-        evac(2, 1)
-        evac(2, 2)
-        prepare_d(1)
-        y_acc = [psum.tile([P, M1], F32, name=f"y_acc{nt}", tag="acc", bufs=4) for nt in range(N_TILES)]
-        last_group(2)
+        held_at = H_AT + 8 * KB * (H_SLOTS - 1)
+        quantize_pair(0, held_at + 6 * KB)
+        product(nc.vector, 2, prod[:], 2)
+        held = place("held", [3 * P], U32, held_at)
+        wb_mx[0, 0], wb_mx[1, 0] = quantize("wb_a", wb_early[:, : 2 * PASS], held[:, : 2 * P])[0]
+        wb_mx[2, 0] = quantize("wb_b", wb_low[:, :PASS], held[:, 2 * P :])[0][0]
+        quantize_pair(1, held_at + 2 * KB)
+        for nt in range(N_TILES - 1):
+            d_pass(0, nt, True, False)
+        b_pass(0, 0, False, False)
+        d_pass(1, 0, False, False)
+        b_mx[2] = quantize("b2", prod[:])[1]
+        d_mx[2] = quantize("d2", dist[:])[1]
+        b_pass(1, 0, False, False)
+        b_pass(2, 0, False, False)
+        d_pass(2, 0, False, True)
+        wb_high = place("wb_high", [2 * PASS], BF16, TURN_AT + 17 * KB // 2)
+        round_plain(nc.scalar, wb_high[:], wb_raw[2][:, :, 2 * P :], -1.0)
+        late = place("late", [9 * P], U32, LAST_AT)
+        wb_mx[0, 1], wb_mx[1, 1] = quantize("wb_c", wb_early[:, 2 * PASS : 4 * PASS], late[:, : 2 * P])[0]
+        wb_mx[2, 1] = quantize("wb_d", wb_low[:, PASS:], late[:, 2 * P : 3 * P])[0][0]
+        wb_mx[0, 2], wb_mx[1, 2], wb_mx[0, 3], wb_mx[1, 3] = quantize("wb_e", wb_early[:, 4 * PASS :], late[:, 3 * P : 7 * P])[0]
+        wb_mx[2, 2], wb_mx[2, 3] = quantize("wb_f", wb_high[:], late[:, 7 * P :])[0]
+        for nt in range(1, N_TILES):
+            d_pass(2, nt, nt == N_TILES - 1, False)
+            d_pass(1, nt, False, False)
+            if nt == N_TILES - 1:
+                d_pass(0, nt, False, False)
+            for g in range(H_PASSES):
+                b_pass(g, nt, False, g == H_PASSES - 1)
 
         ys = []
         for nt in range(N_TILES):
-            y = ring.tile([P, M1], F32, name="y", tag="raw_half", bufs=4, align_bytes=64)
+            y = place(f"y{nt}", [M1], F32, X_AT + 2 * KB * nt)
             nc.scalar.copy(y[:], y_acc[nt][:])
             ys.append(y)
-        first = ring.tile([P, N_TILES, M2], F32, name="first", tag="x1", bufs=3, align_bytes=64)
-        other = ring.tile([P, N_TILES, M2], F32, name="other", tag="x2", bufs=3, align_bytes=64)
-        top = ring.tile([P, N_TILES, M2], F32, name="top", tag="even", bufs=1, align_bytes=64)
-        squared = ring.tile([P, N_TILES, M2], F32, name="squared", tag="last_dist", bufs=1, align_bytes=64)
-        score = ring.tile([P, N_TILES, M2], F32, name="score", tag="last_prod", bufs=1, align_bytes=64)
+        first = place("first", [N_TILES, M2], F32, X_AT + 8 * KB)
+        other = place("other", [N_TILES, M2], F32, X_AT + 12 * KB)
+        top = place("top", [N_TILES, M2], F32, TAB_AT)
+        squared = place("squared", [N_TILES, M2], F32, LAST_AT)
+        score = place("score", [N_TILES, M2], F32, TAB_AT + 4 * KB)
 
         def pick_y(nt):
             nc.vector.tensor_copy(first[:, nt, :], ys[nt][:].indirect(pos3_sb[:]))
@@ -442,11 +474,11 @@ def tile_list_subtitle_couple_score_kernel(
             nc.scalar.activation(score[:, tiles, :], squared[:, tiles, :], ACT.Copy, bias=1.0)
             store(tiles)
         pick_y(last)
-        halves = [slice(0, M2 // 2), slice(M2 // 2, M2)]
-        for c in halves:
+        parts = [slice(0, M2 // 2), slice(M2 // 2, M2)]
+        for c in parts:
             nc.vector.tensor_tensor(top[:, last, c], first[:, last, c], other[:, last, c], ALU.max)
-        for c in halves:
+        for c in parts:
             nc.vector.tensor_tensor(squared[:, last, c], top[:, last, c], top[:, last, c], ALU.mult)
-        for c in halves:
+        for c in parts:
             nc.vector.tensor_scalar(score[:, last, c], squared[:, last, c], 1.0, None, ALU.add)
         store(slice(last, N_TILES))

@@ -36,9 +36,9 @@ XN_AT = 66 * KB
 RAW_AT = 78 * KB
 WB_AT = 101 * KB
 CAST_AT = 118 * KB
-PAIR_AT = 137 * KB
-LAST_AT = 145 * KB
-TURN_AT = 154 * KB
+PAIR_AT = 139 * KB
+LAST_AT = 147 * KB
+TURN_AT = 156 * KB
 WIDE_AT = CAST_AT - 13 * KB // 2
 
 
@@ -141,6 +141,7 @@ def tile_list_subtitle_couple_score_kernel(
         nc.vector.tensor_copy(v_codes[0][:], tab_sb[0][:].bitcast(U32).indirect(offs_sb[:]))
         nc.vector.tensor_copy(v_planes[:], tab_planes[:].indirect(offs_sb[:]))
 
+        raw[8, 1] = load_rows(place("stage9", [PACK * PASS], F32, TAB_AT)[:], w1, 1, 2 * PASS)
         w1_mx = {}
         cast0 = place("cast0", [K_PASSES, PASS], BF16, CAST_AT + 11 * KB)
         for a in range(K_PASSES):
@@ -188,10 +189,10 @@ def tile_list_subtitle_couple_score_kernel(
                 between()
             nc.vector.tensor_scalar(x2, h[:].indirect(pos2_sb[:]), -1.0, 0.0, ALU.mult, ALU.add)
 
-        x1_at = [XN_AT, XN_AT + 10 * KB, XN_AT + 2 * KB, CAST_AT + 12 * KB]
-        x2_at = [XN_AT + 4 * KB, XN_AT + 6 * KB, XN_AT + 8 * KB, CAST_AT - KB]
+        x1_at = [XN_AT, XN_AT + 10 * KB, XN_AT + 2 * KB, CAST_AT + 27 * KB // 2]
+        x2_at = [XN_AT + 4 * KB, XN_AT + 6 * KB, XN_AT + 8 * KB, CAST_AT + 9 * KB]
         first_x, first_diff, first_prod = {}, {}, {}
-        prod_at = [CAST_AT + 29 * KB // 2, CAST_AT + 11 * KB, RAW_AT + 16 * KB, RAW_AT + 17 * KB]
+        prod_at = [CAST_AT + 25 * KB // 2, CAST_AT + 31 * KB // 2, RAW_AT + 16 * KB, RAW_AT + 17 * KB]
 
         def pick_first(j, between=None):
             first_x[j] = place(f"x1n{j}", [M1], F32, x1_at[j]), place(f"x2n{j}", [M1], F32, x2_at[j])
@@ -219,7 +220,7 @@ def tile_list_subtitle_couple_score_kernel(
             words = turned[:].rearrange("m mt u p e -> m (mt u p e)").bitcast(F32)
             words = words.rearrange("m (mt u p) -> m mt u p", mt=M_TILES, u=2)
             for pair in range(M_TILES // 2):
-                across = bank("across", [2, PASS], BF16, 2 + pair)
+                across = bank("across", [2, PASS], BF16, pair)
                 for jj in range(2):
                     cols = slice((2 * pair + jj) * P, (2 * pair + jj + 1) * P)
                     for j in range(PACK):
@@ -255,16 +256,18 @@ def tile_list_subtitle_couple_score_kernel(
         def pick(g, t):
             gather(g * PACK + t, xs[g][0][:, t, :], xs[g][1][:, t, :])
 
-        def distance(g, u, first_bank, at):
+        def distance(g, u, first_bank, at, between=None):
             diffs = [bank("diff", [2, 2, P], F32, first_bank + pair) for pair in range(M_TILES // 2)]
             for e in range(2):
-                for pair, diff in enumerate(diffs):
-                    for jj in range(2):
-                        cols = slice((2 * pair + jj) * P, (2 * pair + jj + 1) * P)
-                        for x, first in zip(xs[g], (True, False)):
+                if e == 1 and between:
+                    between()
+                for i, x in enumerate(xs[g]):
+                    for pair, diff in enumerate(diffs):
+                        for jj in range(2):
+                            cols = slice((2 * pair + jj) * P, (2 * pair + jj + 1) * P)
                             nc.tensor.matmul(
                                 diff[:, jj, e, :], lhsT=x[:, 2 * u + e, cols], rhs=identity[:],
-                                is_transpose=True, start=first, stop=not first,
+                                is_transpose=True, start=(e, i, jj) == (0, 0, 0), stop=(e, i, jj) == (1, 1, 1),
                             )
             for pair, diff in enumerate(diffs):
                 turned = place(f"turned{g}{u}{pair}", [2, P, 2], BF16, at + pair * KB)
@@ -281,9 +284,7 @@ def tile_list_subtitle_couple_score_kernel(
             return x.rearrange("p (c i t) -> p c t i", i=PACK, t=PACK)
 
         def product(engine, g, prod, pieces):
-            quads = M1 // PACK // pieces
-            for piece in range(pieces):
-                c = slice(piece * quads, (piece + 1) * quads)
+            for c in pieces:
                 engine.tensor_tensor(
                     interleaved_out(prod)[:, c], interleaved_in(xs[g][0])[:, c], interleaved_in(xs[g][1])[:, c], ALU.mult
                 )
@@ -292,100 +293,7 @@ def tile_list_subtitle_couple_score_kernel(
             for i, operand in enumerate(quantize(f"w{n}", grouped.rearrange("p a t m j -> p (a t m j)"))[0]):
                 w1_mx[n + i % tiles, i // tiles] = operand
 
-        for half in range(2):
-            h_pass(0, half, 0, True, False)
-        h_pass(0, 0, 1, False, True)
-        nc.scalar.copy(h_tiles[0][:, :BANK], accs[0, 0][:])
-        h_pass(0, 1, 1, False, True)
-        nc.vector.tensor_copy(h_tiles[0][:, BANK:S], accs[0, 1][:])
-        casts = [place(f"cast{n}", [K_PASSES, PASS], BF16, at) for n, at in ((2, x2_at[0]), (3, CAST_AT + 13 * KB))]
-        for i, cast in enumerate(casts):
-            round_plain(nc.gpsimd, cast[:, 0], raw[2, 0][:, :, i * P : (i + 1) * P])
-        evac_half(1, 0)
-        for i, cast in enumerate(casts):
-            round_plain(nc.scalar, cast[:, 1], raw[2, 1][:, :, i * P : (i + 1) * P])
-        evac_half(1, 1)
-        pick_first(0, lambda: quantize_w1(2, 1, casts[0][:].rearrange("p a (t m j) -> p a t m j", t=1, j=PACK)))
-        w1_mx[3, 0], w1_mx[3, 1] = quantize("w3", casts[1][:].rearrange("p a c -> p (a c)"))[0]
-        evac(2)
-        pick_first(1)
-        first_product(0)
-        cast4 = place("cast4", [K_PASSES, 2, P, PACK], BF16, CAST_AT + 10 * KB)
-        cast6 = place("cast6", [K_PASSES, 2, P, PACK], BF16, CAST_AT - 2 * KB)
-        round_dealt(nc.gpsimd, cast4[:, 0], raw[4, 0], slice(0, 2))
-        round_dealt(nc.gpsimd, cast6[:, 0], raw[4, 0], slice(2, 4))
-        evac(3)
-        round_dealt(nc.scalar, cast4[:, 1], raw[4, 1], slice(0, 2))
-        round_dealt(nc.scalar, cast6[:, 1], raw[4, 1], slice(2, 4))
-        pick_first(2)
-        quantize_w1(4, 2, cast4[:])
-        first_product(1)
-        pick_first(3, lambda: quantize_w1(6, 2, cast6[:]))
-        raw[8, 1] = load_rows(h_tiles[2][:], w1, 1, 2 * PASS)
-        wb_raw = [load_rows(place(f"wb_stage{g}", [PACK * N], F32, RAW_AT - KB)[:], wb, g, 0) for g in range(1)]
-        wb_raw.append(load_rows(place("wb_stage1", [PACK * N], F32, WB_AT)[:], wb, 1, 0))
-        wd_sb = place("wd_sb", [H_PASSES, 2 * N], U8, CAST_AT + 31 * KB // 2)
-        nc.sync.dma_start(out=wd_sb[:].bitcast(I32), in_=wd_words.rearrange("g p c -> p g c").bitcast(I32))
-        for q in range(4):
-            nc.sync.dma_start(
-                out=wd_planes[32 * q : 32 * q + 4, :, :].bitcast(I32),
-                in_=wd_scales[:, 4 * q : 4 * q + 4, :].rearrange("g r n -> r g n").bitcast(I32),
-            )
-        pos3_sb = load_list(pos3, "pos3_sb")
-        pos4_sb = load_list(pos4, "pos4_sb")
-        turned_d = place("turned_d", [M_TILES, 2, P, 2], BF16, RAW_AT + 8 * KB)
-        first_distance(0, turned_d)
-        first_distance(1, turned_d)
-        evac(4)
-        evac(5)
-        cast8 = place("cast8", [K_PASSES, PACK, P, PACK], BF16, CAST_AT + KB)
-        round_dealt(nc.gpsimd, cast8[:, 0], raw[8, 0])
-        round_dealt(nc.scalar, cast8[:, 1], raw[8, 1])
-        first_distance(2, turned_d)
-        first_distance(3, turned_d)
-        evac(6)
-        evac(7)
-        first_product(2)
-        first_product(3)
-        picked(1, X_AT)
-        pick(1, 0)
-        pick(1, 1)
-        quantize_w1(8, PACK, cast8[:])
-        wb_raw.append(load_rows(place("wb_stage2", [PACK * N], F32, XN_AT)[:], wb, 2, 0))
-        wb_early = place("wb_early", [N_TILES, H_PASSES - 1, P, PACK], BF16, WIDE_AT)
-        for g in range(H_PASSES - 1):
-            rounded(nc.gpsimd, wb_early[:, :, g], wb_raw[g].rearrange("p j (a c) -> p a c j", c=P), -1.0)
-        wb_early = wb_early[:].rearrange("p a g c j -> p (a g c j)")
-        pairs = [place(f"pair{g}", [2, PACK * M1], BF16, (PAIR_AT, WB_AT)[g]) for g in range(2)]
-        pick(1, 2)
-        distance(1, 0, 0, CAST_AT + 3 * KB // 2)
-        evac(8)
-        turn_back(first_words(turned_d), pairs[0][:, 0], 0)
-        evac(9)
-        pick(1, 3)
-        turned_b = place("turned_b", [M_TILES, 2, P, 2], BF16, CAST_AT + 7 * KB // 2)
-        turn_first_products(turned_b)
-        product(nc.gpsimd, 1, pairs[1][:, 1], SIDE_PIECES)
-        evac(10)
-        distance(1, 1, 0, TURN_AT + 2 * KB)
-        picked(2, TAB_AT)
-        pick(2, 0)
-        evac(11)
-        turn_back(first_words(turned_b), pairs[0][:, 1], 2)
-        pick(2, 1)
-        turn_back(later_words(1), pairs[1][:, 0], 0)
-        distance(2, 0, 4, TURN_AT)
-        pick(2, 2)
-        pick(2, 3)
-
         wb_mx, b_mx, d_mx = {}, {}, {}
-        wb_low = place("wb_low", [2 * PASS], BF16, TURN_AT + 2 * KB)
-        round_plain(nc.scalar, wb_low[:], wb_raw[2][:, :, : 2 * P], -1.0)
-        distance(2, 1, 0, TURN_AT + 7 * KB)
-        dist = place("dist", [PACK * M1], BF16, LAST_AT)
-        prod = place("prod", [PACK * M1], BF16, LAST_AT + 5 * KB)
-        turn_back(later_words(2), dist[:], 2)
-        y_acc = [bank(f"y_acc{nt}", [M1], F32, (nt + 1) % N_TILES) for nt in range(N_TILES)]
 
         def quantize_pair(g, at):
             codes, scales = quantize(f"pair{g}", pairs[g][:].rearrange("p s c -> p (s c)"), place(f"pair_codes{g}", [2 * M1], U32, at)[:])[1]
@@ -414,51 +322,158 @@ def tile_list_subtitle_couple_score_kernel(
                 stop=stop,
             )
 
+        for half in range(2):
+            h_pass(0, half, 0, True, False)
+        h_pass(0, 0, 1, False, True)
+        nc.scalar.copy(h_tiles[0][:, :BANK], accs[0, 0][:])
+        h_pass(0, 1, 1, False, True)
+        nc.vector.tensor_copy(h_tiles[0][:, BANK:S], accs[0, 1][:])
+        casts = [place(f"cast{n}", [K_PASSES, PASS], BF16, at) for n, at in ((2, x2_at[0]), (3, CAST_AT + 13 * KB))]
+        for i, cast in enumerate(casts):
+            round_plain(nc.gpsimd, cast[:, 0], raw[2, 0][:, :, i * P : (i + 1) * P])
+        evac_half(1, 0)
+        for i, cast in enumerate(casts):
+            round_plain(nc.scalar, cast[:, 1], raw[2, 1][:, :, i * P : (i + 1) * P])
+        evac_half(1, 1)
+        pick_first(0, lambda: quantize_w1(2, 1, casts[0][:].rearrange("p a (t m j) -> p a t m j", t=1, j=PACK)))
+        w1_mx[3, 0], w1_mx[3, 1] = quantize("w3", casts[1][:].rearrange("p a c -> p (a c)"))[0]
+        evac(2)
+        pick_first(1)
+        first_product(0)
+        cast4 = place("cast4", [K_PASSES, 2, P, PACK], BF16, CAST_AT + 27 * KB // 2)
+        cast6 = place("cast6", [K_PASSES, 2, P, PACK], BF16, CAST_AT + 17 * KB // 2)
+        round_dealt(nc.gpsimd, cast4[:, 0], raw[4, 0], slice(0, 2))
+        round_dealt(nc.gpsimd, cast6[:, 0], raw[4, 0], slice(2, 4))
+        evac(3)
+        round_dealt(nc.scalar, cast4[:, 1], raw[4, 1], slice(0, 2))
+        round_dealt(nc.scalar, cast6[:, 1], raw[4, 1], slice(2, 4))
+        pick_first(2)
+        quantize_w1(4, 2, cast4[:])
+        first_product(1)
+        pick_first(3, lambda: quantize_w1(6, 2, cast6[:]))
+        wb_raw = [load_rows(place(f"wb_stage{g}", [PACK * N], F32, RAW_AT - KB)[:], wb, g, 0) for g in range(1)]
+        wb_raw.append(load_rows(place("wb_stage1", [PACK * N], F32, WB_AT)[:], wb, 1, 0))
+        wd_sb = place("wd_sb", [H_PASSES, 2 * N], U8, CAST_AT + 35 * KB // 2)
+        nc.sync.dma_start(out=wd_sb[:].bitcast(I32), in_=wd_words.rearrange("g p c -> p g c").bitcast(I32))
+        for q in range(4):
+            nc.sync.dma_start(
+                out=wd_planes[32 * q : 32 * q + 4, :, :].bitcast(I32),
+                in_=wd_scales[:, 4 * q : 4 * q + 4, :].rearrange("g r n -> r g n").bitcast(I32),
+            )
+        pos3_sb = load_list(pos3, "pos3_sb")
+        pos4_sb = load_list(pos4, "pos4_sb")
+        turned_d = place("turned_d", [M_TILES, 2, P, 2], BF16, RAW_AT + 8 * KB)
+        first_distance(0, turned_d)
+        first_distance(1, turned_d)
+        evac(4)
+        evac(5)
+        cast8 = place("cast8", [K_PASSES, PACK, P, PACK], BF16, CAST_AT + KB)
+        round_dealt(nc.gpsimd, cast8[:, 0], raw[8, 0])
+        round_dealt(nc.scalar, cast8[:, 1], raw[8, 1])
+        first_distance(2, turned_d)
+        first_distance(3, turned_d)
+        evac(6)
+        evac(7)
+        first_product(2)
+        first_product(3)
+        picked(1, X_AT)
+        pick(1, 0)
+        pick(1, 1)
+        quantize_w1(8, PACK, cast8[:])
+        wb_raw.append(load_rows(place("wb_stage2", [PACK * N], F32, XN_AT)[:], wb, 2, 0))
+        wb_early = place("wb_early", [6 * PASS], BF16, WIDE_AT + 2 * KB)
+        wb_front = wb_early[:, : 4 * PASS].rearrange("p (a g c j) -> p g a c j", a=2, g=2, j=PACK)
+        round_plain(nc.gpsimd, wb_early[:, 4 * PASS :], wb_raw[0][:, :, 2 * P :], -1.0)
+        for g in range(2):
+            rounded(nc.gpsimd, wb_front[:, g], wb_raw[g][:, :, : 2 * P].rearrange("p j (a c) -> p a c j", c=P), -1.0)
+        pairs = [place(f"pair{g}", [2, PACK * M1], BF16, (PAIR_AT, RAW_AT - KB)[g]) for g in range(2)]
+        pick(1, 2)
+        distance(1, 0, 0, CAST_AT + 3 * KB // 2)
+        evac(8)
+        turn_back(first_words(turned_d), pairs[0][:, 0], 2)
+        evac(9)
+        pick(1, 3)
+        turned_b = place("turned_b", [M_TILES, 2, P, 2], BF16, CAST_AT + 7 * KB // 2)
+        turn_first_products(turned_b)
+        side = M1 // PACK // SIDE_PIECES
+        product(nc.gpsimd, 1, pairs[1][:, 1], [slice(i * side, (i + 1) * side) for i in range(SIDE_PIECES)])
+        evac(10)
+        turn_back(first_words(turned_b), pairs[0][:, 1], 0)
+        distance(1, 1, 2, TURN_AT + 2 * KB)
+        evac(11)
+        turn_back(later_words(1), pairs[1][:, 0], 2)
+        picked(2, TAB_AT)
+        pick(2, 0)
+        pick(2, 1)
+        distance(2, 0, 0, TURN_AT)
+        pick(2, 2)
+        quantize_pair(0, H_AT + 16 * KB)
+        y_acc = [bank(f"y_acc{nt}", [M1], F32, 4 + nt) for nt in range(N_TILES)]
+
+        def last_picks():
+            for nt in range(N_TILES):
+                d_pass(0, nt, True, False)
+            pick(2, 3)
+
+        wb_low = place("wb_low", [2 * PASS], BF16, TURN_AT + 2 * KB)
+        round_plain(nc.scalar, wb_low[:], wb_raw[2][:, :, : 2 * P], -1.0)
+        distance(2, 1, 2, TURN_AT + 7 * KB, last_picks)
+        dist = place("dist", [PACK * M1], BF16, LAST_AT)
+        prod = place("prod", [PACK * M1], BF16, LAST_AT + 5 * KB)
+        turn_back(later_words(2), dist[:], 0)
+
         held_at = H_AT + 8 * KB * (H_SLOTS - 1)
-        quantize_pair(0, held_at + 6 * KB)
-        product(nc.vector, 2, prod[:], 2)
-        held = place("held", [3 * P], U32, held_at)
-        wb_mx[0, 0], wb_mx[1, 0] = quantize("wb_a", wb_early[:, : 2 * PASS], held[:, : 2 * P])[0]
-        wb_mx[2, 0] = quantize("wb_b", wb_low[:, :PASS], held[:, 2 * P :])[0][0]
-        quantize_pair(1, held_at + 2 * KB)
-        for nt in range(N_TILES - 1):
-            d_pass(0, nt, True, False)
-        b_pass(0, 0, False, False)
-        d_pass(1, 0, False, False)
+        held = place("held", [2 * M1 + 6 * P], U32, held_at)
+        quads = M1 // PACK // 2
+        d_mx[1] = quantize("d1", pairs[1][:, 0], held[:, :M1])[1]
+        product(nc.vector, 2, prod[:], [slice(0, quads)])
+        wb_mx[0, 0], wb_mx[1, 0], wb_mx[0, 1], wb_mx[1, 1] = quantize(
+            "wb_a", wb_early[:, : 4 * PASS], held[:, 2 * M1 : 2 * M1 + 4 * P]
+        )[0]
+        product(nc.vector, 2, prod[:], [slice(quads, 2 * quads)])
+        b_mx[1] = quantize("b1", pairs[1][:, 1], held[:, M1 : 2 * M1])[1]
+        wb_mx[2, 0], wb_mx[2, 1] = quantize("wb_b", wb_low[:], held[:, 2 * M1 + 4 * P :])[0]
         b_mx[2] = quantize("b2", prod[:])[1]
         d_mx[2] = quantize("d2", dist[:])[1]
-        b_pass(1, 0, False, False)
-        b_pass(2, 0, False, False)
-        d_pass(2, 0, False, True)
-        wb_high = place("wb_high", [2 * PASS], BF16, TURN_AT + 17 * KB // 2)
-        round_plain(nc.scalar, wb_high[:], wb_raw[2][:, :, 2 * P :], -1.0)
-        late = place("late", [9 * P], U32, LAST_AT)
-        wb_mx[0, 1], wb_mx[1, 1] = quantize("wb_c", wb_early[:, 2 * PASS : 4 * PASS], late[:, : 2 * P])[0]
-        wb_mx[2, 1] = quantize("wb_d", wb_low[:, PASS:], late[:, 2 * P : 3 * P])[0][0]
-        wb_mx[0, 2], wb_mx[1, 2], wb_mx[0, 3], wb_mx[1, 3] = quantize("wb_e", wb_early[:, 4 * PASS :], late[:, 3 * P : 7 * P])[0]
-        wb_mx[2, 2], wb_mx[2, 3] = quantize("wb_f", wb_high[:], late[:, 7 * P :])[0]
-        for nt in range(1, N_TILES):
-            d_pass(2, nt, nt == N_TILES - 1, False)
+        for nt in range(N_TILES):
             d_pass(1, nt, False, False)
-            if nt == N_TILES - 1:
-                d_pass(0, nt, False, False)
+        for g in range(H_PASSES):
+            for nt in range(2):
+                b_pass(g, nt, False, False)
+        for nt in range(2):
+            d_pass(2, nt, False, True)
+        wb_high = place("wb_high", [2, 2 * PASS], BF16, TURN_AT + 17 * KB // 2)
+        for g in (1, 2):
+            round_plain(nc.scalar, wb_high[:, g - 1], wb_raw[g][:, :, 2 * P :], -1.0)
+        late = place("late", [6 * P], U32, LAST_AT)
+        wb_mx[0, 2], wb_mx[0, 3] = quantize("wb_e", wb_early[:, 4 * PASS :], late[:, : 2 * P])[0]
+        wb_mx[1, 2], wb_mx[1, 3], wb_mx[2, 2], wb_mx[2, 3] = quantize(
+            "wb_f", wb_high[:].rearrange("p g c -> p (g c)"), late[:, 2 * P :]
+        )[0]
+        for nt in range(2, N_TILES):
+            d_pass(2, nt, False, False)
             for g in range(H_PASSES):
                 b_pass(g, nt, False, g == H_PASSES - 1)
 
-        ys = []
+        ys = [place(f"y{nt}", [M1], F32, X_AT + 2 * KB * nt) for nt in range(N_TILES)]
         for nt in range(N_TILES):
-            y = place(f"y{nt}", [M1], F32, X_AT + 2 * KB * nt)
-            nc.scalar.copy(y[:], y_acc[nt][:])
-            ys.append(y)
+            nc.scalar.copy(ys[nt][:], y_acc[nt][:])
         first = place("first", [N_TILES, M2], F32, X_AT + 8 * KB)
         other = place("other", [N_TILES, M2], F32, X_AT + 12 * KB)
         top = place("top", [N_TILES, M2], F32, TAB_AT)
         squared = place("squared", [N_TILES, M2], F32, LAST_AT)
         score = place("score", [N_TILES, M2], F32, TAB_AT + 4 * KB)
 
-        def pick_y(nt):
-            nc.vector.tensor_copy(first[:, nt, :], ys[nt][:].indirect(pos3_sb[:]))
-            nc.vector.tensor_copy(other[:, nt, :], ys[nt][:].indirect(pos4_sb[:]))
+        def pick_y(nt, c, dst, pos):
+            entries = slice(c.start // 16, c.stop // 16)
+            nc.vector.tensor_copy(dst[:, nt, c], ys[nt][:].indirect(pos[:, entries]))
+
+        def larger(tiles, c):
+            nc.vector.tensor_tensor(top[:, tiles, c], first[:, tiles, c], other[:, tiles, c], ALU.max)
+
+        def finish(tiles, c):
+            nc.scalar.activation(squared[:, tiles, c], top[:, tiles, c], ACT.Square)
+            nc.scalar.activation(score[:, tiles, c], squared[:, tiles, c], ACT.Copy, bias=1.0)
 
         def store(tiles):
             nc.sync.dma_start(
@@ -466,19 +481,24 @@ def tile_list_subtitle_couple_score_kernel(
             )
 
         last = N_TILES - 1
-        for tiles in (slice(0, last - 1), slice(last - 1, last)):
-            for nt in range(tiles.start, tiles.stop):
-                pick_y(nt)
-            nc.vector.tensor_tensor(top[:, tiles, :], first[:, tiles, :], other[:, tiles, :], ALU.max)
-            nc.scalar.activation(squared[:, tiles, :], top[:, tiles, :], ACT.Square)
-            nc.scalar.activation(score[:, tiles, :], squared[:, tiles, :], ACT.Copy, bias=1.0)
-            store(tiles)
-        pick_y(last)
-        parts = [slice(0, M2 // 2), slice(M2 // 2, M2)]
-        for c in parts:
-            nc.vector.tensor_tensor(top[:, last, c], first[:, last, c], other[:, last, c], ALU.max)
-        for c in parts:
-            nc.vector.tensor_tensor(squared[:, last, c], top[:, last, c], top[:, last, c], ALU.mult)
-        for c in parts:
-            nc.vector.tensor_scalar(score[:, last, c], squared[:, last, c], 1.0, None, ALU.add)
+        whole, low, high = slice(0, M2), slice(0, M2 // 2), slice(M2 // 2, M2)
+        for nt in range(2):
+            pick_y(nt, whole, first, pos3_sb)
+            pick_y(nt, whole, other, pos4_sb)
+        pick_y(2, whole, first, pos3_sb)
+        larger(slice(0, 2), whole)
+        finish(slice(0, 2), whole)
+        store(slice(0, 2))
+        pick_y(2, whole, other, pos4_sb)
+        pick_y(last, whole, first, pos3_sb)
+        larger(slice(2, 3), whole)
+        finish(slice(2, 3), whole)
+        store(slice(2, 3))
+        pick_y(last, low, other, pos4_sb)
+        pick_y(last, high, other, pos4_sb)
+        larger(last, low)
+        larger(last, high)
+        finish(last, low)
+        nc.vector.tensor_tensor(squared[:, last, high], top[:, last, high], top[:, last, high], ALU.mult)
+        nc.vector.tensor_scalar(score[:, last, high], squared[:, last, high], 1.0, None, ALU.add)
         store(slice(last, N_TILES))

@@ -30,15 +30,15 @@ SIDE_PIECES = 4
 KB = 1024
 
 H_AT = 0
-TAB_AT = 34 * KB
-X_AT = 50 * KB
-XN_AT = 66 * KB
-RAW_AT = 78 * KB
-WB_AT = 101 * KB
-CAST_AT = 118 * KB
-PAIR_AT = 139 * KB
-LAST_AT = 147 * KB
-TURN_AT = 156 * KB
+TAB_AT = 35 * KB
+X_AT = 51 * KB
+XN_AT = 67 * KB
+RAW_AT = 79 * KB
+WB_AT = 102 * KB
+CAST_AT = 119 * KB
+PAIR_AT = 140 * KB
+LAST_AT = 148 * KB
+TURN_AT = 157 * KB
 WIDE_AT = CAST_AT - 13 * KB // 2
 
 
@@ -256,11 +256,9 @@ def tile_list_subtitle_couple_score_kernel(
         def pick(g, t):
             gather(g * PACK + t, xs[g][0][:, t, :], xs[g][1][:, t, :])
 
-        def distance(g, u, first_bank, at, between=None):
+        def distance(g, u, first_bank, at):
             diffs = [bank("diff", [2, 2, P], F32, first_bank + pair) for pair in range(M_TILES // 2)]
             for e in range(2):
-                if e == 1 and between:
-                    between()
                 for i, x in enumerate(xs[g]):
                     for pair, diff in enumerate(diffs):
                         for jj in range(2):
@@ -407,36 +405,33 @@ def tile_list_subtitle_couple_score_kernel(
         pick(2, 1)
         distance(2, 0, 0, TURN_AT)
         pick(2, 2)
-        quantize_pair(0, H_AT + 16 * KB)
-        y_acc = [bank(f"y_acc{nt}", [M1], F32, 4 + nt) for nt in range(N_TILES)]
-
-        def last_picks():
-            for nt in range(N_TILES):
-                d_pass(0, nt, True, False)
-            pick(2, 3)
+        pick(2, 3)
 
         wb_low = place("wb_low", [2 * PASS], BF16, TURN_AT + 2 * KB)
         round_plain(nc.scalar, wb_low[:], wb_raw[2][:, :, : 2 * P], -1.0)
-        distance(2, 1, 2, TURN_AT + 7 * KB, last_picks)
+        distance(2, 1, 2, TURN_AT + 7 * KB)
         dist = place("dist", [PACK * M1], BF16, LAST_AT)
         prod = place("prod", [PACK * M1], BF16, LAST_AT + 5 * KB)
         turn_back(later_words(2), dist[:], 0)
+        y_acc = [bank(f"y_acc{nt}", [M1], F32, (3, 0, 1, 4)[nt]) for nt in range(N_TILES)]
 
         held_at = H_AT + 8 * KB * (H_SLOTS - 1)
         held = place("held", [2 * M1 + 6 * P], U32, held_at)
+        quantize_pair(0, held_at + 7 * KB)
         quads = M1 // PACK // 2
-        d_mx[1] = quantize("d1", pairs[1][:, 0], held[:, :M1])[1]
         product(nc.vector, 2, prod[:], [slice(0, quads)])
+        d_mx[1] = quantize("d1", pairs[1][:, 0], held[:, :M1])[1]
+        product(nc.vector, 2, prod[:], [slice(quads, 2 * quads)])
         wb_mx[0, 0], wb_mx[1, 0], wb_mx[0, 1], wb_mx[1, 1] = quantize(
             "wb_a", wb_early[:, : 4 * PASS], held[:, 2 * M1 : 2 * M1 + 4 * P]
         )[0]
-        product(nc.vector, 2, prod[:], [slice(quads, 2 * quads)])
         b_mx[1] = quantize("b1", pairs[1][:, 1], held[:, M1 : 2 * M1])[1]
         wb_mx[2, 0], wb_mx[2, 1] = quantize("wb_b", wb_low[:], held[:, 2 * M1 + 4 * P :])[0]
         b_mx[2] = quantize("b2", prod[:])[1]
         d_mx[2] = quantize("d2", dist[:])[1]
-        for nt in range(N_TILES):
-            d_pass(1, nt, False, False)
+        for g in range(2):
+            for nt in range(N_TILES):
+                d_pass(g, nt, g == 0, False)
         for g in range(H_PASSES):
             for nt in range(2):
                 b_pass(g, nt, False, False)

@@ -79,7 +79,9 @@ def tile_list_subtitle_couple_score_kernel(
             return [(codes[:, c : c + P], scales[:, c : c + P]) for c in range(0, width, P)], (codes, scales[:])
 
         def rounded(engine, dst, src, sign):
-            if engine is nc.scalar:
+            if engine is nc.vector:
+                nc.vector.tensor_copy(dst, src)
+            elif engine is nc.scalar:
                 nc.scalar.activation(dst, src, ACT.Copy, scale=sign)
             else:
                 nc.gpsimd.tensor_scalar(dst, src, sign, 0.0, ALU.mult, ALU.add)
@@ -192,7 +194,7 @@ def tile_list_subtitle_couple_score_kernel(
         x1_at = [XN_AT, XN_AT + 10 * KB, XN_AT + 2 * KB, CAST_AT + 27 * KB // 2]
         x2_at = [XN_AT + 4 * KB, XN_AT + 6 * KB, XN_AT + 8 * KB, CAST_AT + 9 * KB]
         first_x, first_diff, first_prod = {}, {}, {}
-        prod_at = [CAST_AT + 25 * KB // 2, CAST_AT + 31 * KB // 2, RAW_AT + 16 * KB, RAW_AT + 17 * KB]
+        prod_at = [CAST_AT + 31 * KB // 2, CAST_AT + 11 * KB, CAST_AT + 12 * KB, CAST_AT + 8 * KB]
 
         def pick_first(j, between=None):
             first_x[j] = place(f"x1n{j}", [M1], F32, x1_at[j]), place(f"x2n{j}", [M1], F32, x2_at[j])
@@ -325,19 +327,19 @@ def tile_list_subtitle_couple_score_kernel(
         h_pass(0, 0, 1, False, True)
         nc.scalar.copy(h_tiles[0][:, :BANK], accs[0, 0][:])
         h_pass(0, 1, 1, False, True)
-        nc.vector.tensor_copy(h_tiles[0][:, BANK:S], accs[0, 1][:])
-        casts = [place(f"cast{n}", [K_PASSES, PASS], BF16, at) for n, at in ((2, x2_at[0]), (3, CAST_AT + 13 * KB))]
+        nc.scalar.copy(h_tiles[0][:, BANK:S], accs[0, 1][:])
+        casts = [place(f"cast{n}", [K_PASSES, PASS], BF16, at) for n, at in ((2, TURN_AT), (3, CAST_AT + 13 * KB))]
         for i, cast in enumerate(casts):
             round_plain(nc.gpsimd, cast[:, 0], raw[2, 0][:, :, i * P : (i + 1) * P])
         evac_half(1, 0)
         for i, cast in enumerate(casts):
             round_plain(nc.scalar, cast[:, 1], raw[2, 1][:, :, i * P : (i + 1) * P])
         evac_half(1, 1)
-        pick_first(0, lambda: quantize_w1(2, 1, casts[0][:].rearrange("p a (t m j) -> p a t m j", t=1, j=PACK)))
+        pick_first(0)
+        w1_mx[2, 0], w1_mx[2, 1] = quantize("w2", casts[0][:].rearrange("p a c -> p (a c)"))[0]
         w1_mx[3, 0], w1_mx[3, 1] = quantize("w3", casts[1][:].rearrange("p a c -> p (a c)"))[0]
         evac(2)
         pick_first(1)
-        first_product(0)
         cast4 = place("cast4", [K_PASSES, 2, P, PACK], BF16, CAST_AT + 27 * KB // 2)
         cast6 = place("cast6", [K_PASSES, 2, P, PACK], BF16, CAST_AT + 17 * KB // 2)
         round_dealt(nc.gpsimd, cast4[:, 0], raw[4, 0], slice(0, 2))
@@ -347,11 +349,11 @@ def tile_list_subtitle_couple_score_kernel(
         round_dealt(nc.scalar, cast6[:, 1], raw[4, 1], slice(2, 4))
         pick_first(2)
         quantize_w1(4, 2, cast4[:])
-        first_product(1)
+        first_product(0)
         pick_first(3, lambda: quantize_w1(6, 2, cast6[:]))
-        wb_raw = [load_rows(place(f"wb_stage{g}", [PACK * N], F32, RAW_AT - KB)[:], wb, g, 0) for g in range(1)]
+        wb_raw = [load_rows(place(f"wb_stage{g}", [PACK * N], F32, RAW_AT)[:], wb, g, 0) for g in range(1)]
         wb_raw.append(load_rows(place("wb_stage1", [PACK * N], F32, WB_AT)[:], wb, 1, 0))
-        wd_sb = place("wd_sb", [H_PASSES, 2 * N], U8, CAST_AT + 35 * KB // 2)
+        wd_sb = place("wd_sb", [H_PASSES, 2 * N], U8, RAW_AT + 12 * KB)
         nc.sync.dma_start(out=wd_sb[:].bitcast(I32), in_=wd_words.rearrange("g p c -> p g c").bitcast(I32))
         for q in range(4):
             nc.sync.dma_start(
@@ -365,26 +367,26 @@ def tile_list_subtitle_couple_score_kernel(
         first_distance(1, turned_d)
         evac(4)
         evac(5)
-        cast8 = place("cast8", [K_PASSES, PACK, P, PACK], BF16, CAST_AT + KB)
-        round_dealt(nc.gpsimd, cast8[:, 0], raw[8, 0])
+        cast8 = place("cast8", [K_PASSES, PACK, P, PACK], BF16, CAST_AT)
         round_dealt(nc.scalar, cast8[:, 1], raw[8, 1])
         first_distance(2, turned_d)
         first_distance(3, turned_d)
         evac(6)
         evac(7)
+        first_product(1)
         first_product(2)
         first_product(3)
         picked(1, X_AT)
         pick(1, 0)
         pick(1, 1)
+        round_dealt(nc.vector, cast8[:, 0], raw[8, 0])
         quantize_w1(8, PACK, cast8[:])
         wb_raw.append(load_rows(place("wb_stage2", [PACK * N], F32, XN_AT)[:], wb, 2, 0))
-        wb_early = place("wb_early", [6 * PASS], BF16, WIDE_AT + 2 * KB)
-        wb_front = wb_early[:, : 4 * PASS].rearrange("p (a g c j) -> p g a c j", a=2, g=2, j=PACK)
-        round_plain(nc.gpsimd, wb_early[:, 4 * PASS :], wb_raw[0][:, :, 2 * P :], -1.0)
-        for g in range(2):
-            rounded(nc.gpsimd, wb_front[:, g], wb_raw[g][:, :, : 2 * P].rearrange("p j (a c) -> p a c j", c=P), -1.0)
-        pairs = [place(f"pair{g}", [2, PACK * M1], BF16, (PAIR_AT, RAW_AT - KB)[g]) for g in range(2)]
+        wb_early = place("wb_early", [N_TILES, H_PASSES - 1, P, PACK], BF16, WIDE_AT)
+        for g in range(H_PASSES - 1):
+            rounded(nc.gpsimd, wb_early[:, :, g], wb_raw[g].rearrange("p j (a c) -> p a c j", c=P), -1.0)
+        wb_early = wb_early[:].rearrange("p a g c j -> p (a g c j)")
+        pairs = [place(f"pair{g}", [2, PACK * M1], BF16, (PAIR_AT, WB_AT)[g]) for g in range(2)]
         pick(1, 2)
         distance(1, 0, 0, CAST_AT + 3 * KB // 2)
         evac(8)
@@ -430,23 +432,23 @@ def tile_list_subtitle_couple_score_kernel(
         b_mx[2] = quantize("b2", prod[:])[1]
         d_mx[2] = quantize("d2", dist[:])[1]
         for g in range(2):
-            for nt in range(N_TILES):
+            for nt in range(N_TILES - 1):
                 d_pass(g, nt, g == 0, False)
         for g in range(H_PASSES):
             for nt in range(2):
                 b_pass(g, nt, False, False)
         for nt in range(2):
             d_pass(2, nt, False, True)
-        wb_high = place("wb_high", [2, 2 * PASS], BF16, TURN_AT + 17 * KB // 2)
-        for g in (1, 2):
-            round_plain(nc.scalar, wb_high[:, g - 1], wb_raw[g][:, :, 2 * P :], -1.0)
+        wb_high = place("wb_high", [2 * PASS], BF16, TURN_AT + 17 * KB // 2)
+        round_plain(nc.scalar, wb_high[:], wb_raw[2][:, :, 2 * P :], -1.0)
         late = place("late", [6 * P], U32, LAST_AT)
-        wb_mx[0, 2], wb_mx[0, 3] = quantize("wb_e", wb_early[:, 4 * PASS :], late[:, : 2 * P])[0]
-        wb_mx[1, 2], wb_mx[1, 3], wb_mx[2, 2], wb_mx[2, 3] = quantize(
-            "wb_f", wb_high[:].rearrange("p g c -> p (g c)"), late[:, 2 * P :]
-        )[0]
+        wb_mx[0, 2], wb_mx[1, 2], wb_mx[0, 3], wb_mx[1, 3] = quantize("wb_e", wb_early[:, 4 * PASS :], late[:, : 4 * P])[0]
+        wb_mx[2, 2], wb_mx[2, 3] = quantize("wb_f", wb_high[:], late[:, 4 * P :])[0]
         for nt in range(2, N_TILES):
-            d_pass(2, nt, False, False)
+            d_pass(2, nt, nt == N_TILES - 1, False)
+            if nt == N_TILES - 1:
+                d_pass(0, nt, False, False)
+                d_pass(1, nt, False, False)
             for g in range(H_PASSES):
                 b_pass(g, nt, False, g == H_PASSES - 1)
 

@@ -39,7 +39,7 @@ CAST_AT = 119 * KB
 PAIR_AT = 140 * KB
 LAST_AT = 148 * KB
 TURN_AT = 157 * KB
-WIDE_AT = CAST_AT - 13 * KB // 2
+WIDE_AT = CAST_AT - 7 * KB
 
 
 def tile_list_subtitle_couple_score_kernel(
@@ -136,7 +136,7 @@ def tile_list_subtitle_couple_score_kernel(
         raw[2, 1] = load_rows(h_tiles[1][:, BANK : BANK + S], w1, 1, 2 * P)
         raw[4, 0] = load_rows(place("stage4", [PACK * PASS], F32, RAW_AT)[:], w1, 0, PASS)
         raw[4, 1] = load_rows(place("stage5", [PACK * PASS], F32, RAW_AT + 8 * KB)[:], w1, 1, PASS)
-        raw[8, 0] = load_rows(place("stage8", [PACK * PASS], F32, RAW_AT + 16 * KB)[:], w1, 0, 2 * PASS)
+        raw[8, 0] = load_rows(place("stage8", [2 * PASS], F32, RAW_AT + 20 * KB)[:], w1, 0, 2 * PASS)
 
         v_codes = [keep.tile([P, S], U32, name=f"v_codes{a}", align_bytes=64) for a in range(K_PASSES)]
         v_planes = keep.tile([P, S], U8, name="v_planes", align_bytes=64)
@@ -191,10 +191,10 @@ def tile_list_subtitle_couple_score_kernel(
                 between()
             nc.vector.tensor_scalar(x2, h[:].indirect(pos2_sb[:]), -1.0, 0.0, ALU.mult, ALU.add)
 
-        x1_at = [XN_AT, XN_AT + 10 * KB, XN_AT + 2 * KB, CAST_AT + 27 * KB // 2]
+        x1_at = [XN_AT, XN_AT + 10 * KB, XN_AT + 2 * KB, CAST_AT + 33 * KB // 2]
         x2_at = [XN_AT + 4 * KB, XN_AT + 6 * KB, XN_AT + 8 * KB, CAST_AT + 9 * KB]
         first_x, first_diff, first_prod = {}, {}, {}
-        prod_at = [CAST_AT + 31 * KB // 2, CAST_AT + 11 * KB, CAST_AT + 12 * KB, CAST_AT + 8 * KB]
+        prod_at = [CAST_AT + 37 * KB // 2, CAST_AT + 11 * KB, CAST_AT + 8 * KB, CAST_AT + 7 * KB]
 
         def pick_first(j, between=None):
             first_x[j] = place(f"x1n{j}", [M1], F32, x1_at[j]), place(f"x2n{j}", [M1], F32, x2_at[j])
@@ -328,19 +328,18 @@ def tile_list_subtitle_couple_score_kernel(
         nc.scalar.copy(h_tiles[0][:, :BANK], accs[0, 0][:])
         h_pass(0, 1, 1, False, True)
         nc.scalar.copy(h_tiles[0][:, BANK:S], accs[0, 1][:])
-        casts = [place(f"cast{n}", [K_PASSES, PASS], BF16, at) for n, at in ((2, TURN_AT), (3, CAST_AT + 13 * KB))]
+        casts = [place(f"cast{n}", [K_PASSES, PASS], BF16, at) for n, at in ((2, x2_at[0]), (3, CAST_AT + 16 * KB))]
         for i, cast in enumerate(casts):
             round_plain(nc.gpsimd, cast[:, 0], raw[2, 0][:, :, i * P : (i + 1) * P])
         evac_half(1, 0)
         for i, cast in enumerate(casts):
             round_plain(nc.scalar, cast[:, 1], raw[2, 1][:, :, i * P : (i + 1) * P])
         evac_half(1, 1)
-        pick_first(0)
-        w1_mx[2, 0], w1_mx[2, 1] = quantize("w2", casts[0][:].rearrange("p a c -> p (a c)"))[0]
+        pick_first(0, lambda: quantize_w1(2, 1, casts[0][:].rearrange("p a (t m j) -> p a t m j", t=1, j=PACK)))
         w1_mx[3, 0], w1_mx[3, 1] = quantize("w3", casts[1][:].rearrange("p a c -> p (a c)"))[0]
         evac(2)
         pick_first(1)
-        cast4 = place("cast4", [K_PASSES, 2, P, PACK], BF16, CAST_AT + 27 * KB // 2)
+        cast4 = place("cast4", [K_PASSES, 2, P, PACK], BF16, CAST_AT + 33 * KB // 2)
         cast6 = place("cast6", [K_PASSES, 2, P, PACK], BF16, CAST_AT + 17 * KB // 2)
         round_dealt(nc.gpsimd, cast4[:, 0], raw[4, 0], slice(0, 2))
         round_dealt(nc.gpsimd, cast6[:, 0], raw[4, 0], slice(2, 4))
@@ -350,7 +349,14 @@ def tile_list_subtitle_couple_score_kernel(
         pick_first(2)
         quantize_w1(4, 2, cast4[:])
         first_product(0)
-        pick_first(3, lambda: quantize_w1(6, 2, cast6[:]))
+        cast8 = place("cast8", [K_PASSES, PACK, P, PACK], BF16, CAST_AT)
+
+        def weights_ahead():
+            round_dealt(nc.vector, cast8[:, 0, :, : P // 2], raw[8, 0])
+            quantize_w1(6, 2, cast6[:])
+
+        pick_first(3, weights_ahead)
+        late_rows = load_rows(place("stage10", [2 * PASS], F32, CAST_AT + 12 * KB)[:], w1, 0, 2 * PASS + PASS // 2)
         wb_raw = [load_rows(place(f"wb_stage{g}", [PACK * N], F32, RAW_AT)[:], wb, g, 0) for g in range(1)]
         wb_raw.append(load_rows(place("wb_stage1", [PACK * N], F32, WB_AT)[:], wb, 1, 0))
         wd_sb = place("wd_sb", [H_PASSES, 2 * N], U8, RAW_AT + 12 * KB)
@@ -367,7 +373,6 @@ def tile_list_subtitle_couple_score_kernel(
         first_distance(1, turned_d)
         evac(4)
         evac(5)
-        cast8 = place("cast8", [K_PASSES, PACK, P, PACK], BF16, CAST_AT)
         round_dealt(nc.scalar, cast8[:, 1], raw[8, 1])
         first_distance(2, turned_d)
         first_distance(3, turned_d)
@@ -375,25 +380,26 @@ def tile_list_subtitle_couple_score_kernel(
         evac(7)
         first_product(1)
         first_product(2)
-        first_product(3)
+        round_dealt(nc.gpsimd, cast8[:, 0, :, P // 2 :], late_rows)
         picked(1, X_AT)
         pick(1, 0)
         pick(1, 1)
-        round_dealt(nc.vector, cast8[:, 0], raw[8, 0])
         quantize_w1(8, PACK, cast8[:])
+        first_product(3)
         wb_raw.append(load_rows(place("wb_stage2", [PACK * N], F32, XN_AT)[:], wb, 2, 0))
-        wb_early = place("wb_early", [N_TILES, H_PASSES - 1, P, PACK], BF16, WIDE_AT)
-        for g in range(H_PASSES - 1):
-            rounded(nc.gpsimd, wb_early[:, :, g], wb_raw[g].rearrange("p j (a c) -> p a c j", c=P), -1.0)
-        wb_early = wb_early[:].rearrange("p a g c j -> p (a g c j)")
-        pairs = [place(f"pair{g}", [2, PACK * M1], BF16, (PAIR_AT, WB_AT)[g]) for g in range(2)]
+        wb_early = place("wb_early", [6 * PASS], BF16, WIDE_AT + 2 * KB)
+        wb_front = wb_early[:, : 4 * PASS].rearrange("p (a g c j) -> p g a c j", a=2, g=2, j=PACK)
+        for g in (1, 0):
+            rounded(nc.gpsimd, wb_front[:, g], wb_raw[g][:, :, : 2 * P].rearrange("p j (a c) -> p a c j", c=P), -1.0)
+        round_plain(nc.gpsimd, wb_early[:, 4 * PASS :], wb_raw[0][:, :, 2 * P :], -1.0)
+        pairs = [place(f"pair{g}", [2, PACK * M1], BF16, (PAIR_AT, RAW_AT)[g]) for g in range(2)]
         pick(1, 2)
-        distance(1, 0, 0, CAST_AT + 3 * KB // 2)
+        distance(1, 0, 0, CAST_AT + KB)
         evac(8)
         turn_back(first_words(turned_d), pairs[0][:, 0], 2)
         evac(9)
         pick(1, 3)
-        turned_b = place("turned_b", [M_TILES, 2, P, 2], BF16, CAST_AT + 7 * KB // 2)
+        turned_b = place("turned_b", [M_TILES, 2, P, 2], BF16, CAST_AT + 3 * KB)
         turn_first_products(turned_b)
         side = M1 // PACK // SIDE_PIECES
         product(nc.gpsimd, 1, pairs[1][:, 1], [slice(i * side, (i + 1) * side) for i in range(SIDE_PIECES)])
@@ -415,7 +421,7 @@ def tile_list_subtitle_couple_score_kernel(
         dist = place("dist", [PACK * M1], BF16, LAST_AT)
         prod = place("prod", [PACK * M1], BF16, LAST_AT + 5 * KB)
         turn_back(later_words(2), dist[:], 0)
-        y_acc = [bank(f"y_acc{nt}", [M1], F32, (3, 0, 1, 4)[nt]) for nt in range(N_TILES)]
+        y_acc = [bank(f"y_acc{nt}", [M1], F32, (3, 0, 4, 5)[nt]) for nt in range(N_TILES)]
 
         held_at = H_AT + 8 * KB * (H_SLOTS - 1)
         held = place("held", [2 * M1 + 6 * P], U32, held_at)
@@ -432,23 +438,24 @@ def tile_list_subtitle_couple_score_kernel(
         b_mx[2] = quantize("b2", prod[:])[1]
         d_mx[2] = quantize("d2", dist[:])[1]
         for g in range(2):
-            for nt in range(N_TILES - 1):
+            for nt in range(2):
                 d_pass(g, nt, g == 0, False)
         for g in range(H_PASSES):
             for nt in range(2):
                 b_pass(g, nt, False, False)
         for nt in range(2):
             d_pass(2, nt, False, True)
-        wb_high = place("wb_high", [2 * PASS], BF16, TURN_AT + 17 * KB // 2)
-        round_plain(nc.scalar, wb_high[:], wb_raw[2][:, :, 2 * P :], -1.0)
+        wb_high = place("wb_high", [2, 2 * PASS], BF16, TURN_AT + 17 * KB // 2)
+        for g in (1, 2):
+            round_plain(nc.scalar, wb_high[:, g - 1], wb_raw[g][:, :, 2 * P :], -1.0)
         late = place("late", [6 * P], U32, LAST_AT)
-        wb_mx[0, 2], wb_mx[1, 2], wb_mx[0, 3], wb_mx[1, 3] = quantize("wb_e", wb_early[:, 4 * PASS :], late[:, : 4 * P])[0]
-        wb_mx[2, 2], wb_mx[2, 3] = quantize("wb_f", wb_high[:], late[:, 4 * P :])[0]
+        wb_mx[0, 2], wb_mx[0, 3] = quantize("wb_e", wb_early[:, 4 * PASS :], late[:, : 2 * P])[0]
+        wb_mx[1, 2], wb_mx[1, 3], wb_mx[2, 2], wb_mx[2, 3] = quantize(
+            "wb_f", wb_high[:].rearrange("p g c -> p (g c)"), late[:, 2 * P :]
+        )[0]
         for nt in range(2, N_TILES):
-            d_pass(2, nt, nt == N_TILES - 1, False)
-            if nt == N_TILES - 1:
-                d_pass(0, nt, False, False)
-                d_pass(1, nt, False, False)
+            for g in reversed(range(H_PASSES)):
+                d_pass(g, nt, g == H_PASSES - 1, False)
             for g in range(H_PASSES):
                 b_pass(g, nt, False, g == H_PASSES - 1)
 

@@ -39,7 +39,6 @@ CAST_AT = 119 * KB
 PAIR_AT = 140 * KB
 LAST_AT = 148 * KB
 TURN_AT = 157 * KB
-WIDE_AT = CAST_AT - 7 * KB
 
 
 def tile_list_subtitle_couple_score_kernel(
@@ -129,14 +128,14 @@ def tile_list_subtitle_couple_score_kernel(
         raw[0, 1] = load_rows(h_tiles[0][:, S + PASS :], w1, 1, 0)
         tab_sb.append(load_table(1))
         raw[1, 0] = load_rows(h_tiles[1][:, S + PASS :], w1, 0, P)
-        raw[1, 1] = load_rows(h_tiles[0][:, :PASS], w1, 1, P)
+        raw[1, 1] = load_rows(h_tiles[0][:, BANK // 2 : BANK // 2 + PASS], w1, 1, P)
         pos1_sb = load_list(pos1, "pos1_sb")
         pos2_sb = load_list(pos2, "pos2_sb")
         raw[2, 0] = load_rows(h_tiles[2][:, S:], w1, 0, 2 * P)
         raw[2, 1] = load_rows(h_tiles[1][:, BANK : BANK + S], w1, 1, 2 * P)
         raw[4, 0] = load_rows(place("stage4", [PACK * PASS], F32, RAW_AT)[:], w1, 0, PASS)
         raw[4, 1] = load_rows(place("stage5", [PACK * PASS], F32, RAW_AT + 8 * KB)[:], w1, 1, PASS)
-        raw[8, 0] = load_rows(place("stage8", [2 * PASS], F32, RAW_AT + 20 * KB)[:], w1, 0, 2 * PASS)
+        raw[8, 0] = load_rows(place("stage8", [PACK * PASS], F32, CAST_AT - 16 * KB)[:], w1, 0, 2 * PASS)
 
         v_codes = [keep.tile([P, S], U32, name=f"v_codes{a}", align_bytes=64) for a in range(K_PASSES)]
         v_planes = keep.tile([P, S], U8, name="v_planes", align_bytes=64)
@@ -154,7 +153,7 @@ def tile_list_subtitle_couple_score_kernel(
             nc.vector.tensor_copy(
                 v_codes[1][:, half * BANK : (half + 1) * BANK], tab_sb[1][:].bitcast(U32).indirect(offs_sb[:, entries])
             )
-        cast1 = h_tiles[0][:, BANK:S].bitcast(BF16).rearrange("p (a c) -> p a c", a=K_PASSES)
+        cast1 = place("cast1", [K_PASSES, PASS], BF16, CAST_AT + 15 * KB)[:]
         for a in range(K_PASSES):
             round_plain(nc.scalar, cast1[:, a], raw[1, a])
         w1_mx[1, 0], w1_mx[1, 1] = quantize("w1", cast1.rearrange("p a c -> p (a c)"))[0]
@@ -192,9 +191,8 @@ def tile_list_subtitle_couple_score_kernel(
             nc.vector.tensor_scalar(x2, h[:].indirect(pos2_sb[:]), -1.0, 0.0, ALU.mult, ALU.add)
 
         x1_at = [XN_AT, XN_AT + 10 * KB, XN_AT + 2 * KB, CAST_AT + 33 * KB // 2]
-        x2_at = [XN_AT + 4 * KB, XN_AT + 6 * KB, XN_AT + 8 * KB, CAST_AT + 9 * KB]
+        x2_at = [CAST_AT + 14 * KB, XN_AT + 6 * KB, XN_AT + 8 * KB, CAST_AT - 11 * KB // 2]
         first_x, first_diff, first_prod = {}, {}, {}
-        prod_at = [CAST_AT + 37 * KB // 2, CAST_AT + 11 * KB, CAST_AT + 8 * KB, CAST_AT + 7 * KB]
 
         def pick_first(j, between=None):
             first_x[j] = place(f"x1n{j}", [M1], F32, x1_at[j]), place(f"x2n{j}", [M1], F32, x2_at[j])
@@ -215,8 +213,7 @@ def tile_list_subtitle_couple_score_kernel(
             )
 
         def first_product(j):
-            first_prod[j] = place(f"prodn{j}", [M1], BF16, prod_at[j])
-            nc.gpsimd.tensor_tensor(first_prod[j][:], first_x[j][0][:], first_x[j][1][:], ALU.mult)
+            nc.gpsimd.tensor_tensor(first_prod[j], first_x[j][0][:], first_x[j][1][:], ALU.mult)
 
         def turn_first_products(turned):
             words = turned[:].rearrange("m mt u p e -> m (mt u p e)").bitcast(F32)
@@ -340,7 +337,7 @@ def tile_list_subtitle_couple_score_kernel(
         evac(2)
         pick_first(1)
         cast4 = place("cast4", [K_PASSES, 2, P, PACK], BF16, CAST_AT + 33 * KB // 2)
-        cast6 = place("cast6", [K_PASSES, 2, P, PACK], BF16, CAST_AT + 17 * KB // 2)
+        cast6 = place("cast6", [K_PASSES, 2, P, PACK], BF16, CAST_AT - 8 * KB)
         round_dealt(nc.gpsimd, cast4[:, 0], raw[4, 0], slice(0, 2))
         round_dealt(nc.gpsimd, cast6[:, 0], raw[4, 0], slice(2, 4))
         evac(3)
@@ -348,15 +345,15 @@ def tile_list_subtitle_couple_score_kernel(
         round_dealt(nc.scalar, cast6[:, 1], raw[4, 1], slice(2, 4))
         pick_first(2)
         quantize_w1(4, 2, cast4[:])
+        first_prod[0] = place("prod_first", [M1], BF16, CAST_AT + 37 * KB // 2)[:]
         first_product(0)
         cast8 = place("cast8", [K_PASSES, PACK, P, PACK], BF16, CAST_AT)
 
         def weights_ahead():
-            round_dealt(nc.vector, cast8[:, 0, :, : P // 2], raw[8, 0])
+            round_dealt(nc.vector, cast8[:, 0], raw[8, 0])
             quantize_w1(6, 2, cast6[:])
 
         pick_first(3, weights_ahead)
-        late_rows = load_rows(place("stage10", [2 * PASS], F32, CAST_AT + 12 * KB)[:], w1, 0, 2 * PASS + PASS // 2)
         wb_raw = [load_rows(place(f"wb_stage{g}", [PACK * N], F32, RAW_AT)[:], wb, g, 0) for g in range(1)]
         wb_raw.append(load_rows(place("wb_stage1", [PACK * N], F32, WB_AT)[:], wb, 1, 0))
         wd_sb = place("wd_sb", [H_PASSES, 2 * N], U8, RAW_AT + 12 * KB)
@@ -378,28 +375,30 @@ def tile_list_subtitle_couple_score_kernel(
         first_distance(3, turned_d)
         evac(6)
         evac(7)
+        prod_rest = place("prod_rest", [PACK - 1, M1], BF16, CAST_AT - 17 * KB // 2)
+        for j in range(1, PACK):
+            first_prod[j] = prod_rest[:, j - 1]
         first_product(1)
         first_product(2)
-        round_dealt(nc.gpsimd, cast8[:, 0, :, P // 2 :], late_rows)
+        first_product(3)
         picked(1, X_AT)
         pick(1, 0)
         pick(1, 1)
         quantize_w1(8, PACK, cast8[:])
-        first_product(3)
         wb_raw.append(load_rows(place("wb_stage2", [PACK * N], F32, XN_AT)[:], wb, 2, 0))
-        wb_early = place("wb_early", [6 * PASS], BF16, WIDE_AT + 2 * KB)
+        wb_early = place("wb_early", [6 * PASS], BF16, CAST_AT - 7 * KB // 2)
         wb_front = wb_early[:, : 4 * PASS].rearrange("p (a g c j) -> p g a c j", a=2, g=2, j=PACK)
         for g in (1, 0):
             rounded(nc.gpsimd, wb_front[:, g], wb_raw[g][:, :, : 2 * P].rearrange("p j (a c) -> p a c j", c=P), -1.0)
         round_plain(nc.gpsimd, wb_early[:, 4 * PASS :], wb_raw[0][:, :, 2 * P :], -1.0)
         pairs = [place(f"pair{g}", [2, PACK * M1], BF16, (PAIR_AT, RAW_AT)[g]) for g in range(2)]
         pick(1, 2)
-        distance(1, 0, 0, CAST_AT + KB)
+        distance(1, 0, 0, CAST_AT + 5 * KB // 2)
         evac(8)
         turn_back(first_words(turned_d), pairs[0][:, 0], 2)
         evac(9)
         pick(1, 3)
-        turned_b = place("turned_b", [M_TILES, 2, P, 2], BF16, CAST_AT + 3 * KB)
+        turned_b = place("turned_b", [M_TILES, 2, P, 2], BF16, CAST_AT + 9 * KB // 2)
         turn_first_products(turned_b)
         side = M1 // PACK // SIDE_PIECES
         product(nc.gpsimd, 1, pairs[1][:, 1], [slice(i * side, (i + 1) * side) for i in range(SIDE_PIECES)])

@@ -27,6 +27,7 @@ N_TILES = N // P
 M_TILES = M1 // P
 H_SLOTS = 4
 SIDE_PIECES = 4
+RUN = 8
 KB = 1024
 
 H_AT = 0
@@ -69,6 +70,13 @@ def tile_list_subtitle_couple_score_kernel(
             )
             return rows
 
+        def load_runs(raw, src, g):
+            rows = raw.rearrange("p (t c) -> p t c", t=PACK)
+            runs = src[g * PASS : (g + 1) * PASS, :].rearrange("(b t i) c -> t b i c", t=PACK, i=RUN)
+            for t in range(PACK):
+                nc.sync.dma_start(out=rows[:, t], in_=runs[t])
+            return rows
+
         def quantize(name, grouped, codes=None):
             width = grouped.shape[1] // PACK
             if codes is None:
@@ -95,10 +103,17 @@ def tile_list_subtitle_couple_score_kernel(
                 sign,
             )
 
-        def round_dealt(engine, grouped, raw, tiles=slice(0, PACK)):
-            walk = "p t m j" if engine is nc.gpsimd else "p m j t"
-            src = raw.rearrange("p j (m t) -> p t m j", t=PACK)[:, tiles]
-            rounded(engine, grouped.rearrange("p t m j -> " + walk), src.rearrange("p t m j -> " + walk), 1.0)
+        def round_dealt(engine, grouped, raw):
+            rounded(engine, grouped.rearrange("p t m j -> p m j t"), raw.rearrange("p j (m t) -> p m j t", t=PACK), 1.0)
+
+        def round_runs(engine, grouped, raw, tiles):
+            if engine is nc.gpsimd:
+                src = raw.rearrange("p j (b t i) -> p b t i j", t=PACK, i=RUN)[:, :, tiles]
+                return rounded(engine, grouped.rearrange("p t (b i) j -> p b t i j", i=RUN), src, 1.0)
+            src = raw.rearrange("p j (b t h i) -> p t b h j i", t=PACK, h=RUN // PACK, i=PACK)
+            dst = grouped.rearrange("p t (b h i) j -> p t b h j i", h=RUN // PACK, i=PACK)
+            for t in range(tiles.start, tiles.stop):
+                nc.scalar.copy(dst[:, t - tiles.start], src[:, t])
 
         tab_planes = keep.tile([P, T], U8, name="tab_planes", align_bytes=64)
         nc.vector.memset(tab_planes[:].bitcast(I32), 0)
@@ -271,6 +286,27 @@ def tile_list_subtitle_couple_score_kernel(
                 nc.scalar.activation(turned[:], diff[:].rearrange("m jj e p -> m jj p e"), ACT.Abs)
                 halves[g, u, pair] = turned[:].rearrange("m jj p e -> m jj (p e)").bitcast(F32)
 
+        def run_distance(g, u, first_bank, turned):
+            diffs = [bank("diff", [2, 2, P], F32, first_bank + pair) for pair in range(M_TILES // 2)]
+            for e in range(2):
+                for i, x in enumerate(xs[g]):
+                    for pair, diff in enumerate(diffs):
+                        for jj in range(2):
+                            cols = slice((2 * pair + jj) * P, (2 * pair + jj + 1) * P)
+                            nc.tensor.matmul(
+                                diff[:, e, jj, :], lhsT=x[:, 2 * u + e, cols], rhs=identity[:],
+                                is_transpose=True, start=(e, i, jj) == (0, 0, 0), stop=(e, i, jj) == (1, 1, 1),
+                            )
+            for pair, diff in enumerate(diffs):
+                nc.scalar.activation(
+                    turned[pair][:].rearrange("m jj (b u e i) -> m u jj b e i", u=2, e=2, i=RUN)[:, u],
+                    diff[:].rearrange("m e jj (b i) -> m jj b e i", i=RUN),
+                    ACT.Abs,
+                )
+
+        def run_words(turned):
+            return lambda mt, u: turned[mt // 2][:].bitcast(F32)[:, mt % 2, u : 2 * P : 2]
+
         def later_words(g):
             return lambda mt, u: halves[g, u, mt // 2][:, mt % 2, :]
 
@@ -338,11 +374,11 @@ def tile_list_subtitle_couple_score_kernel(
         pick_first(1)
         cast4 = place("cast4", [K_PASSES, 2, P, PACK], BF16, CAST_AT + 33 * KB // 2)
         cast6 = place("cast6", [K_PASSES, 2, P, PACK], BF16, CAST_AT - 8 * KB)
-        round_dealt(nc.gpsimd, cast4[:, 0], raw[4, 0], slice(0, 2))
-        round_dealt(nc.gpsimd, cast6[:, 0], raw[4, 0], slice(2, 4))
+        round_runs(nc.gpsimd, cast4[:, 0], raw[4, 0], slice(0, 2))
+        round_runs(nc.gpsimd, cast6[:, 0], raw[4, 0], slice(2, 4))
         evac(3)
-        round_dealt(nc.scalar, cast4[:, 1], raw[4, 1], slice(0, 2))
-        round_dealt(nc.scalar, cast6[:, 1], raw[4, 1], slice(2, 4))
+        round_runs(nc.scalar, cast4[:, 1], raw[4, 1], slice(0, 2))
+        round_runs(nc.scalar, cast6[:, 1], raw[4, 1], slice(2, 4))
         pick_first(2)
         quantize_w1(4, 2, cast4[:])
         first_prod[0] = place("prod_first", [M1], BF16, CAST_AT + 37 * KB // 2)[:]
@@ -355,7 +391,7 @@ def tile_list_subtitle_couple_score_kernel(
 
         pick_first(3, weights_ahead)
         wb_raw = [load_rows(place(f"wb_stage{g}", [PACK * N], F32, RAW_AT)[:], wb, g, 0) for g in range(1)]
-        wb_raw.append(load_rows(place("wb_stage1", [PACK * N], F32, WB_AT)[:], wb, 1, 0))
+        wb_raw.append(load_runs(place("wb_stage1", [PACK * N], F32, WB_AT)[:], wb, 1))
         wd_sb = place("wd_sb", [H_PASSES, 2 * N], U8, RAW_AT + 12 * KB)
         nc.sync.dma_start(out=wd_sb[:].bitcast(I32), in_=wd_words.rearrange("g p c -> p g c").bitcast(I32))
         for q in range(4):
@@ -386,14 +422,15 @@ def tile_list_subtitle_couple_score_kernel(
         pick(1, 1)
         quantize_w1(8, PACK, cast8[:])
         wb_raw.append(load_rows(place("wb_stage2", [PACK * N], F32, XN_AT)[:], wb, 2, 0))
-        wb_early = place("wb_early", [6 * PASS], BF16, CAST_AT - 7 * KB // 2)
+        wb_early = place("wb_early", [6 * PASS], BF16, CAST_AT - 11 * KB // 2)
         wb_front = wb_early[:, : 4 * PASS].rearrange("p (a g c j) -> p g a c j", a=2, g=2, j=PACK)
         for g in (1, 0):
             rounded(nc.gpsimd, wb_front[:, g], wb_raw[g][:, :, : 2 * P].rearrange("p j (a c) -> p a c j", c=P), -1.0)
         round_plain(nc.gpsimd, wb_early[:, 4 * PASS :], wb_raw[0][:, :, 2 * P :], -1.0)
         pairs = [place(f"pair{g}", [2, PACK * M1], BF16, (PAIR_AT, RAW_AT)[g]) for g in range(2)]
         pick(1, 2)
-        distance(1, 0, 0, CAST_AT + 5 * KB // 2)
+        turned1 = [place(f"turned1{pair}", [2, PASS], BF16, CAST_AT + KB // 2 + 2 * KB * pair) for pair in range(2)]
+        run_distance(1, 0, 0, turned1)
         evac(8)
         turn_back(first_words(turned_d), pairs[0][:, 0], 2)
         evac(9)
@@ -404,9 +441,9 @@ def tile_list_subtitle_couple_score_kernel(
         product(nc.gpsimd, 1, pairs[1][:, 1], [slice(i * side, (i + 1) * side) for i in range(SIDE_PIECES)])
         evac(10)
         turn_back(first_words(turned_b), pairs[0][:, 1], 0)
-        distance(1, 1, 2, TURN_AT + 2 * KB)
+        run_distance(1, 1, 2, turned1)
         evac(11)
-        turn_back(later_words(1), pairs[1][:, 0], 2)
+        turn_back(run_words(turned1), pairs[1][:, 0], 2)
         picked(2, TAB_AT)
         pick(2, 0)
         pick(2, 1)
@@ -414,7 +451,7 @@ def tile_list_subtitle_couple_score_kernel(
         pick(2, 2)
         pick(2, 3)
 
-        wb_low = place("wb_low", [2 * PASS], BF16, TURN_AT + 2 * KB)
+        wb_low = place("wb_low", [2 * PASS], BF16, CAST_AT + 5 * KB // 2)
         round_plain(nc.scalar, wb_low[:], wb_raw[2][:, :, : 2 * P], -1.0)
         distance(2, 1, 2, TURN_AT + 7 * KB)
         dist = place("dist", [PACK * M1], BF16, LAST_AT)

@@ -86,9 +86,7 @@ def tile_list_subtitle_couple_score_kernel(
             return [(codes[:, c : c + P], scales[:, c : c + P]) for c in range(0, width, P)], (codes, scales[:])
 
         def rounded(engine, dst, src, sign):
-            if engine is nc.vector:
-                nc.vector.tensor_copy(dst, src)
-            elif engine is nc.scalar:
+            if engine is nc.scalar:
                 nc.scalar.activation(dst, src, ACT.Copy, scale=sign)
             else:
                 nc.gpsimd.tensor_scalar(dst, src, sign, 0.0, ALU.mult, ALU.add)
@@ -102,9 +100,6 @@ def tile_list_subtitle_couple_score_kernel(
                 raw.rearrange("p j (c i) -> p c j i", i=PACK),
                 sign,
             )
-
-        def round_dealt(engine, grouped, raw):
-            rounded(engine, grouped.rearrange("p t m j -> p m j t"), raw.rearrange("p j (m t) -> p m j t", t=PACK), 1.0)
 
         def round_runs(engine, grouped, raw, tiles):
             if engine is nc.gpsimd:
@@ -206,7 +201,7 @@ def tile_list_subtitle_couple_score_kernel(
             nc.vector.tensor_scalar(x2, h[:].indirect(pos2_sb[:]), -1.0, 0.0, ALU.mult, ALU.add)
 
         x1_at = [XN_AT, XN_AT + 10 * KB, XN_AT + 2 * KB, CAST_AT + 33 * KB // 2]
-        x2_at = [CAST_AT + 14 * KB, XN_AT + 6 * KB, XN_AT + 8 * KB, CAST_AT - 11 * KB // 2]
+        x2_at = [CAST_AT + 14 * KB, XN_AT + 6 * KB, XN_AT + 8 * KB, CAST_AT - 7 * KB]
         first_x, first_diff, first_prod = {}, {}, {}
 
         def pick_first(j, between=None):
@@ -260,7 +255,7 @@ def tile_list_subtitle_couple_score_kernel(
             words = turned[:].rearrange("m mt u p e -> m mt u (p e)").bitcast(F32)
             return lambda mt, u: words[:, mt, u, :]
 
-        xs, halves = {}, {}
+        xs = {}
 
         def picked(g, at):
             flat = [place(f"x{i + 1}_{g}", [PACK * M1], F32, at + 8 * KB * i) for i in range(2)]
@@ -269,22 +264,6 @@ def tile_list_subtitle_couple_score_kernel(
 
         def pick(g, t):
             gather(g * PACK + t, xs[g][0][:, t, :], xs[g][1][:, t, :])
-
-        def distance(g, u, first_bank, at):
-            diffs = [bank("diff", [2, 2, P], F32, first_bank + pair) for pair in range(M_TILES // 2)]
-            for e in range(2):
-                for i, x in enumerate(xs[g]):
-                    for pair, diff in enumerate(diffs):
-                        for jj in range(2):
-                            cols = slice((2 * pair + jj) * P, (2 * pair + jj + 1) * P)
-                            nc.tensor.matmul(
-                                diff[:, jj, e, :], lhsT=x[:, 2 * u + e, cols], rhs=identity[:],
-                                is_transpose=True, start=(e, i, jj) == (0, 0, 0), stop=(e, i, jj) == (1, 1, 1),
-                            )
-            for pair, diff in enumerate(diffs):
-                turned = place(f"turned{g}{u}{pair}", [2, P, 2], BF16, at + pair * KB)
-                nc.scalar.activation(turned[:], diff[:].rearrange("m jj e p -> m jj p e"), ACT.Abs)
-                halves[g, u, pair] = turned[:].rearrange("m jj p e -> m jj (p e)").bitcast(F32)
 
         def run_distance(g, u, first_bank, turned):
             diffs = [bank("diff", [2, 2, P], F32, first_bank + pair) for pair in range(M_TILES // 2)]
@@ -306,9 +285,6 @@ def tile_list_subtitle_couple_score_kernel(
 
         def run_words(turned):
             return lambda mt, u: turned[mt // 2][:].bitcast(F32)[:, mt % 2, u : 2 * P : 2]
-
-        def later_words(g):
-            return lambda mt, u: halves[g, u, mt // 2][:, mt % 2, :]
 
         def interleaved_in(x):
             return x.rearrange("p t (c i) -> p c t i", i=PACK)
@@ -373,7 +349,7 @@ def tile_list_subtitle_couple_score_kernel(
         evac(2)
         pick_first(1)
         cast4 = place("cast4", [K_PASSES, 2, P, PACK], BF16, CAST_AT + 33 * KB // 2)
-        cast6 = place("cast6", [K_PASSES, 2, P, PACK], BF16, CAST_AT - 8 * KB)
+        cast6 = place("cast6", [K_PASSES, 2, P, PACK], BF16, CAST_AT - 15 * KB // 2)
         round_runs(nc.gpsimd, cast4[:, 0], raw[4, 0], slice(0, 2))
         round_runs(nc.gpsimd, cast6[:, 0], raw[4, 0], slice(2, 4))
         evac(3)
@@ -383,13 +359,9 @@ def tile_list_subtitle_couple_score_kernel(
         quantize_w1(4, 2, cast4[:])
         first_prod[0] = place("prod_first", [M1], BF16, CAST_AT + 37 * KB // 2)[:]
         first_product(0)
-        cast8 = place("cast8", [K_PASSES, PACK, P, PACK], BF16, CAST_AT)
-
-        def weights_ahead():
-            round_dealt(nc.vector, cast8[:, 0], raw[8, 0])
-            quantize_w1(6, 2, cast6[:])
-
-        pick_first(3, weights_ahead)
+        cast8 = place("cast8", [K_PASSES, PACK, P, PACK], BF16, CAST_AT - 5 * KB)
+        pick_first(3, lambda: quantize_w1(6, 2, cast6[:]))
+        round_runs(nc.gpsimd, cast8[:, 0], raw[8, 0], slice(0, PACK))
         wb_raw = [load_rows(place(f"wb_stage{g}", [PACK * N], F32, RAW_AT)[:], wb, g, 0) for g in range(1)]
         wb_raw.append(load_runs(place("wb_stage1", [PACK * N], F32, WB_AT)[:], wb, 1))
         wd_sb = place("wd_sb", [H_PASSES, 2 * N], U8, RAW_AT + 12 * KB)
@@ -406,36 +378,36 @@ def tile_list_subtitle_couple_score_kernel(
         first_distance(1, turned_d)
         evac(4)
         evac(5)
-        round_dealt(nc.scalar, cast8[:, 1], raw[8, 1])
+        round_runs(nc.scalar, cast8[:, 1], raw[8, 1], slice(0, PACK))
         first_distance(2, turned_d)
         first_distance(3, turned_d)
         evac(6)
         evac(7)
-        prod_rest = place("prod_rest", [PACK - 1, M1], BF16, CAST_AT - 17 * KB // 2)
-        for j in range(1, PACK):
+        prod_rest = place("prod_rest", [2, M1], BF16, CAST_AT - 9 * KB)
+        for j in (1, 2):
             first_prod[j] = prod_rest[:, j - 1]
-        first_product(1)
-        first_product(2)
-        first_product(3)
+            first_product(j)
         picked(1, X_AT)
         pick(1, 0)
         pick(1, 1)
         quantize_w1(8, PACK, cast8[:])
-        wb_raw.append(load_rows(place("wb_stage2", [PACK * N], F32, XN_AT)[:], wb, 2, 0))
-        wb_early = place("wb_early", [6 * PASS], BF16, CAST_AT - 11 * KB // 2)
+        first_prod[3] = place("prod_last", [M1], BF16, CAST_AT - 5 * KB)[:]
+        first_product(3)
+        wb_raw.append(load_runs(place("wb_stage2", [PACK * N], F32, XN_AT)[:], wb, 2))
+        wb_early = place("wb_early", [6 * PASS], BF16, CAST_AT)
         wb_front = wb_early[:, : 4 * PASS].rearrange("p (a g c j) -> p g a c j", a=2, g=2, j=PACK)
         for g in (1, 0):
             rounded(nc.gpsimd, wb_front[:, g], wb_raw[g][:, :, : 2 * P].rearrange("p j (a c) -> p a c j", c=P), -1.0)
         round_plain(nc.gpsimd, wb_early[:, 4 * PASS :], wb_raw[0][:, :, 2 * P :], -1.0)
         pairs = [place(f"pair{g}", [2, PACK * M1], BF16, (PAIR_AT, RAW_AT)[g]) for g in range(2)]
         pick(1, 2)
-        turned1 = [place(f"turned1{pair}", [2, PASS], BF16, CAST_AT + KB // 2 + 2 * KB * pair) for pair in range(2)]
+        turned1 = [place(f"turned1{pair}", [2, PASS], BF16, CAST_AT - 4 * KB + 2 * KB * pair) for pair in range(2)]
         run_distance(1, 0, 0, turned1)
         evac(8)
         turn_back(first_words(turned_d), pairs[0][:, 0], 2)
         evac(9)
         pick(1, 3)
-        turned_b = place("turned_b", [M_TILES, 2, P, 2], BF16, CAST_AT + 9 * KB // 2)
+        turned_b = place("turned_b", [M_TILES, 2, P, 2], BF16, CAST_AT + 6 * KB)
         turn_first_products(turned_b)
         side = M1 // PACK // SIDE_PIECES
         product(nc.gpsimd, 1, pairs[1][:, 1], [slice(i * side, (i + 1) * side) for i in range(SIDE_PIECES)])
@@ -447,16 +419,17 @@ def tile_list_subtitle_couple_score_kernel(
         picked(2, TAB_AT)
         pick(2, 0)
         pick(2, 1)
-        distance(2, 0, 0, TURN_AT)
+        turned2 = [place(f"turned2{pair}", [2, PASS], BF16, TURN_AT + 7 * KB * pair) for pair in range(2)]
+        run_distance(2, 0, 0, turned2)
         pick(2, 2)
         pick(2, 3)
 
-        wb_low = place("wb_low", [2 * PASS], BF16, CAST_AT + 5 * KB // 2)
+        wb_low = place("wb_low", [2 * PASS], BF16, CAST_AT - 2 * KB)
         round_plain(nc.scalar, wb_low[:], wb_raw[2][:, :, : 2 * P], -1.0)
-        distance(2, 1, 2, TURN_AT + 7 * KB)
+        run_distance(2, 1, 2, turned2)
         dist = place("dist", [PACK * M1], BF16, LAST_AT)
         prod = place("prod", [PACK * M1], BF16, LAST_AT + 5 * KB)
-        turn_back(later_words(2), dist[:], 0)
+        turn_back(run_words(turned2), dist[:], 0)
         y_acc = [bank(f"y_acc{nt}", [M1], F32, (3, 0, 4, 5)[nt]) for nt in range(N_TILES)]
 
         held_at = H_AT + 8 * KB * (H_SLOTS - 1)

@@ -255,7 +255,7 @@ def tile_list_subtitle_couple_score_kernel(
             words = turned[:].rearrange("m mt u p e -> m mt u (p e)").bitcast(F32)
             return lambda mt, u: words[:, mt, u, :]
 
-        xs = {}
+        xs, diffs = {}, {}
 
         def picked(g, at):
             flat = [place(f"x{i + 1}_{g}", [PACK * M1], F32, at + 8 * KB * i) for i in range(2)]
@@ -265,23 +265,30 @@ def tile_list_subtitle_couple_score_kernel(
         def pick(g, t):
             gather(g * PACK + t, xs[g][0][:, t, :], xs[g][1][:, t, :])
 
-        def run_distance(g, u, first_bank, turned):
-            diffs = [bank("diff", [2, 2, P], F32, first_bank + pair) for pair in range(M_TILES // 2)]
-            for e in range(2):
-                for i, x in enumerate(xs[g]):
-                    for pair, diff in enumerate(diffs):
-                        for jj in range(2):
-                            cols = slice((2 * pair + jj) * P, (2 * pair + jj + 1) * P)
-                            nc.tensor.matmul(
-                                diff[:, e, jj, :], lhsT=x[:, 2 * u + e, cols], rhs=identity[:],
-                                is_transpose=True, start=(e, i, jj) == (0, 0, 0), stop=(e, i, jj) == (1, 1, 1),
-                            )
-            for pair, diff in enumerate(diffs):
+        def difference(g, u, e, first_bank):
+            if e == 0:
+                diffs[g, u] = [bank("diff", [2, 2, P], F32, first_bank + pair) for pair in range(M_TILES // 2)]
+            for i, x in enumerate(xs[g]):
+                for pair, diff in enumerate(diffs[g, u]):
+                    for jj in range(2):
+                        cols = slice((2 * pair + jj) * P, (2 * pair + jj + 1) * P)
+                        nc.tensor.matmul(
+                            diff[:, e, jj, :], lhsT=x[:, 2 * u + e, cols], rhs=identity[:],
+                            is_transpose=True, start=(e, i, jj) == (0, 0, 0), stop=(e, i, jj) == (1, 1, 1),
+                        )
+
+        def magnitude(g, u, turned):
+            for pair, diff in enumerate(diffs[g, u]):
                 nc.scalar.activation(
                     turned[pair][:].rearrange("m jj (b u e i) -> m u jj b e i", u=2, e=2, i=RUN)[:, u],
                     diff[:].rearrange("m e jj (b i) -> m jj b e i", i=RUN),
                     ACT.Abs,
                 )
+
+        def run_distance(g, u, first_bank, turned):
+            for e in range(2):
+                difference(g, u, e, first_bank)
+            magnitude(g, u, turned)
 
         def run_words(turned):
             return lambda mt, u: turned[mt // 2][:].bitcast(F32)[:, mt % 2, u : 2 * P : 2]
@@ -303,11 +310,6 @@ def tile_list_subtitle_couple_score_kernel(
                 w1_mx[n + i % tiles, i // tiles] = operand
 
         wb_mx, b_mx, d_mx = {}, {}, {}
-
-        def quantize_pair(g, at):
-            codes, scales = quantize(f"pair{g}", pairs[g][:].rearrange("p s c -> p (s c)"), place(f"pair_codes{g}", [2 * M1], U32, at)[:])[1]
-            d_mx[g] = codes[:, :M1], scales[:, :M1]
-            b_mx[g] = codes[:, M1:], scales[:, M1:]
 
         def b_pass(g, nt, start, stop):
             nc.tensor.matmul_mx(
@@ -394,77 +396,88 @@ def tile_list_subtitle_couple_score_kernel(
         first_prod[3] = place("prod_last", [M1], BF16, CAST_AT - 5 * KB)[:]
         first_product(3)
         wb_raw.append(load_runs(place("wb_stage2", [PACK * N], F32, XN_AT)[:], wb, 2))
-        wb_early = place("wb_early", [6 * PASS], BF16, CAST_AT)
-        wb_front = wb_early[:, : 4 * PASS].rearrange("p (a g c j) -> p g a c j", a=2, g=2, j=PACK)
-        for g in (1, 0):
-            rounded(nc.gpsimd, wb_front[:, g], wb_raw[g][:, :, : 2 * P].rearrange("p j (a c) -> p a c j", c=P), -1.0)
-        round_plain(nc.gpsimd, wb_early[:, 4 * PASS :], wb_raw[0][:, :, 2 * P :], -1.0)
-        pairs = [place(f"pair{g}", [2, PACK * M1], BF16, (PAIR_AT, RAW_AT)[g]) for g in range(2)]
+        wb_low = {1: place("wb_low1", [2 * PASS], BF16, CAST_AT)}
+        round_plain(nc.gpsimd, wb_low[1][:], wb_raw[1][:, :, : 2 * P], -1.0)
+        dists = [place(f"dist{g}", [PACK * M1], BF16, at) for g, at in ((0, PAIR_AT), (1, TURN_AT + 13 * KB))]
         pick(1, 2)
+        turn_back(first_words(turned_d), dists[0][:], 2)
         turned1 = [place(f"turned1{pair}", [2, PASS], BF16, CAST_AT - 4 * KB + 2 * KB * pair) for pair in range(2)]
         run_distance(1, 0, 0, turned1)
         evac(8)
-        turn_back(first_words(turned_d), pairs[0][:, 0], 2)
         evac(9)
         pick(1, 3)
+        d_mx[0] = quantize("d0", dists[0][:])[1]
         turned_b = place("turned_b", [M_TILES, 2, P, 2], BF16, CAST_AT + 6 * KB)
         turn_first_products(turned_b)
+        prods = [place(f"prod{g}", [PACK * M1], BF16, at) for g, at in ((0, PAIR_AT + 4 * KB), (1, PAIR_AT))]
         side = M1 // PACK // SIDE_PIECES
-        product(nc.gpsimd, 1, pairs[1][:, 1], [slice(i * side, (i + 1) * side) for i in range(SIDE_PIECES)])
+        product(nc.gpsimd, 1, prods[1][:], [slice(i * side, (i + 1) * side) for i in range(SIDE_PIECES)])
         evac(10)
-        turn_back(first_words(turned_b), pairs[0][:, 1], 0)
+        turn_back(first_words(turned_b), prods[0][:], 0)
+        evac_half(11, 0)
         run_distance(1, 1, 2, turned1)
-        evac(11)
-        turn_back(run_words(turned1), pairs[1][:, 0], 2)
+        wb_low[0] = place("wb_low0", [2 * PASS], BF16, X_AT)
+        round_plain(nc.gpsimd, wb_low[0][:], wb_raw[0][:, :, : 2 * P], -1.0)
+        evac_half(11, 1)
         picked(2, TAB_AT)
         pick(2, 0)
         pick(2, 1)
         turned2 = [place(f"turned2{pair}", [2, PASS], BF16, TURN_AT + 7 * KB * pair) for pair in range(2)]
         run_distance(2, 0, 0, turned2)
+        turn_back(run_words(turned1), dists[1][:], 2)
+        y_acc = [bank(f"y_acc{nt}", [M1], F32, (2, 3, 6, 7)[nt]) for nt in range(N_TILES)]
+        for nt in (2, 3):
+            d_pass(0, nt, True, False)
         pick(2, 2)
+        difference(2, 1, 0, 4)
+        for nt in (0, 1):
+            d_pass(0, nt, True, False)
         pick(2, 3)
 
-        wb_low = place("wb_low", [2 * PASS], BF16, CAST_AT - 2 * KB)
-        round_plain(nc.scalar, wb_low[:], wb_raw[2][:, :, : 2 * P], -1.0)
-        run_distance(2, 1, 2, turned2)
+        wb_low[2] = place("wb_low2", [2 * PASS], BF16, CAST_AT - 2 * KB)
+        round_plain(nc.scalar, wb_low[2][:], wb_raw[2][:, :, : 2 * P], -1.0)
+        wb_first = place("wb_first", [2 * PASS], BF16, CAST_AT - 4 * KB)
+        round_plain(nc.scalar, wb_first[:], wb_raw[0][:, :, 2 * P :], -1.0)
+        difference(2, 1, 1, 4)
+        magnitude(2, 1, turned2)
+        d_mx[1] = quantize("d1", dists[1][:], place("d1_codes", [M1], U32, H_AT + 8 * KB * (H_SLOTS - 1))[:])[1]
+        for nt in range(N_TILES):
+            d_pass(1, nt, False, False)
         dist = place("dist", [PACK * M1], BF16, LAST_AT)
-        prod = place("prod", [PACK * M1], BF16, LAST_AT + 5 * KB)
+        prod = place("prod", [PACK * M1], BF16, TURN_AT + 15 * KB)
         turn_back(run_words(turned2), dist[:], 0)
-        y_acc = [bank(f"y_acc{nt}", [M1], F32, (3, 0, 4, 5)[nt]) for nt in range(N_TILES)]
+        b_codes = place("b_codes", [M1], U32, TURN_AT + 13 * KB)
+        low_codes = place("low_codes", [6 * P + 2 * M1], U32, TURN_AT)
 
-        held_at = H_AT + 8 * KB * (H_SLOTS - 1)
-        held = place("held", [2 * M1 + 6 * P], U32, held_at)
-        quantize_pair(0, held_at + 7 * KB)
+        def quantize_low(g):
+            wb_mx[g, 0], wb_mx[g, 1] = quantize(f"wb_low{g}", wb_low[g][:], low_codes[:, 2 * P * g : 2 * P * (g + 1)])[0]
+
         quads = M1 // PACK // 2
         product(nc.vector, 2, prod[:], [slice(0, quads)])
-        d_mx[1] = quantize("d1", pairs[1][:, 0], held[:, :M1])[1]
+        b_mx[0] = quantize("b0", prods[0][:], b_codes[:, :M1])[1]
         product(nc.vector, 2, prod[:], [slice(quads, 2 * quads)])
-        wb_mx[0, 0], wb_mx[1, 0], wb_mx[0, 1], wb_mx[1, 1] = quantize(
-            "wb_a", wb_early[:, : 4 * PASS], held[:, 2 * M1 : 2 * M1 + 4 * P]
-        )[0]
-        b_mx[1] = quantize("b1", pairs[1][:, 1], held[:, M1 : 2 * M1])[1]
-        wb_mx[2, 0], wb_mx[2, 1] = quantize("wb_b", wb_low[:], held[:, 2 * M1 + 4 * P :])[0]
-        b_mx[2] = quantize("b2", prod[:])[1]
+        quantize_low(0)
+        b_mx[1] = quantize("b1", prods[1][:], low_codes[:, 6 * P : 6 * P + M1])[1]
+        quantize_low(1)
+        quantize_low(2)
+        b_mx[2] = quantize("b2", prod[:], low_codes[:, 6 * P + M1 :])[1]
         d_mx[2] = quantize("d2", dist[:])[1]
         for g in range(2):
             for nt in range(2):
-                d_pass(g, nt, g == 0, False)
-        for g in range(H_PASSES):
-            for nt in range(2):
                 b_pass(g, nt, False, False)
         for nt in range(2):
+            b_pass(2, nt, False, False)
             d_pass(2, nt, False, True)
         wb_high = place("wb_high", [2, 2 * PASS], BF16, TURN_AT + 17 * KB // 2)
         for g in (1, 2):
             round_plain(nc.scalar, wb_high[:, g - 1], wb_raw[g][:, :, 2 * P :], -1.0)
         late = place("late", [6 * P], U32, LAST_AT)
-        wb_mx[0, 2], wb_mx[0, 3] = quantize("wb_e", wb_early[:, 4 * PASS :], late[:, : 2 * P])[0]
+        wb_mx[0, 2], wb_mx[0, 3] = quantize("wb_first", wb_first[:], late[:, : 2 * P])[0]
         wb_mx[1, 2], wb_mx[1, 3], wb_mx[2, 2], wb_mx[2, 3] = quantize(
-            "wb_f", wb_high[:].rearrange("p g c -> p (g c)"), late[:, 2 * P :]
+            "wb_high", wb_high[:].rearrange("p g c -> p (g c)"), late[:, 2 * P :]
         )[0]
         for nt in range(2, N_TILES):
-            for g in reversed(range(H_PASSES)):
-                d_pass(g, nt, g == H_PASSES - 1, False)
+            d_pass(2, nt, False, False)
             for g in range(H_PASSES):
                 b_pass(g, nt, False, g == H_PASSES - 1)
 

@@ -137,12 +137,12 @@ def tile_list_subtitle_couple_score_kernel(
         raw[0, 0] = load_rows(h_tiles[0][:, S : S + PASS], w1, 0, 0)
         raw[0, 1] = load_rows(h_tiles[0][:, S + PASS :], w1, 1, 0)
         tab_sb.append(load_table(1))
-        raw[1, 0] = load_rows(h_tiles[1][:, S + PASS :], w1, 0, P)
-        raw[1, 1] = load_rows(h_tiles[0][:, BANK // 2 : BANK // 2 + PASS], w1, 1, P)
+        raw[1, 0] = load_rows(place("stage0", [PASS], F32, PAIR_AT + 2 * KB)[:], w1, 0, P)
+        raw[1, 1] = load_rows(place("stage1", [PASS], F32, PAIR_AT)[:], w1, 1, P)
         pos1_sb = load_list(pos1, "pos1_sb")
         pos2_sb = load_list(pos2, "pos2_sb")
         raw[2, 0] = load_rows(h_tiles[2][:, S:], w1, 0, 2 * P)
-        raw[2, 1] = load_rows(h_tiles[1][:, BANK : BANK + S], w1, 1, 2 * P)
+        raw[2, 1] = load_rows(h_tiles[1][:, S:], w1, 1, 2 * P)
         raw[4, 0] = load_rows(place("stage4", [PACK * PASS], F32, RAW_AT)[:], w1, 0, PASS)
         raw[4, 1] = load_rows(place("stage5", [PACK * PASS], F32, RAW_AT + 8 * KB)[:], w1, 1, PASS)
         raw[8, 0] = load_rows(place("stage8", [PACK * PASS], F32, CAST_AT - 16 * KB)[:], w1, 0, 2 * PASS)
@@ -158,24 +158,17 @@ def tile_list_subtitle_couple_score_kernel(
         for a in range(K_PASSES):
             round_plain(nc.scalar, cast0[:, a], raw[0, a])
         w1_mx[0, 0], w1_mx[0, 1] = quantize("w0", cast0[:].rearrange("p a c -> p (a c)"))[0]
-        for half in range(2):
-            entries = slice(half * BANK // 16, (half + 1) * BANK // 16)
-            nc.vector.tensor_copy(
-                v_codes[1][:, half * BANK : (half + 1) * BANK], tab_sb[1][:].bitcast(U32).indirect(offs_sb[:, entries])
-            )
+        pieces = [slice(0, BANK), slice(BANK, BANK + BANK // 2), slice(BANK + BANK // 2, S)]
+        for c in pieces:
+            nc.vector.tensor_copy(v_codes[1][:, c], tab_sb[1][:].bitcast(U32).indirect(offs_sb[:, c.start // 16 : c.stop // 16]))
         cast1 = place("cast1", [K_PASSES, PASS], BF16, CAST_AT + 15 * KB)[:]
-        for a in range(K_PASSES):
-            round_plain(nc.scalar, cast1[:, a], raw[1, a])
+        for a, engine in enumerate((nc.scalar, nc.gpsimd)):
+            round_plain(engine, cast1[:, a], raw[1, a])
         w1_mx[1, 0], w1_mx[1, 1] = quantize("w1", cast1.rearrange("p a c -> p (a c)"))[0]
 
-        accs = {}
-
-        def h_pass(n, half, a, start, stop):
-            if start:
-                accs[n, half] = bank("acc", [BANK], F32, ((0, 2, 0, 4, 2)[n] if n <= PACK else 4 + 2 * (n % 2)) + half)
-            cols = slice(half * BANK, (half + 1) * BANK)
+        def h_pass(n, acc, cols, a, start, stop):
             nc.tensor.matmul_mx(
-                out=accs[n, half][:],
+                out=acc[:],
                 lhsT=w1_mx[n, a][0].bitcast(FP8X4),
                 lhsT_scale=w1_mx[n, a][1],
                 rhs=v_codes[a][:, cols].bitcast(FP8X4),
@@ -185,9 +178,11 @@ def tile_list_subtitle_couple_score_kernel(
             )
 
         def evac_half(n, half):
+            acc = bank("acc", [BANK], F32, ((0, 2, 0, 4, 2)[n] if n <= PACK else 4 + 2 * (n % 2)) + half)
+            cols = slice(half * BANK, (half + 1) * BANK)
             for a in reversed(range(K_PASSES)):
-                h_pass(n, half, a, a == K_PASSES - 1, a == 0)
-            nc.scalar.copy(h_tiles[n % H_SLOTS][:, half * BANK : (half + 1) * BANK], accs[n, half][:])
+                h_pass(n, acc, cols, a, a == K_PASSES - 1, a == 0)
+            nc.scalar.copy(h_tiles[n % H_SLOTS][:, cols], acc[:])
 
         def evac(n):
             evac_half(n, 0)
@@ -200,8 +195,8 @@ def tile_list_subtitle_couple_score_kernel(
                 between()
             nc.vector.tensor_scalar(x2, h[:].indirect(pos2_sb[:]), -1.0, 0.0, ALU.mult, ALU.add)
 
-        x1_at = [XN_AT, XN_AT + 10 * KB, XN_AT + 2 * KB, CAST_AT + 33 * KB // 2]
-        x2_at = [CAST_AT + 14 * KB, XN_AT + 6 * KB, XN_AT + 8 * KB, CAST_AT - 7 * KB]
+        x1_at = [XN_AT, CAST_AT + 25 * KB // 2, XN_AT + 2 * KB, CAST_AT + 33 * KB // 2]
+        x2_at = [XN_AT + 10 * KB, CAST_AT + 29 * KB // 2, XN_AT + 8 * KB, CAST_AT - 7 * KB]
         first_x, first_diff, first_prod = {}, {}, {}
 
         def pick_first(j, between=None):
@@ -333,21 +328,21 @@ def tile_list_subtitle_couple_score_kernel(
                 stop=stop,
             )
 
-        for half in range(2):
-            h_pass(0, half, 0, True, False)
-        h_pass(0, 0, 1, False, True)
-        nc.scalar.copy(h_tiles[0][:, :BANK], accs[0, 0][:])
-        h_pass(0, 1, 1, False, True)
-        nc.scalar.copy(h_tiles[0][:, BANK:S], accs[0, 1][:])
-        casts = [place(f"cast{n}", [K_PASSES, PASS], BF16, at) for n, at in ((2, x2_at[0]), (3, CAST_AT + 16 * KB))]
+        accs = [bank("acc", [c.stop - c.start], F32, number) for c, number in zip(pieces, (0, 1, 6))]
+        for c, acc in zip(pieces, accs):
+            h_pass(0, acc, c, 0, True, False)
+        for c, acc in zip(pieces, accs):
+            h_pass(0, acc, c, 1, False, True)
+            nc.scalar.copy(h_tiles[0][:, c], acc[:])
+        casts = [place(f"cast{n}", [K_PASSES, PASS], BF16, at) for n, at in ((2, CAST_AT + 27 * KB // 2), (3, CAST_AT + 16 * KB))]
         for i, cast in enumerate(casts):
             round_plain(nc.gpsimd, cast[:, 0], raw[2, 0][:, :, i * P : (i + 1) * P])
-        evac_half(1, 0)
+        evac(1)
         for i, cast in enumerate(casts):
             round_plain(nc.scalar, cast[:, 1], raw[2, 1][:, :, i * P : (i + 1) * P])
-        evac_half(1, 1)
-        pick_first(0, lambda: quantize_w1(2, 1, casts[0][:].rearrange("p a (t m j) -> p a t m j", t=1, j=PACK)))
-        w1_mx[3, 0], w1_mx[3, 1] = quantize("w3", casts[1][:].rearrange("p a c -> p (a c)"))[0]
+        pick_first(0)
+        for n, cast in zip((2, 3), casts):
+            w1_mx[n, 0], w1_mx[n, 1] = quantize(f"w{n}", cast[:].rearrange("p a c -> p (a c)"))[0]
         evac(2)
         pick_first(1)
         cast4 = place("cast4", [K_PASSES, 2, P, PACK], BF16, CAST_AT + 33 * KB // 2)
@@ -396,9 +391,10 @@ def tile_list_subtitle_couple_score_kernel(
         first_prod[3] = place("prod_last", [M1], BF16, CAST_AT - 5 * KB)[:]
         first_product(3)
         wb_raw.append(load_runs(place("wb_stage2", [PACK * N], F32, XN_AT)[:], wb, 2))
-        wb_low = {1: place("wb_low1", [2 * PASS], BF16, CAST_AT)}
-        round_plain(nc.gpsimd, wb_low[1][:], wb_raw[1][:, :, : 2 * P], -1.0)
-        dists = [place(f"dist{g}", [PACK * M1], BF16, at) for g, at in ((0, PAIR_AT), (1, TURN_AT + 13 * KB))]
+        wb_front = place("wb_front", [2, 2, P, PACK], BF16, CAST_AT)
+        for g in (1, 0):
+            rounded(nc.gpsimd, wb_front[:, :, g], wb_raw[g][:, :, : 2 * P].rearrange("p j (a c) -> p a c j", c=P), -1.0)
+        dists = [place(f"dist{g}", [PACK * M1], BF16, at) for g, at in ((0, PAIR_AT), (1, TURN_AT + 15 * KB))]
         pick(1, 2)
         turn_back(first_words(turned_d), dists[0][:], 2)
         turned1 = [place(f"turned1{pair}", [2, PASS], BF16, CAST_AT - 4 * KB + 2 * KB * pair) for pair in range(2)]
@@ -416,65 +412,65 @@ def tile_list_subtitle_couple_score_kernel(
         turn_back(first_words(turned_b), prods[0][:], 0)
         evac_half(11, 0)
         run_distance(1, 1, 2, turned1)
-        wb_low[0] = place("wb_low0", [2 * PASS], BF16, X_AT)
-        round_plain(nc.gpsimd, wb_low[0][:], wb_raw[0][:, :, : 2 * P], -1.0)
+        wb_first = place("wb_first", [2 * PASS], BF16, X_AT)
+        round_plain(nc.gpsimd, wb_first[:], wb_raw[0][:, :, 2 * P :], -1.0)
         evac_half(11, 1)
         picked(2, TAB_AT)
         pick(2, 0)
         pick(2, 1)
         turned2 = [place(f"turned2{pair}", [2, PASS], BF16, TURN_AT + 7 * KB * pair) for pair in range(2)]
         run_distance(2, 0, 0, turned2)
-        turn_back(run_words(turned1), dists[1][:], 2)
-        y_acc = [bank(f"y_acc{nt}", [M1], F32, (2, 3, 6, 7)[nt]) for nt in range(N_TILES)]
+        y_acc = {nt: bank(f"y_acc{nt}", [M1], F32, 4 + nt) for nt in (2, 3)}
         for nt in (2, 3):
             d_pass(0, nt, True, False)
+        turn_back(run_words(turned1), dists[1][:], 2)
         pick(2, 2)
         difference(2, 1, 0, 4)
         for nt in (0, 1):
+            y_acc[nt] = bank(f"y_acc{nt}", [M1], F32, 2 + nt)
             d_pass(0, nt, True, False)
         pick(2, 3)
 
-        wb_low[2] = place("wb_low2", [2 * PASS], BF16, CAST_AT - 2 * KB)
-        round_plain(nc.scalar, wb_low[2][:], wb_raw[2][:, :, : 2 * P], -1.0)
-        wb_first = place("wb_first", [2 * PASS], BF16, CAST_AT - 4 * KB)
-        round_plain(nc.scalar, wb_first[:], wb_raw[0][:, :, 2 * P :], -1.0)
+        wb_low = place("wb_low", [2, PASS], BF16, CAST_AT - 2 * KB)
+        round_plain(nc.scalar, wb_low[:].rearrange("p a c -> p (a c)"), wb_raw[2][:, :, : 2 * P], -1.0)
         difference(2, 1, 1, 4)
         magnitude(2, 1, turned2)
         d_mx[1] = quantize("d1", dists[1][:], place("d1_codes", [M1], U32, H_AT + 8 * KB * (H_SLOTS - 1))[:])[1]
         for nt in range(N_TILES):
             d_pass(1, nt, False, False)
         dist = place("dist", [PACK * M1], BF16, LAST_AT)
-        prod = place("prod", [PACK * M1], BF16, TURN_AT + 15 * KB)
+        prod = place("prod", [PACK * M1], BF16, TURN_AT + 17 * KB)
         turn_back(run_words(turned2), dist[:], 0)
-        b_codes = place("b_codes", [M1], U32, TURN_AT + 13 * KB)
-        low_codes = place("low_codes", [6 * P + 2 * M1], U32, TURN_AT)
+        b_codes = place("b_codes", [2 * M1], U32, TURN_AT + 13 * KB)
+        low_codes = place("low_codes", [3 * P + M1], U32, TURN_AT)
 
-        def quantize_low(g):
-            wb_mx[g, 0], wb_mx[g, 1] = quantize(f"wb_low{g}", wb_low[g][:], low_codes[:, 2 * P * g : 2 * P * (g + 1)])[0]
+        def quantize_low(nt, codes):
+            front = wb_front[:, nt].rearrange("p g c j -> p (g c j)")
+            wb_mx[0, nt], wb_mx[1, nt] = quantize(f"wb_front{nt}", front, codes[:, : 2 * P])[0]
+            wb_mx[2, nt] = quantize(f"wb_low{nt}", wb_low[:, nt], codes[:, 2 * P : 3 * P])[0][0]
 
         quads = M1 // PACK // 2
         product(nc.vector, 2, prod[:], [slice(0, quads)])
         b_mx[0] = quantize("b0", prods[0][:], b_codes[:, :M1])[1]
         product(nc.vector, 2, prod[:], [slice(quads, 2 * quads)])
-        quantize_low(0)
-        b_mx[1] = quantize("b1", prods[1][:], low_codes[:, 6 * P : 6 * P + M1])[1]
-        quantize_low(1)
-        quantize_low(2)
-        b_mx[2] = quantize("b2", prod[:], low_codes[:, 6 * P + M1 :])[1]
+        b_mx[1] = quantize("b1", prods[1][:], b_codes[:, M1:])[1]
+        quantize_low(0, low_codes)
+        b_mx[2] = quantize("b2", prod[:], low_codes[:, 3 * P : 3 * P + M1])[1]
         d_mx[2] = quantize("d2", dist[:])[1]
-        for g in range(2):
-            for nt in range(2):
-                b_pass(g, nt, False, False)
-        for nt in range(2):
-            b_pass(2, nt, False, False)
-            d_pass(2, nt, False, True)
+        for g in range(H_PASSES):
+            b_pass(g, 0, False, False)
+        d_pass(2, 0, False, True)
+        late = place("late", [9 * P], U32, LAST_AT)
+        quantize_low(1, late)
+        d_pass(2, 1, False, False)
+        for g in range(H_PASSES):
+            b_pass(g, 1, False, g == H_PASSES - 1)
         wb_high = place("wb_high", [2, 2 * PASS], BF16, TURN_AT + 17 * KB // 2)
         for g in (1, 2):
             round_plain(nc.scalar, wb_high[:, g - 1], wb_raw[g][:, :, 2 * P :], -1.0)
-        late = place("late", [6 * P], U32, LAST_AT)
-        wb_mx[0, 2], wb_mx[0, 3] = quantize("wb_first", wb_first[:], late[:, : 2 * P])[0]
+        wb_mx[0, 2], wb_mx[0, 3] = quantize("wb_first", wb_first[:], late[:, 3 * P : 5 * P])[0]
         wb_mx[1, 2], wb_mx[1, 3], wb_mx[2, 2], wb_mx[2, 3] = quantize(
-            "wb_high", wb_high[:].rearrange("p g c -> p (g c)"), late[:, 2 * P :]
+            "wb_high", wb_high[:].rearrange("p g c -> p (g c)"), late[:, 5 * P :]
         )[0]
         for nt in range(2, N_TILES):
             d_pass(2, nt, False, False)

@@ -420,14 +420,11 @@ def tile_list_subtitle_couple_score_kernel(
         pick(2, 1)
         turned2 = [place(f"turned2{pair}", [2, PASS], BF16, TURN_AT + 7 * KB * pair) for pair in range(2)]
         run_distance(2, 0, 0, turned2)
-        y_acc = {nt: bank(f"y_acc{nt}", [M1], F32, 4 + nt) for nt in (2, 3)}
-        for nt in (2, 3):
-            d_pass(0, nt, True, False)
         turn_back(run_words(turned1), dists[1][:], 2)
         pick(2, 2)
         difference(2, 1, 0, 4)
-        for nt in (0, 1):
-            y_acc[nt] = bank(f"y_acc{nt}", [M1], F32, 2 + nt)
+        y_acc = {nt: bank(f"y_acc{nt}", [M1], F32, nt) for nt in (2, 3)}
+        for nt in (2, 3):
             d_pass(0, nt, True, False)
         pick(2, 3)
 
@@ -436,11 +433,15 @@ def tile_list_subtitle_couple_score_kernel(
         difference(2, 1, 1, 4)
         magnitude(2, 1, turned2)
         d_mx[1] = quantize("d1", dists[1][:], place("d1_codes", [M1], U32, H_AT + 8 * KB * (H_SLOTS - 1))[:])[1]
-        for nt in range(N_TILES):
+        for nt in (2, 3):
             d_pass(1, nt, False, False)
         dist = place("dist", [PACK * M1], BF16, LAST_AT)
         prod = place("prod", [PACK * M1], BF16, TURN_AT + 17 * KB)
         turn_back(run_words(turned2), dist[:], 0)
+        for nt in (0, 1):
+            y_acc[nt] = bank(f"y_acc{nt}", [M1], F32, 4 + nt)
+            for g in range(2):
+                d_pass(g, nt, g == 0, False)
         b_codes = place("b_codes", [2 * M1], U32, TURN_AT + 13 * KB)
         low_codes = place("low_codes", [3 * P + M1], U32, TURN_AT)
 

@@ -412,7 +412,7 @@ def tile_list_subtitle_couple_score_kernel(
         turn_back(first_words(turned_b), prods[0][:], 0)
         evac_half(11, 0)
         run_distance(1, 1, 2, turned1)
-        wb_first = place("wb_first", [2 * PASS], BF16, X_AT)
+        wb_first = place("wb_first", [2 * PASS], BF16, X_AT + 6 * KB)
         round_plain(nc.gpsimd, wb_first[:], wb_raw[0][:, :, 2 * P :], -1.0)
         evac_half(11, 1)
         picked(2, TAB_AT)
@@ -430,9 +430,11 @@ def tile_list_subtitle_couple_score_kernel(
 
         wb_low = place("wb_low", [2, PASS], BF16, CAST_AT - 2 * KB)
         round_plain(nc.scalar, wb_low[:].rearrange("p a c -> p (a c)"), wb_raw[2][:, :, : 2 * P], -1.0)
+        wb_second = place("wb_second", [2 * PASS], BF16, CAST_AT - 4 * KB)
+        round_plain(nc.scalar, wb_second[:], wb_raw[1][:, :, 2 * P :], -1.0)
         difference(2, 1, 1, 4)
         magnitude(2, 1, turned2)
-        d_mx[1] = quantize("d1", dists[1][:], place("d1_codes", [M1], U32, H_AT + 8 * KB * (H_SLOTS - 1))[:])[1]
+        d_mx[1] = quantize("d1", dists[1][:], place("d1_codes", [M1], U32, H_AT + 8 * KB * (H_SLOTS - 2))[:])[1]
         for nt in (2, 3):
             d_pass(1, nt, False, False)
         dist = place("dist", [PACK * M1], BF16, LAST_AT)
@@ -466,13 +468,10 @@ def tile_list_subtitle_couple_score_kernel(
         d_pass(2, 1, False, False)
         for g in range(H_PASSES):
             b_pass(g, 1, False, g == H_PASSES - 1)
-        wb_high = place("wb_high", [2, 2 * PASS], BF16, TURN_AT + 17 * KB // 2)
-        for g in (1, 2):
-            round_plain(nc.scalar, wb_high[:, g - 1], wb_raw[g][:, :, 2 * P :], -1.0)
-        wb_mx[0, 2], wb_mx[0, 3] = quantize("wb_first", wb_first[:], late[:, 3 * P : 5 * P])[0]
-        wb_mx[1, 2], wb_mx[1, 3], wb_mx[2, 2], wb_mx[2, 3] = quantize(
-            "wb_high", wb_high[:].rearrange("p g c -> p (g c)"), late[:, 5 * P :]
-        )[0]
+        wb_last = place("wb_last", [2 * PASS], BF16, TURN_AT + 17 * KB // 2)
+        round_plain(nc.scalar, wb_last[:], wb_raw[2][:, :, 2 * P :], -1.0)
+        for g, cast in enumerate((wb_first, wb_second, wb_last)):
+            wb_mx[g, 2], wb_mx[g, 3] = quantize(f"wb_high{g}", cast[:], late[:, (3 + 2 * g) * P : (5 + 2 * g) * P])[0]
         for nt in range(2, N_TILES):
             d_pass(2, nt, False, False)
             for g in range(H_PASSES):

@@ -26,7 +26,7 @@ H_PASSES = H // PASS
 N_TILES = N // P
 M_TILES = M1 // P
 H_SLOTS = 4
-SIDE_PIECES = 4
+SIDE_PIECES = 2
 RUN = 8
 KB = 1024
 
@@ -40,6 +40,7 @@ CAST_AT = 119 * KB
 PAIR_AT = 140 * KB
 LAST_AT = 148 * KB
 TURN_AT = 157 * KB
+HEAD_AT = 180 * KB
 
 
 def tile_list_subtitle_couple_score_kernel(
@@ -77,13 +78,14 @@ def tile_list_subtitle_couple_score_kernel(
                 nc.sync.dma_start(out=rows[:, t], in_=runs[t])
             return rows
 
-        def quantize(name, grouped, codes=None):
+        def quantize(name, grouped, codes=None, scales=None):
             width = grouped.shape[1] // PACK
             if codes is None:
                 codes = keep.tile([P, width], U32, name=name + "_codes", align_bytes=64)[:]
-            scales = keep.tile([P, width], U8, name=name + "_scales", align_bytes=64)
-            nc.vector.quantize_mx(out=codes.bitcast(FP8X4), scales=scales[:], in_=grouped)
-            return [(codes[:, c : c + P], scales[:, c : c + P]) for c in range(0, width, P)], (codes, scales[:])
+            if scales is None:
+                scales = keep.tile([P, width], U8, name=name + "_scales", align_bytes=64)[:]
+            nc.vector.quantize_mx(out=codes.bitcast(FP8X4), scales=scales, in_=grouped)
+            return [(codes[:, c : c + P], scales[:, c : c + P]) for c in range(0, width, P)], (codes, scales)
 
         def rounded(engine, dst, src, sign):
             if engine is nc.scalar:
@@ -280,6 +282,32 @@ def tile_list_subtitle_couple_score_kernel(
                     ACT.Abs,
                 )
 
+        def lone_difference(t, number):
+            diffs[t] = bank("diff", [M_TILES, P], F32, number)
+            for i, x in enumerate(xs[2]):
+                for mt in range(M_TILES):
+                    nc.tensor.matmul(
+                        diffs[t][:, mt, :], lhsT=x[:, t, mt * P : (mt + 1) * P], rhs=identity[:],
+                        is_transpose=True, start=(i, mt) == (0, 0), stop=(i, mt) == (1, M_TILES - 1),
+                    )
+
+        def lone_magnitude(t, turned):
+            for pair in range(M_TILES // 2):
+                nc.scalar.activation(
+                    turned[pair][:].rearrange("m jj (b t i) -> m t jj b i", t=PACK, i=RUN)[:, t],
+                    diffs[t][:, 2 * pair : 2 * pair + 2].rearrange("m jj (b i) -> m jj b i", i=RUN),
+                    ACT.Abs,
+                )
+
+        def turn_back_half(words, dist, pair, number):
+            back = bank("back", [2, 2, P], F32, number)
+            for jj in range(2):
+                for u in range(2):
+                    nc.tensor.transpose(back[:, jj, u, :], words(2 * pair + jj, u), identity[:])
+            nc.scalar.copy(
+                dist.bitcast(F32).rearrange("p (jj m u) -> p jj m u", jj=2, u=2), back[:].rearrange("p jj u m -> p jj m u")
+            )
+
         def run_distance(g, u, first_bank, turned):
             for e in range(2):
                 difference(g, u, e, first_bank)
@@ -317,13 +345,13 @@ def tile_list_subtitle_couple_score_kernel(
                 stop=stop,
             )
 
-        def d_pass(g, nt, start, stop):
+        def d_pass(g, nt, start, stop, cols=slice(0, M1)):
             nc.tensor.matmul_mx(
-                out=y_acc[nt][:],
+                out=y_acc[nt][:, cols],
                 lhsT=wd_sb[:, g, 2 * nt * P : 2 * (nt + 1) * P].bitcast(FP4X4),
                 lhsT_scale=wd_planes[:, g, nt * P : (nt + 1) * P],
-                rhs=d_mx[g][0].bitcast(FP8X4),
-                rhs_scale=d_mx[g][1],
+                rhs=d_mx[g][0][:, cols].bitcast(FP8X4),
+                rhs_scale=d_mx[g][1][:, cols],
                 start=start,
                 stop=stop,
             )
@@ -394,7 +422,7 @@ def tile_list_subtitle_couple_score_kernel(
         wb_front = place("wb_front", [2, 2, P, PACK], BF16, CAST_AT)
         for g in (1, 0):
             rounded(nc.gpsimd, wb_front[:, :, g], wb_raw[g][:, :, : 2 * P].rearrange("p j (a c) -> p a c j", c=P), -1.0)
-        dists = [place(f"dist{g}", [PACK * M1], BF16, at) for g, at in ((0, PAIR_AT), (1, TURN_AT + 15 * KB))]
+        dists = [place("dist0", [PACK * M1], BF16, PAIR_AT)]
         pick(1, 2)
         turn_back(first_words(turned_d), dists[0][:], 2)
         turned1 = [place(f"turned1{pair}", [2, PASS], BF16, CAST_AT - 4 * KB + 2 * KB * pair) for pair in range(2)]
@@ -420,9 +448,11 @@ def tile_list_subtitle_couple_score_kernel(
         pick(2, 1)
         turned2 = [place(f"turned2{pair}", [2, PASS], BF16, TURN_AT + 7 * KB * pair) for pair in range(2)]
         run_distance(2, 0, 0, turned2)
-        turn_back(run_words(turned1), dists[1][:], 2)
+        dist1 = [place(f"dist1{pair}", [S], BF16, TURN_AT + (17 - 2 * pair) * KB) for pair in range(2)]
+        for pair in range(2):
+            turn_back_half(run_words(turned1), dist1[pair][:], pair, 2 + pair)
         pick(2, 2)
-        difference(2, 1, 0, 4)
+        lone_difference(2, 4)
         y_acc = {nt: bank(f"y_acc{nt}", [M1], F32, nt) for nt in (2, 3)}
         for nt in (2, 3):
             d_pass(0, nt, True, False)
@@ -430,16 +460,25 @@ def tile_list_subtitle_couple_score_kernel(
 
         wb_low = place("wb_low", [2, PASS], BF16, CAST_AT - 2 * KB)
         round_plain(nc.scalar, wb_low[:].rearrange("p a c -> p (a c)"), wb_raw[2][:, :, : 2 * P], -1.0)
+        lone_magnitude(2, turned2)
         wb_second = place("wb_second", [2 * PASS], BF16, CAST_AT - 4 * KB)
         round_plain(nc.scalar, wb_second[:], wb_raw[1][:, :, 2 * P :], -1.0)
-        difference(2, 1, 1, 4)
-        magnitude(2, 1, turned2)
-        d_mx[1] = quantize("d1", dists[1][:], place("d1_codes", [M1], U32, H_AT + 8 * KB * (H_SLOTS - 2))[:])[1]
+        lone_difference(3, 5)
+        lone_magnitude(3, turned2)
+        couples = [slice(0, M1 // 2), slice(M1 // 2, M1)]
+
+        def quantize_halves(g, halves, codes):
+            d_mx[g] = codes, keep.tile([P, M1], U8, name=f"d{g}_scales", align_bytes=64)[:]
+            for c, half in zip(couples, halves):
+                quantize(f"d{g}", half[:], d_mx[g][0][:, c], d_mx[g][1][:, c])
+
+        quantize_halves(1, dist1, place("d1_codes", [M1], U32, H_AT + 8 * KB * (H_SLOTS - 2))[:])
         for nt in (2, 3):
             d_pass(1, nt, False, False)
-        dist = place("dist", [PACK * M1], BF16, LAST_AT)
+        dist = [place(f"dist2{pair}", [S], BF16, LAST_AT + 3 * KB * pair) for pair in range(2)]
         prod = place("prod", [PACK * M1], BF16, TURN_AT + 17 * KB)
-        turn_back(run_words(turned2), dist[:], 0)
+        for pair in range(2):
+            turn_back_half(run_words(turned2), dist[pair][:], pair, pair)
         for nt in (0, 1):
             y_acc[nt] = bank(f"y_acc{nt}", [M1], F32, 4 + nt)
             for g in range(2):
@@ -459,11 +498,12 @@ def tile_list_subtitle_couple_score_kernel(
         b_mx[1] = quantize("b1", prods[1][:], b_codes[:, M1:])[1]
         quantize_low(0, low_codes)
         b_mx[2] = quantize("b2", prod[:], low_codes[:, 3 * P : 3 * P + M1])[1]
-        d_mx[2] = quantize("d2", dist[:])[1]
+        quantize_halves(2, dist, keep.tile([P, M1], U32, name="d2_codes", align_bytes=64)[:])
         for g in range(H_PASSES):
             b_pass(g, 0, False, False)
-        d_pass(2, 0, False, True)
-        late = place("late", [9 * P], U32, LAST_AT)
+        for c in couples:
+            d_pass(2, 0, False, c == couples[-1], c)
+        late = place("late", [9 * P], U32, LAST_AT - 5 * KB // 2)
         quantize_low(1, late)
         d_pass(2, 1, False, False)
         for g in range(H_PASSES):
@@ -482,7 +522,7 @@ def tile_list_subtitle_couple_score_kernel(
             nc.scalar.copy(ys[nt][:], y_acc[nt][:])
         first = place("first", [N_TILES, M2], F32, X_AT + 8 * KB)
         other = place("other", [N_TILES, M2], F32, X_AT + 12 * KB)
-        top = place("top", [N_TILES, M2], F32, TAB_AT)
+        top = place("top", [N_TILES, M2], F32, LAST_AT - 6 * KB)
         squared = place("squared", [N_TILES, M2], F32, LAST_AT)
         score = place("score", [N_TILES, M2], F32, TAB_AT + 4 * KB)
 
@@ -493,8 +533,10 @@ def tile_list_subtitle_couple_score_kernel(
         def larger(tiles, c):
             nc.vector.tensor_tensor(top[:, tiles, c], first[:, tiles, c], other[:, tiles, c], ALU.max)
 
-        def finish(tiles, c):
+        def square(tiles, c):
             nc.scalar.activation(squared[:, tiles, c], top[:, tiles, c], ACT.Square)
+
+        def add_one(tiles, c):
             nc.scalar.activation(score[:, tiles, c], squared[:, tiles, c], ACT.Copy, bias=1.0)
 
         def store(tiles):
@@ -504,23 +546,22 @@ def tile_list_subtitle_couple_score_kernel(
 
         last = N_TILES - 1
         whole, low, high = slice(0, M2), slice(0, M2 // 2), slice(M2 // 2, M2)
-        for nt in range(2):
+        for nt in range(last):
             pick_y(nt, whole, first, pos3_sb)
             pick_y(nt, whole, other, pos4_sb)
-        pick_y(2, whole, first, pos3_sb)
-        larger(slice(0, 2), whole)
-        finish(slice(0, 2), whole)
-        store(slice(0, 2))
-        pick_y(2, whole, other, pos4_sb)
+        for tiles in (slice(0, 2), slice(2, 3)):
+            larger(tiles, whole)
+            square(tiles, whole)
+        for tiles in (slice(0, 2), slice(2, 3)):
+            add_one(tiles, whole)
+            store(tiles)
         pick_y(last, whole, first, pos3_sb)
-        larger(slice(2, 3), whole)
-        finish(slice(2, 3), whole)
-        store(slice(2, 3))
         pick_y(last, low, other, pos4_sb)
         pick_y(last, high, other, pos4_sb)
         larger(last, low)
         larger(last, high)
-        finish(last, low)
+        square(last, low)
+        add_one(last, low)
         nc.vector.tensor_tensor(squared[:, last, high], top[:, last, high], top[:, last, high], ALU.mult)
         nc.vector.tensor_scalar(score[:, last, high], squared[:, last, high], 1.0, None, ALU.add)
         store(slice(last, N_TILES))

@@ -282,20 +282,20 @@ def tile_list_subtitle_couple_score_kernel(
                     ACT.Abs,
                 )
 
-        def lone_difference(t, number):
-            diffs[t] = bank("diff", [M_TILES, P], F32, number)
+        def lone_difference(t, first_bank):
+            diffs[t] = [bank("diff", [2, P], F32, first_bank + pair) for pair in range(M_TILES // 2)]
             for i, x in enumerate(xs[2]):
                 for mt in range(M_TILES):
                     nc.tensor.matmul(
-                        diffs[t][:, mt, :], lhsT=x[:, t, mt * P : (mt + 1) * P], rhs=identity[:],
-                        is_transpose=True, start=(i, mt) == (0, 0), stop=(i, mt) == (1, M_TILES - 1),
+                        diffs[t][mt // 2][:, mt % 2, :], lhsT=x[:, t, mt * P : (mt + 1) * P], rhs=identity[:],
+                        is_transpose=True, start=(i, mt % 2) == (0, 0), stop=(i, mt % 2) == (1, 1),
                     )
 
         def lone_magnitude(t, turned):
-            for pair in range(M_TILES // 2):
+            for pair, diff in enumerate(diffs[t]):
                 nc.scalar.activation(
                     turned[pair][:].rearrange("m jj (b t i) -> m t jj b i", t=PACK, i=RUN)[:, t],
-                    diffs[t][:, 2 * pair : 2 * pair + 2].rearrange("m jj (b i) -> m jj b i", i=RUN),
+                    diff[:].rearrange("m jj (b i) -> m jj b i", i=RUN),
                     ACT.Abs,
                 )
 
@@ -452,7 +452,7 @@ def tile_list_subtitle_couple_score_kernel(
         for pair in range(2):
             turn_back_half(run_words(turned1), dist1[pair][:], pair, 2 + pair)
         pick(2, 2)
-        lone_difference(2, 4)
+        lone_difference(2, 6)
         y_acc = {nt: bank(f"y_acc{nt}", [M1], F32, nt) for nt in (2, 3)}
         for nt in (2, 3):
             d_pass(0, nt, True, False)
@@ -463,7 +463,7 @@ def tile_list_subtitle_couple_score_kernel(
         lone_magnitude(2, turned2)
         wb_second = place("wb_second", [2 * PASS], BF16, CAST_AT - 4 * KB)
         round_plain(nc.scalar, wb_second[:], wb_raw[1][:, :, 2 * P :], -1.0)
-        lone_difference(3, 5)
+        lone_difference(3, 4)
         lone_magnitude(3, turned2)
         couples = [slice(0, M1 // 2), slice(M1 // 2, M1)]
 

from contextlib import ExitStack

import concourse.mybir as mybir
from concourse.masks import make_identity

K, H, N, T, S, M1, M2 = 1024, 1536, 512, 2048, 1024, 512, 256
FLOPS = 2 * K * H * S + 2 * 2 * H * N * M1

F32 = mybir.dt.float32
BF16 = mybir.dt.bfloat16
I32 = mybir.dt.int32
U32 = mybir.dt.uint32
U16 = mybir.dt.uint16
U8 = mybir.dt.uint8
FP8X4 = mybir.dt.float8_e4m3fn_x4
FP4X4 = mybir.dt.float4_e2m1fn_x4
ACT = mybir.ActivationFunctionType
ALU = mybir.AluOpType

P = 128
PACK = 4
PASS = P * PACK
BANK = 512
K_PASSES = K // PASS
H_PASSES = H // PASS
N_TILES = N // P
M_TILES = M1 // P
H_SLOTS = 4
SIDE_PIECES = 2
RUN = 8
KB = 1024

H_AT = 0
TAB_AT = 35 * KB
X_AT = 51 * KB
XN_AT = 67 * KB
RAW_AT = 79 * KB
WB_AT = 102 * KB
CAST_AT = 119 * KB
PAIR_AT = 140 * KB
LAST_AT = 148 * KB
TURN_AT = 157 * KB
HEAD_AT = 180 * KB


def tile_list_subtitle_couple_score_kernel(
    tc, tab_words, tab_scales, offs, pos1, pos2, pos3, pos4, w1, wd_words, wd_scales, wb, out
):
    nc = tc.nc
    with ExitStack() as ctx:
        keep = ctx.enter_context(tc.tile_pool(name="keep", bufs=1))
        shared = ctx.enter_context(tc.tile_pool(name="shared", bufs=1))
        psum = ctx.enter_context(tc.psum_pool(name="psum", bufs=1))

        def place(name, shape, dtype, at):
            return shared.tile([P] + shape, dtype, name=name, offset=at, align_bytes=64)

        def bank(name, shape, dtype, number):
            return psum.tile([P] + shape, dtype, name=name, tag=f"bank{number}")

        def load_list(src, name):
            tile = keep.tile(list(src.shape), U16, name=name)
            nc.sync.dma_start(tile[:], src)
            return tile

        def load_rows(raw, src, g, c0):
            rows = raw.rearrange("p (j c) -> p j c", j=PACK)
            nc.sync.dma_start(
                out=rows,
                in_=src[g * PASS : (g + 1) * PASS, c0 : c0 + rows.shape[2]].rearrange("(p j) c -> p j c", j=PACK),
            )
            return rows

        def load_runs(raw, src, g):
            rows = raw.rearrange("p (t c) -> p t c", t=PACK)
            runs = src[g * PASS : (g + 1) * PASS, :].rearrange("(b t i) c -> t b i c", t=PACK, i=RUN)
            for t in range(PACK):
                nc.sync.dma_start(out=rows[:, t], in_=runs[t])
            return rows

        def quantize(name, grouped, codes=None, scales=None):
            width = grouped.shape[1] // PACK
            if codes is None:
                codes = keep.tile([P, width], U32, name=name + "_codes", align_bytes=64)[:]
            if scales is None:
                scales = keep.tile([P, width], U8, name=name + "_scales", align_bytes=64)[:]
            nc.vector.quantize_mx(out=codes.bitcast(FP8X4), scales=scales, in_=grouped)
            return [(codes[:, c : c + P], scales[:, c : c + P]) for c in range(0, width, P)], (codes, scales)

        def rounded(engine, dst, src, sign):
            if engine is nc.scalar:
                nc.scalar.activation(dst, src, ACT.Copy, scale=sign)
            else:
                nc.gpsimd.tensor_scalar(dst, src, sign, 0.0, ALU.mult, ALU.add)

        def round_plain(engine, grouped, raw, sign=1.0):
            if engine is nc.gpsimd:
                return rounded(engine, grouped.rearrange("p (c j) -> p c j", j=PACK), raw.rearrange("p j c -> p c j"), sign)
            rounded(
                engine,
                grouped.rearrange("p (c i j) -> p c j i", i=PACK, j=PACK),
                raw.rearrange("p j (c i) -> p c j i", i=PACK),
                sign,
            )

        def round_runs(engine, grouped, raw, tiles):
            if engine is nc.gpsimd:
                src = raw.rearrange("p j (b t i) -> p b t i j", t=PACK, i=RUN)[:, :, tiles]
                return rounded(engine, grouped.rearrange("p t (b i) j -> p b t i j", i=RUN), src, 1.0)
            src = raw.rearrange("p j (b t h i) -> p t b h j i", t=PACK, h=RUN // PACK, i=PACK)
            dst = grouped.rearrange("p t (b h i) j -> p t b h j i", h=RUN // PACK, i=PACK)
            for t in range(tiles.start, tiles.stop):
                nc.scalar.copy(dst[:, t - tiles.start], src[:, t])

        tab_planes = keep.tile([P, T], U8, name="tab_planes", align_bytes=64)
        nc.vector.memset(tab_planes[:].bitcast(I32), 0)
        wd_planes = keep.tile([P, H_PASSES, N], U8, name="wd_planes", align_bytes=64)
        nc.gpsimd.memset(wd_planes[:].rearrange("p g n -> p (g n)").bitcast(I32), 0)
        identity = keep.tile([P, P], F32, name="identity")
        make_identity(nc, identity[:])
        identity_bf = keep.tile([P, P], BF16, name="identity_bf")
        make_identity(nc, identity_bf[:])
        h_tiles = [place(f"h{i}", [2 * S], F32, H_AT + 8 * KB * i) for i in range(H_SLOTS)]
        nc.gpsimd.memset(h_tiles[3][:, S:], 0.0)

        def load_table(a):
            words = place(f"tab{a}", [T], I32, TAB_AT + 8 * KB * a)
            nc.sync.dma_start(out=words[:], in_=tab_words[a].rearrange("p t i -> p (t i)").bitcast(I32))
            return words

        tab_sb = [load_table(0)]
        offs_sb = load_list(offs, "offs_sb")
        for q in range(4):
            nc.sync.dma_start(
                out=tab_planes[32 * q : 32 * q + 4 * K_PASSES, :].bitcast(I32),
                in_=tab_scales[:, 4 * q : 4 * q + 4, :].bitcast(I32),
            )
        raw = {}
        raw[0, 0] = load_rows(h_tiles[0][:, S : S + PASS], w1, 0, 0)
        raw[0, 1] = load_rows(h_tiles[0][:, S + PASS :], w1, 1, 0)
        tab_sb.append(load_table(1))
        raw[1, 0] = load_rows(place("stage0", [PASS], F32, PAIR_AT + 2 * KB)[:], w1, 0, P)
        raw[1, 1] = load_rows(place("stage1", [PASS], F32, PAIR_AT)[:], w1, 1, P)
        pos1_sb = load_list(pos1, "pos1_sb")
        pos2_sb = load_list(pos2, "pos2_sb")
        raw[2, 0] = load_rows(h_tiles[2][:, S:], w1, 0, 2 * P)
        raw[2, 1] = load_rows(h_tiles[1][:, S:], w1, 1, 2 * P)
        raw[4, 0] = load_rows(place("stage4", [PACK * PASS], F32, RAW_AT)[:], w1, 0, PASS)
        raw[4, 1] = load_rows(place("stage5", [PACK * PASS], F32, RAW_AT + 8 * KB)[:], w1, 1, PASS)
        raw[8, 0] = load_rows(place("stage8", [PACK * PASS], F32, CAST_AT - 16 * KB)[:], w1, 0, 2 * PASS)

        v_codes = [keep.tile([P, S], U32, name=f"v_codes{a}", align_bytes=64) for a in range(K_PASSES)]
        v_planes = keep.tile([P, S], U8, name="v_planes", align_bytes=64)
        nc.vector.tensor_copy(v_codes[0][:], tab_sb[0][:].bitcast(U32).indirect(offs_sb[:]))
        nc.vector.tensor_copy(v_planes[:], tab_planes[:].indirect(offs_sb[:]))

        raw[8, 1] = load_rows(place("stage9", [PACK * PASS], F32, TAB_AT)[:], w1, 1, 2 * PASS)
        w1_mx = {}
        cast0 = place("cast0", [K_PASSES, PASS], BF16, CAST_AT + 11 * KB)
        for a in range(K_PASSES):
            round_plain(nc.scalar, cast0[:, a], raw[0, a])
        w1_mx[0, 0], w1_mx[0, 1] = quantize("w0", cast0[:].rearrange("p a c -> p (a c)"))[0]
        pieces = [slice(0, BANK), slice(BANK, BANK + BANK // 2), slice(BANK + BANK // 2, S)]
        for c in pieces:
            nc.vector.tensor_copy(v_codes[1][:, c], tab_sb[1][:].bitcast(U32).indirect(offs_sb[:, c.start // 16 : c.stop // 16]))
        cast1 = place("cast1", [K_PASSES, PASS], BF16, CAST_AT + 15 * KB)[:]
        for a, engine in enumerate((nc.scalar, nc.gpsimd)):
            round_plain(engine, cast1[:, a], raw[1, a])
        w1_mx[1, 0], w1_mx[1, 1] = quantize("w1", cast1.rearrange("p a c -> p (a c)"))[0]

        def h_pass(n, acc, cols, a, start, stop):
            nc.tensor.matmul_mx(
                out=acc[:],
                lhsT=w1_mx[n, a][0].bitcast(FP8X4),
                lhsT_scale=w1_mx[n, a][1],
                rhs=v_codes[a][:, cols].bitcast(FP8X4),
                rhs_scale=v_planes[4 * a : P, cols],
                start=start,
                stop=stop,
            )

        def evac_half(n, half):
            acc = bank("acc", [BANK], F32, ((0, 2, 0, 4, 2)[n] if n <= PACK else 4 + 2 * (n % 2)) + half)
            cols = slice(half * BANK, (half + 1) * BANK)
            for a in reversed(range(K_PASSES)):
                h_pass(n, acc, cols, a, a == K_PASSES - 1, a == 0)
            nc.scalar.copy(h_tiles[n % H_SLOTS][:, cols], acc[:])

        def evac(n):
            evac_half(n, 0)
            evac_half(n, 1)

        def gather(n, x1, x2, between=None):
            h = h_tiles[n % H_SLOTS]
            nc.vector.tensor_copy(x1, h[:].indirect(pos1_sb[:]))
            if between:
                between()
            nc.vector.tensor_scalar(x2, h[:].indirect(pos2_sb[:]), -1.0, 0.0, ALU.mult, ALU.add)

        x1_at = [XN_AT, CAST_AT + 25 * KB // 2, XN_AT + 2 * KB, CAST_AT + 33 * KB // 2]
        x2_at = [XN_AT + 10 * KB, CAST_AT + 29 * KB // 2, XN_AT + 8 * KB, CAST_AT - 7 * KB]
        first_x, first_diff, first_prod = {}, {}, {}

        def pick_first(j, between=None):
            first_x[j] = place(f"x1n{j}", [M1], F32, x1_at[j]), place(f"x2n{j}", [M1], F32, x2_at[j])
            gather(j, first_x[j][0][:], first_x[j][1][:], between)

        def first_distance(j, turned):
            diff = bank("diff0", [M_TILES, P], F32, j)
            for mt in range(M_TILES):
                for x, first in zip(first_x[j], (True, False)):
                    nc.tensor.matmul(
                        diff[:, mt, :], lhsT=x[:, mt * P : (mt + 1) * P], rhs=identity[:],
                        is_transpose=True, start=first, stop=not first,
                    )
            nc.scalar.activation(
                turned[:].rearrange("m mt u (j p) e -> m j u mt p e", j=PACK)[:, j],
                diff[:].rearrange("m mt (p u e) -> m u mt p e", u=2, e=2),
                ACT.Abs,
            )

        def first_product(j):
            nc.gpsimd.tensor_tensor(first_prod[j], first_x[j][0][:], first_x[j][1][:], ALU.mult)

        def turn_first_products(turned):
            words = turned[:].rearrange("m mt u p e -> m (mt u p e)").bitcast(F32)
            words = words.rearrange("m (mt u p) -> m mt u p", mt=M_TILES, u=2)
            for pair in range(M_TILES // 2):
                across = bank("across", [2, PASS], BF16, pair)
                for jj in range(2):
                    cols = slice((2 * pair + jj) * P, (2 * pair + jj + 1) * P)
                    for j in range(PACK):
                        nc.tensor.transpose(across[:, jj, j * P : (j + 1) * P], first_prod[j][:, cols], identity_bf[:])
                nc.scalar.copy(
                    words[:, 2 * pair : 2 * pair + 2], across[:].bitcast(F32).rearrange("m jj (p u) -> m jj u p", u=2)
                )

        def turn_back(words, dist, first_bank):
            dist_words = dist.bitcast(F32)
            backs = [bank("back", [2, 2, P], F32, first_bank + pair) for pair in range(M_TILES // 2)]
            for u in range(2):
                for pair, back in enumerate(backs):
                    for jj in range(2):
                        nc.tensor.transpose(back[:, jj, u, :], words(2 * pair + jj, u), identity[:])
            for pair, back in enumerate(backs):
                nc.scalar.copy(
                    dist_words[:, pair * BANK : (pair + 1) * BANK].rearrange("p (jj m u) -> p jj m u", jj=2, u=2),
                    back[:].rearrange("p jj u m -> p jj m u"),
                )

        def first_words(turned):
            words = turned[:].rearrange("m mt u p e -> m mt u (p e)").bitcast(F32)
            return lambda mt, u: words[:, mt, u, :]

        xs, diffs = {}, {}

        def picked(g, at):
            flat = [place(f"x{i + 1}_{g}", [PACK * M1], F32, at + 8 * KB * i) for i in range(2)]
            xs[g] = [x[:].rearrange("p (t m) -> p t m", t=PACK) for x in flat]
            return flat

        def pick(g, t):
            gather(g * PACK + t, xs[g][0][:, t, :], xs[g][1][:, t, :])

        def difference(g, u, e, first_bank):
            if e == 0:
                diffs[g, u] = [bank("diff", [2, 2, P], F32, first_bank + pair) for pair in range(M_TILES // 2)]
            for i, x in enumerate(xs[g]):
                for pair, diff in enumerate(diffs[g, u]):
                    for jj in range(2):
                        cols = slice((2 * pair + jj) * P, (2 * pair + jj + 1) * P)
                        nc.tensor.matmul(
                            diff[:, e, jj, :], lhsT=x[:, 2 * u + e, cols], rhs=identity[:],
                            is_transpose=True, start=(e, i, jj) == (0, 0, 0), stop=(e, i, jj) == (1, 1, 1),
                        )

        def magnitude(g, u, turned):
            for pair, diff in enumerate(diffs[g, u]):
                nc.scalar.activation(
                    turned[pair][:].rearrange("m jj (b u e i) -> m u jj b e i", u=2, e=2, i=RUN)[:, u],
                    diff[:].rearrange("m e jj (b i) -> m jj b e i", i=RUN),
                    ACT.Abs,
                )

        def lone_difference(t, first_bank):
            diffs[t] = [bank("diff", [2, P], F32, first_bank + pair) for pair in range(M_TILES // 2)]
            for i, x in enumerate(xs[2]):
                for mt in range(M_TILES):
                    nc.tensor.matmul(
                        diffs[t][mt // 2][:, mt % 2, :], lhsT=x[:, t, mt * P : (mt + 1) * P], rhs=identity[:],
                        is_transpose=True, start=(i, mt % 2) == (0, 0), stop=(i, mt % 2) == (1, 1),
                    )

        def lone_magnitude(t, turned):
            for pair, diff in enumerate(diffs[t]):
                nc.scalar.activation(
                    turned[pair][:].rearrange("m jj (b t i) -> m t jj b i", t=PACK, i=RUN)[:, t],
                    diff[:].rearrange("m jj (b i) -> m jj b i", i=RUN),
                    ACT.Abs,
                )

        def turn_back_half(words, dist, pair, number):
            back = bank("back", [2, 2, P], F32, number)
            for jj in range(2):
                for u in range(2):
                    nc.tensor.transpose(back[:, jj, u, :], words(2 * pair + jj, u), identity[:])
            nc.scalar.copy(
                dist.bitcast(F32).rearrange("p (jj m u) -> p jj m u", jj=2, u=2), back[:].rearrange("p jj u m -> p jj m u")
            )

        def run_distance(g, u, first_bank, turned):
            for e in range(2):
                difference(g, u, e, first_bank)
            magnitude(g, u, turned)

        def run_words(turned):
            return lambda mt, u: turned[mt // 2][:].bitcast(F32)[:, mt % 2, u : 2 * P : 2]

        def interleaved_in(x):
            return x.rearrange("p t (c i) -> p c t i", i=PACK)

        def interleaved_out(x):
            return x.rearrange("p (c i t) -> p c t i", i=PACK, t=PACK)

        def product(engine, g, prod, pieces):
            for c in pieces:
                engine.tensor_tensor(
                    interleaved_out(prod)[:, c], interleaved_in(xs[g][0])[:, c], interleaved_in(xs[g][1])[:, c], ALU.mult
                )

        def quantize_w1(n, tiles, grouped):
            for i, operand in enumerate(quantize(f"w{n}", grouped.rearrange("p a t m j -> p (a t m j)"))[0]):
                w1_mx[n + i % tiles, i // tiles] = operand

        wb_mx, b_mx, d_mx = {}, {}, {}

        def b_pass(g, nt, start, stop):
            nc.tensor.matmul_mx(
                out=y_acc[nt][:],
                lhsT=wb_mx[g, nt][0].bitcast(FP8X4),
                lhsT_scale=wb_mx[g, nt][1],
                rhs=b_mx[g][0].bitcast(FP8X4),
                rhs_scale=b_mx[g][1],
                start=start,
                stop=stop,
            )

        def d_pass(g, nt, start, stop, cols=slice(0, M1)):
            nc.tensor.matmul_mx(
                out=y_acc[nt][:, cols],
                lhsT=wd_sb[:, g, 2 * nt * P : 2 * (nt + 1) * P].bitcast(FP4X4),
                lhsT_scale=wd_planes[:, g, nt * P : (nt + 1) * P],
                rhs=d_mx[g][0][:, cols].bitcast(FP8X4),
                rhs_scale=d_mx[g][1][:, cols],
                start=start,
                stop=stop,
            )

        accs = [bank("acc", [c.stop - c.start], F32, number) for c, number in zip(pieces, (0, 1, 6))]
        for c, acc in zip(pieces, accs):
            h_pass(0, acc, c, 0, True, False)
        for c, acc in zip(pieces, accs):
            h_pass(0, acc, c, 1, False, True)
            nc.scalar.copy(h_tiles[0][:, c], acc[:])
        casts = [place(f"cast{n}", [K_PASSES, PASS], BF16, at) for n, at in ((2, CAST_AT + 27 * KB // 2), (3, CAST_AT + 16 * KB))]
        for i, cast in enumerate(casts):
            round_plain(nc.gpsimd, cast[:, 0], raw[2, 0][:, :, i * P : (i + 1) * P])
        evac(1)
        for i, cast in enumerate(casts):
            round_plain(nc.scalar, cast[:, 1], raw[2, 1][:, :, i * P : (i + 1) * P])
        pick_first(0)
        for n, cast in zip((2, 3), casts):
            w1_mx[n, 0], w1_mx[n, 1] = quantize(f"w{n}", cast[:].rearrange("p a c -> p (a c)"))[0]
        evac(2)
        pick_first(1)
        cast4 = place("cast4", [K_PASSES, 2, P, PACK], BF16, CAST_AT + 33 * KB // 2)
        cast6 = place("cast6", [K_PASSES, 2, P, PACK], BF16, CAST_AT - 15 * KB // 2)
        round_runs(nc.gpsimd, cast4[:, 0], raw[4, 0], slice(0, 2))
        round_runs(nc.gpsimd, cast6[:, 0], raw[4, 0], slice(2, 4))
        evac(3)
        round_runs(nc.scalar, cast4[:, 1], raw[4, 1], slice(0, 2))
        round_runs(nc.scalar, cast6[:, 1], raw[4, 1], slice(2, 4))
        pick_first(2)
        quantize_w1(4, 2, cast4[:])
        first_prod[0] = place("prod_first", [M1], BF16, CAST_AT + 37 * KB // 2)[:]
        first_product(0)
        cast8 = place("cast8", [K_PASSES, PACK, P, PACK], BF16, CAST_AT - 5 * KB)
        pick_first(3, lambda: quantize_w1(6, 2, cast6[:]))
        round_runs(nc.gpsimd, cast8[:, 0], raw[8, 0], slice(0, PACK))
        wb_raw = [load_rows(place(f"wb_stage{g}", [PACK * N], F32, RAW_AT)[:], wb, g, 0) for g in range(1)]
        wb_raw.append(load_runs(place("wb_stage1", [PACK * N], F32, WB_AT)[:], wb, 1))
        wd_sb = place("wd_sb", [H_PASSES, 2 * N], U8, RAW_AT + 12 * KB)
        nc.sync.dma_start(out=wd_sb[:].bitcast(I32), in_=wd_words.rearrange("g p c -> p g c").bitcast(I32))
        for q in range(4):
            nc.sync.dma_start(
                out=wd_planes[32 * q : 32 * q + 4, :, :].bitcast(I32),
                in_=wd_scales[:, 4 * q : 4 * q + 4, :].rearrange("g r n -> r g n").bitcast(I32),
            )
        pos3_sb = load_list(pos3, "pos3_sb")
        pos4_sb = load_list(pos4, "pos4_sb")
        turned_d = place("turned_d", [M_TILES, 2, P, 2], BF16, RAW_AT + 8 * KB)
        first_distance(0, turned_d)
        first_distance(1, turned_d)
        evac(4)
        evac(5)
        round_runs(nc.scalar, cast8[:, 1], raw[8, 1], slice(0, PACK))
        first_distance(2, turned_d)
        first_distance(3, turned_d)
        evac(6)
        evac(7)
        prod_rest = place("prod_rest", [2, M1], BF16, CAST_AT - 9 * KB)
        for j in (1, 2):
            first_prod[j] = prod_rest[:, j - 1]
            first_product(j)
        picked(1, X_AT)
        pick(1, 0)
        pick(1, 1)
        quantize_w1(8, PACK, cast8[:])
        first_prod[3] = place("prod_last", [M1], BF16, CAST_AT - 5 * KB)[:]
        first_product(3)
        wb_raw.append(load_runs(place("wb_stage2", [PACK * N], F32, XN_AT)[:], wb, 2))
        wb_front = place("wb_front", [2, 2, P, PACK], BF16, CAST_AT)
        for g in (1, 0):
            rounded(nc.gpsimd, wb_front[:, :, g], wb_raw[g][:, :, : 2 * P].rearrange("p j (a c) -> p a c j", c=P), -1.0)
        dists = [place("dist0", [PACK * M1], BF16, PAIR_AT)]
        pick(1, 2)
        turn_back(first_words(turned_d), dists[0][:], 2)
        turned1 = [place(f"turned1{pair}", [2, PASS], BF16, CAST_AT - 4 * KB + 2 * KB * pair) for pair in range(2)]
        run_distance(1, 0, 0, turned1)
        evac(8)
        evac(9)
        pick(1, 3)
        d_mx[0] = quantize("d0", dists[0][:])[1]
        turned_b = place("turned_b", [M_TILES, 2, P, 2], BF16, CAST_AT + 6 * KB)
        turn_first_products(turned_b)
        prods = [place(f"prod{g}", [PACK * M1], BF16, at) for g, at in ((0, PAIR_AT + 4 * KB), (1, PAIR_AT))]
        side = M1 // PACK // SIDE_PIECES
        product(nc.gpsimd, 1, prods[1][:], [slice(i * side, (i + 1) * side) for i in range(SIDE_PIECES)])
        evac(10)
        turn_back(first_words(turned_b), prods[0][:], 0)
        evac_half(11, 0)
        run_distance(1, 1, 2, turned1)
        wb_first = place("wb_first", [2 * PASS], BF16, X_AT + 6 * KB)
        round_plain(nc.gpsimd, wb_first[:], wb_raw[0][:, :, 2 * P :], -1.0)
        evac_half(11, 1)
        picked(2, TAB_AT)
        pick(2, 0)
        pick(2, 1)
        turned2 = [place(f"turned2{pair}", [2, PASS], BF16, TURN_AT + 7 * KB * pair) for pair in range(2)]
        run_distance(2, 0, 0, turned2)
        dist1 = [place(f"dist1{pair}", [S], BF16, TURN_AT + (17 - 2 * pair) * KB) for pair in range(2)]
        for pair in range(2):
            turn_back_half(run_words(turned1), dist1[pair][:], pair, 2 + pair)
        pick(2, 2)
        lone_difference(2, 6)
        y_acc = {nt: bank(f"y_acc{nt}", [M1], F32, nt) for nt in (2, 3)}
        for nt in (2, 3):
            d_pass(0, nt, True, False)
        pick(2, 3)

        wb_low = place("wb_low", [2, PASS], BF16, CAST_AT - 2 * KB)
        round_plain(nc.scalar, wb_low[:].rearrange("p a c -> p (a c)"), wb_raw[2][:, :, : 2 * P], -1.0)
        lone_magnitude(2, turned2)
        wb_second = place("wb_second", [2 * PASS], BF16, CAST_AT - 4 * KB)
        round_plain(nc.scalar, wb_second[:], wb_raw[1][:, :, 2 * P :], -1.0)
        lone_difference(3, 4)
        lone_magnitude(3, turned2)
        couples = [slice(0, M1 // 2), slice(M1 // 2, M1)]

        def quantize_halves(g, halves, codes):
            d_mx[g] = codes, keep.tile([P, M1], U8, name=f"d{g}_scales", align_bytes=64)[:]
            for c, half in zip(couples, halves):
                quantize(f"d{g}", half[:], d_mx[g][0][:, c], d_mx[g][1][:, c])

        quantize_halves(1, dist1, place("d1_codes", [M1], U32, H_AT + 8 * KB * (H_SLOTS - 2))[:])
        for nt in (2, 3):
            d_pass(1, nt, False, False)
        dist = [place(f"dist2{pair}", [S], BF16, LAST_AT + 3 * KB * pair) for pair in range(2)]
        prod = place("prod", [PACK * M1], BF16, TURN_AT + 17 * KB)
        for pair in range(2):
            turn_back_half(run_words(turned2), dist[pair][:], pair, pair)
        for nt in (0, 1):
            y_acc[nt] = bank(f"y_acc{nt}", [M1], F32, 4 + nt)
            for g in range(2):
                d_pass(g, nt, g == 0, False)
        b_codes = place("b_codes", [2 * M1], U32, TURN_AT + 13 * KB)
        low_codes = place("low_codes", [3 * P + M1], U32, TURN_AT)

        def quantize_low(nt, codes):
            front = wb_front[:, nt].rearrange("p g c j -> p (g c j)")
            wb_mx[0, nt], wb_mx[1, nt] = quantize(f"wb_front{nt}", front, codes[:, : 2 * P])[0]
            wb_mx[2, nt] = quantize(f"wb_low{nt}", wb_low[:, nt], codes[:, 2 * P : 3 * P])[0][0]

        quads = M1 // PACK // 2
        product(nc.vector, 2, prod[:], [slice(0, quads)])
        b_mx[0] = quantize("b0", prods[0][:], b_codes[:, :M1])[1]
        product(nc.vector, 2, prod[:], [slice(quads, 2 * quads)])
        b_mx[1] = quantize("b1", prods[1][:], b_codes[:, M1:])[1]
        quantize_low(0, low_codes)
        b_mx[2] = quantize("b2", prod[:], low_codes[:, 3 * P : 3 * P + M1])[1]
        quantize_halves(2, dist, keep.tile([P, M1], U32, name="d2_codes", align_bytes=64)[:])
        for g in range(H_PASSES):
            b_pass(g, 0, False, False)
        for c in couples:
            d_pass(2, 0, False, c == couples[-1], c)
        late = place("late", [9 * P], U32, LAST_AT - 5 * KB // 2)
        quantize_low(1, late)
        d_pass(2, 1, False, False)
        for g in range(H_PASSES):
            b_pass(g, 1, False, g == H_PASSES - 1)
        wb_last = place("wb_last", [2 * PASS], BF16, TURN_AT + 17 * KB // 2)
        round_plain(nc.scalar, wb_last[:], wb_raw[2][:, :, 2 * P :], -1.0)
        for g, cast in enumerate((wb_first, wb_second, wb_last)):
            wb_mx[g, 2], wb_mx[g, 3] = quantize(f"wb_high{g}", cast[:], late[:, (3 + 2 * g) * P : (5 + 2 * g) * P])[0]
        for nt in range(2, N_TILES):
            d_pass(2, nt, False, False)
            for g in range(H_PASSES):
                b_pass(g, nt, False, g == H_PASSES - 1)

        ys = [place(f"y{nt}", [M1], F32, X_AT + 2 * KB * nt) for nt in range(N_TILES)]
        for nt in range(N_TILES):
            nc.scalar.copy(ys[nt][:], y_acc[nt][:])
        first = place("first", [N_TILES, M2], F32, X_AT + 8 * KB)
        other = place("other", [N_TILES, M2], F32, X_AT + 12 * KB)
        top = place("top", [N_TILES, M2], F32, LAST_AT - 6 * KB)
        squared = place("squared", [N_TILES, M2], F32, LAST_AT)
        score = place("score", [N_TILES, M2], F32, TAB_AT + 4 * KB)

        def pick_y(nt, c, dst, pos):
            entries = slice(c.start // 16, c.stop // 16)
            nc.vector.tensor_copy(dst[:, nt, c], ys[nt][:].indirect(pos[:, entries]))

        def larger(tiles, c):
            nc.vector.tensor_tensor(top[:, tiles, c], first[:, tiles, c], other[:, tiles, c], ALU.max)

        def square(tiles, c):
            nc.scalar.activation(squared[:, tiles, c], top[:, tiles, c], ACT.Square)

        def add_one(tiles, c):
            nc.scalar.activation(score[:, tiles, c], squared[:, tiles, c], ACT.Copy, bias=1.0)

        def store(tiles):
            nc.sync.dma_start(
                out=out[tiles.start * P : tiles.stop * P, :].rearrange("(a p) j -> p a j", p=P), in_=score[:, tiles, :]
            )

        last = N_TILES - 1
        whole, low, high = slice(0, M2), slice(0, M2 // 2), slice(M2 // 2, M2)
        for nt in range(last):
            pick_y(nt, whole, first, pos3_sb)
            pick_y(nt, whole, other, pos4_sb)
        for tiles in (slice(0, 2), slice(2, 3)):
            larger(tiles, whole)
            square(tiles, whole)
        for tiles in (slice(0, 2), slice(2, 3)):
            add_one(tiles, whole)
            store(tiles)
        pick_y(last, whole, first, pos3_sb)
        pick_y(last, low, other, pos4_sb)
        pick_y(last, high, other, pos4_sb)
        larger(last, low)
        larger(last, high)
        square(last, low)
        add_one(last, low)
        nc.vector.tensor_tensor(squared[:, last, high], top[:, last, high], top[:, last, high], ALU.mult)
        nc.vector.tensor_scalar(score[:, last, high], squared[:, last, high], 1.0, None, ALU.add)
        store(slice(last, N_TILES))
